import numpy as np
import ml_dtypes


def mxq(x, axis, fmt="e4m3"):
    dtype, down = {"e4m3": (ml_dtypes.float8_e4m3fn, 7), "e5m2": (ml_dtypes.float8_e5m2, 14)}[fmt]
    v = np.moveaxis(np.asarray(x, np.float32).astype(ml_dtypes.bfloat16).astype(np.float64), axis, -1)
    blocks = v.reshape(v.shape[:-1] + (-1, 32))
    amax = np.abs(blocks).max(-1, keepdims=True)
    byte = np.maximum(np.where(amax > 0, np.frexp(amax)[1] - 1 + 127, 0) - down, 1)
    scale = np.exp2(byte - 127.0)
    codes = (blocks / scale).astype(np.float32).astype(dtype).astype(np.float64)
    return np.moveaxis((codes * scale).reshape(v.shape), -1, axis)


WIDE = False


def mx_kscale(k):
    if not WIDE:
        return np.ones(k)
    levels = np.array([10, -10, 5, -5, 0])
    if k % 512:
        return np.exp2(np.random.permutation(np.resize(levels, k // 32))).repeat(32)
    a = np.empty((k // 512, 16))
    for p in range(k // 512):
        a[p, :8] = np.random.permutation(np.resize(levels, 8))
        for g in range(8):
            far = levels[np.abs(levels - a[p, g]) >= 10]
            a[p, g + 8] = far[np.random.randint(len(far))]
    return np.exp2(a.ravel()).repeat(32)


def f64(x):
    return np.asarray(x).astype(np.float64)


def planes(y):
    n, m = y.shape
    v = y.astype(np.float32).astype(ml_dtypes.bfloat16).astype(np.float64).reshape(n // 32, 32, m)
    top = np.abs(v).max(1)
    byte = np.clip(np.where(top > 0, np.frexp(top)[1] - 1 + 127 - 7, 1), 1, 254)
    codes = (v * np.exp2(127.0 - byte)[:, None, :]).reshape(n, m).astype(np.float32).astype(ml_dtypes.float8_e4m3fn).view(np.uint8)
    words = codes.reshape(n // 512, 128, 4, m).transpose(0, 1, 3, 2)
    return np.ascontiguousarray(words), np.ascontiguousarray(byte.astype(np.uint8).reshape(n // 512, 16, m))


def split(x):
    m, e = np.frexp(f64(x))
    hi = np.ldexp(np.trunc(16.0 * m) / 16.0, e)
    return hi, f64(x) - hi


def silu(v):
    return v / (1.0 + np.exp(-np.maximum(v, -700.0)))


K, M, T = 512, 1024, 1536


def setup_inputs():
    n = np.random.standard_normal
    s = mx_kscale(K)[:, None]
    return {
        "w": (n((K, M)) / np.sqrt(K) / s).astype(np.float32),
        "x": (n((K, T)) * s).astype(np.float32),
        "b": (0.3 * n(1024)).astype(np.float32),
    }


def reference(w, x, b):
    w_hi, w_lo = split(w)
    w_hi_, w_lo_ = mxq(w_hi, 0, "e4m3"), mxq(w_lo, 0, "e4m3")
    x_ = mxq(f64(x), 0, "e4m3")
    y = x_.T @ w_hi_ + x_.T @ w_lo_
    out_0 = silu(y + f64(b)[None, :])
    return (out_0,) + planes(out_0)

@@ -1,0 +1,414 @@
+from contextlib import ExitStack
+
+import concourse.mybir as mybir
+from concourse.masks import make_identity
+
+K, M, T = 512, 1024, 1536
+FLOPS = 2 * 2 * K * M * T
+
+F32 = mybir.dt.float32
+BF16 = mybir.dt.bfloat16
+I32 = mybir.dt.int32
+U32 = mybir.dt.uint32
+U8 = mybir.dt.uint8
+FP8X4 = mybir.dt.float8_e4m3fn_x4
+ALU = mybir.AluOpType
+SILU = mybir.ActivationFunctionType.Silu
+
+P = 128
+PACK = 4
+CHUNK = P * PACK
+QUARTER = 256
+HI_MASK_PAIR = 0xFFF0FFF0 - (1 << 32)
+BANKS = {"sum": 4, "turn": 4}
+MID_BUFS = 6
+GROUPS = [(0, 256), (256, 512), (512, 768), (768, 1024)]
+BIAS_TILES = []
+TOKEN_MAJOR = []
+
+
+def tile_mix_hilo_tm_pl_silu_kernel(tc, w, x, b, out_0, out_1, out_2):
+    nc = tc.nc
+    engines = {"V": nc.vector.tensor_copy, "S": nc.scalar.copy}
+
+    with ExitStack() as ctx:
+        keep = ctx.enter_context(tc.tile_pool(name="keep", bufs=1))
+        psum = ctx.enter_context(tc.psum_pool(name="psum", bufs=1))
+        ctx.enter_context(tc.manual_schedule())
+
+        w_rows = w.rearrange("(p j) n -> p j n", j=PACK)
+        x_rows = x.rearrange("(p j) t -> p j t", j=PACK)
+        tiles = {}
+        bank_count = {"sum": 0, "turn": 0}
+
+        def bank(kind):
+            index = bank_count[kind] % BANKS[kind]
+            bank_count[kind] = bank_count[kind] + 1
+            return psum.tile([P, PACK, P], F32, name="%s%d" % (kind, index))
+
+        def load_w(n0, n1):
+            raw = keep.tile([P, PACK, n1 - n0], F32, name="w_raw%d" % n0)
+            nc.sync.dma_start(out=raw[:], in_=w_rows[:, :, n0:n1])
+            tiles["w_raw", n0] = raw
+            tiles["w_parts", n0] = keep.tile([P, 2, n1 - n0, PACK], BF16, name="w_parts%d" % n0, align_bytes=64)
+            codes = keep.tile([P, 2, n1 - n0], U32, name="w_codes%d" % n0, align_bytes=64)
+            scales = keep.tile([P, 2, n1 - n0], U8, name="w_scales%d" % n0, align_bytes=64)
+            tiles["w_mx", n0] = (codes, scales)
+            for n in range(n0, n1, P):
+                tiles["w_tile", n // P] = (codes, scales, n - n0)
+
+        def load_x(t0, t1):
+            raw = keep.tile([P, PACK, t1 - t0], F32, name="x_raw%d" % t0)
+            nc.sync.dma_start(out=raw[:], in_=x_rows[:, :, t0:t1])
+            tiles["x_raw", t0] = raw
+
+        def w_top(n0, engine):
+            halves = tiles["w_raw", n0][:].bitcast(BF16).rearrange("p j (c i e) -> p c j i e", i=4, e=2)
+            top = tiles["w_parts", n0][:, 0].rearrange("p (c i) j -> p c j i", i=4)
+            engines[engine](out=top, in_=halves[:, :, :, :, 1])
+
+        def w_mask(n0):
+            pairs = tiles["w_parts", n0][:, 0].rearrange("p n j -> p (n j)").bitcast(I32)
+            nc.vector.tensor_scalar(out=pairs, in0=pairs, scalar1=HI_MASK_PAIR, scalar2=None, op0=ALU.bitwise_and)
+
+        def w_low(n0):
+            parts = tiles["w_parts", n0]
+            nc.vector.tensor_tensor(
+                out=parts[:, 1].rearrange("p (c i) j -> p c j i", i=4),
+                in0=tiles["w_raw", n0][:].rearrange("p j (c i) -> p c j i", i=4),
+                in1=parts[:, 0].rearrange("p (c i) j -> p c j i", i=4),
+                op=ALU.subtract,
+            )
+
+        def w_quantize(n0):
+            codes, scales = tiles["w_mx", n0]
+            nc.vector.quantize_mx(
+                out=codes[:].rearrange("p h n -> p (h n)").bitcast(FP8X4),
+                scales=scales[:].rearrange("p h n -> p (h n)"),
+                in_=tiles["w_parts", n0][:].rearrange("p h n j -> p (h n j)"),
+            )
+
+        def x_cast(t0, engine):
+            a = t0 // CHUNK
+            if ("x_bf", a) not in tiles:
+                tiles["x_bf", a] = keep.tile([P, PACK, P, PACK], BF16, name="x_bf%d" % a, align_bytes=64)
+            raw = tiles["x_raw", t0]
+            m0 = (t0 % CHUNK) // PACK
+            m1 = m0 + raw.shape[2] // PACK
+            engines[engine](
+                out=tiles["x_bf", a][:, :, m0:m1, :].rearrange("p r m j -> p m j r"),
+                in_=raw[:].rearrange("p j (m r) -> p m j r", r=PACK),
+            )
+
+        def x_quantize(a):
+            codes = keep.tile([P, CHUNK], U32, name="x_codes%d" % a, align_bytes=64)
+            scales = keep.tile([P, CHUNK], U8, name="x_scales%d" % a, align_bytes=64)
+            nc.vector.quantize_mx(
+                out=codes[:].bitcast(FP8X4), scales=scales[:], in_=tiles["x_bf", a][:].rearrange("p r m j -> p (r m j)")
+            )
+            tiles["x_mx", a] = (codes, scales)
+
+        def multiply(a, nt):
+            x_codes, x_scales = tiles["x_mx", a]
+            w_codes, w_scales, c0 = tiles["w_tile", nt]
+            acc = bank("sum")
+            tiles["acc", a, nt] = acc
+            if (a, nt) in TOKEN_MAJOR:
+                for r in range(PACK):
+                    for h in range(2):
+                        nc.tensor.matmul_mx(
+                            out=acc[:, r, :],
+                            lhsT=x_codes[:, r * P : (r + 1) * P].bitcast(FP8X4),
+                            lhsT_scale=x_scales[:, r * P : (r + 1) * P],
+                            rhs=w_codes[:, h, c0 : c0 + P].bitcast(FP8X4),
+                            rhs_scale=w_scales[:, h, c0 : c0 + P],
+                            start=(h == 0),
+                            stop=(h == 1),
+                        )
+            else:
+                for h in range(2):
+                    nc.tensor.matmul_mx(
+                        out=acc[:].rearrange("p r m -> p (r m)"),
+                        lhsT=w_codes[:, h, c0 : c0 + P].bitcast(FP8X4),
+                        lhsT_scale=w_scales[:, h, c0 : c0 + P],
+                        rhs=x_codes[:].bitcast(FP8X4),
+                        rhs_scale=x_scales[:],
+                        start=(h == 0),
+                        stop=(h == 1),
+                    )
+
+        def result_tile(a, nt):
+            g0, g1 = [g for g in GROUPS if g[0] <= nt * P < g[1]][0]
+            if ("res", a, g0) not in tiles:
+                tiles["res", a, g0] = keep.tile([P, PACK, g1 - g0], F32, name="res%d_%d" % (a, g0))
+            return tiles["res", a, g0][:, :, nt * P - g0 : (nt + 1) * P - g0]
+
+        def add_bias(a, nt):
+            mid = keep.tile([P, PACK, P], F32, name="mid", bufs=MID_BUFS)
+            nc.vector.tensor_tensor(
+                out=mid[:],
+                in0=tiles["acc", a, nt][:],
+                in1=bias_rows[:, BIAS_TILES.index(nt), :].unsqueeze(1).to_broadcast([P, PACK, P]),
+                op=ALU.add,
+            )
+            tiles["mid", a, nt] = mid
+
+        def silu(a, nt):
+            if (a, nt) in TOKEN_MAJOR:
+                nc.scalar.activation(out=result_tile(a, nt), in_=tiles["mid", a, nt][:], func=SILU)
+            else:
+                mid = keep.tile([P, PACK, P], F32, name="mid", bufs=MID_BUFS)
+                nc.scalar.activation(out=mid[:], in_=tiles["acc", a, nt][:], func=SILU, bias=bias_cols[:, nt : nt + 1])
+                tiles["mid", a, nt] = mid
+
+        def turn(a, nt):
+            turned = bank("turn")
+            for r in range(PACK):
+                nc.tensor.transpose(turned[:, r, :], tiles["mid", a, nt][:, r, :], ident[:])
+            tiles["turned", a, nt] = turned
+
+        def copy_out(a, nt, engine):
+            engines[engine](out=result_tile(a, nt), in_=tiles["turned", a, nt][:])
+
+        def out_cast(a, n0, n1, engine):
+            g0, g1 = [g for g in GROUPS if g[0] <= n0 < g[1]][0]
+            rounded = keep.tile([P, n1 - n0, PACK], BF16, name="rounded%d_%d" % (a, n0), align_bytes=64)
+            engines[engine](
+                out=rounded[:].rearrange("p (c i) r -> p c r i", i=4),
+                in_=tiles["res", a, g0][:, :, n0 - g0 : n1 - g0].rearrange("p r (c i) -> p c r i", i=4),
+            )
+            tiles["rounded", a, n0] = rounded
+
+        def out_quantize(a, n0, n1):
+            nc.vector.quantize_mx(
+                out=out_codes[:, a, n0:n1].bitcast(FP8X4),
+                scales=out_scales[:, a, n0:n1],
+                in_=tiles["rounded", a, n0][:].rearrange("p n r -> p (n r)"),
+            )
+
+        def store_result(a, n0, n1):
+            g0, g1 = [g for g in GROUPS if g[0] <= n0 < g[1]][0]
+            rows = out_0[a * CHUNK : (a + 1) * CHUNK, n0:n1].rearrange("(p r) n -> p r n", r=PACK)
+            nc.sync.dma_start(out=rows, in_=tiles["res", a, g0][:, :, n0 - g0 : n1 - g0])
+
+        def store_codes(a, n0, n1):
+            words = out_1[a].rearrange("p n i -> p (n i)").bitcast(I32)
+            nc.sync.dma_start(out=words[:, n0:n1], in_=out_codes[:, a, n0:n1].bitcast(I32))
+
+        def store_scales(a0, a1, n0, n1, queues):
+            for q in range(4):
+                rows = out_2[a0:a1, 4 * q : 4 * q + 4, n0:n1].rearrange("a r n -> r a n").bitcast(I32)
+                queues[q].dma_start(out=rows, in_=out_scales[32 * q : 32 * q + 4, a0:a1, n0:n1].bitcast(I32))
+
+        out_codes = keep.tile([P, T // CHUNK, M], U32, name="out_codes", align_bytes=64)
+        out_scales = keep.tile([P, T // CHUNK, M], U8, name="out_scales", align_bytes=64)
+        ident = keep.tile([P, P], F32, name="ident")
+        b_raw = keep.tile([P, P], F32, name="b_raw")
+        bias_cols = keep.tile([P, M // P], F32, name="bias_cols")
+        bias_rows = keep.tile([P, max(1, len(BIAS_TILES)), P], F32, name="bias_rows")
+        warm = keep.tile([P, 8], F32, name="warm")
+
+        def constants():
+            nc.gpsimd.memset(b_raw[:], 0.0)
+            nc.scalar.dma_start(out=b_raw[0 : M // P, :], in_=b.rearrange("(c n) -> c n", n=P))
+            nc.gpsimd.memset(warm[:, 0:1], 0.0)
+            nc.scalar.activation(out=warm[:, 1:2], in_=warm[:, 0:1], func=SILU)
+            make_identity(nc, ident[:])
+
+        def bias_to_columns():
+            turned = bank("turn")
+            nc.tensor.transpose(turned[:, 0, :], b_raw[:], ident[:])
+            nc.scalar.copy(out=bias_cols[:], in_=turned[:, 0, 0 : M // P])
+
+        def bias_to_rows():
+            turned = bank("turn")
+            for i, nt in enumerate(BIAS_TILES):
+                nc.tensor.transpose(turned[:, i, :], bias_cols[:, nt : nt + 1].to_broadcast([P, P]), ident[:])
+            nc.scalar.copy(out=bias_rows[:], in_=turned[:, 0 : len(BIAS_TILES), :])
+
+        constants()
+        load_w(256, 512)
+        load_w(0, 128)
+        w_top(256, "V")
+        w_top(0, "V")
+        bias_to_columns()
+        load_x(0, 256)
+        w_mask(256)
+        load_x(256, 512)
+        w_mask(0)
+        w_low(256)
+        x_cast(0, "S")
+        w_low(0)
+        load_w(128, 256)
+        load_x(768, 1024)
+        w_top(128, "S")
+        x_cast(768, "S")
+        load_x(512, 768)
+        x_cast(256, "V")
+        w_quantize(0)
+        load_x(1024, 1536)
+        x_quantize(0)
+        multiply(0, 0)
+        w_mask(128)
+        w_quantize(256)
+        w_low(128)
+        x_cast(512, "V")
+        multiply(0, 3)
+        load_w(768, 1024)
+        silu(0, 0)
+        multiply(0, 2)
+        w_quantize(128)
+        load_w(512, 768)
+        x_quantize(1)
+        silu(0, 3)
+        silu(0, 2)
+        multiply(0, 1)
+        multiply(1, 0)
+        x_cast(1024, "V")
+        multiply(1, 1)
+        silu(0, 1)
+        w_top(768, "V")
+        silu(1, 0)
+        turn(0, 3)
+        x_quantize(2)
+        silu(1, 1)
+        copy_out(0, 3, "S")
+        turn(0, 2)
+        w_top(512, "V")
+        turn(1, 0)
+        w_mask(768)
+        turn(0, 0)
+        copy_out(0, 2, "S")
+        multiply(1, 2)
+        w_mask(512)
+        turn(1, 1)
+        copy_out(0, 0, "S")
+        turn(0, 1)
+        silu(1, 2)
+        multiply(2, 1)
+        copy_out(0, 1, "S")
+        multiply(1, 3)
+        copy_out(1, 1, "S")
+        multiply(2, 3)
+        multiply(2, 0)
+        silu(2, 1)
+        out_cast(0, 256, 512, "V")
+        copy_out(1, 0, "V")
+        multiply(2, 2)
+        turn(1, 2)
+        out_cast(0, 0, 256, "V")
+        silu(1, 3)
+        w_low(512)
+        out_quantize(0, 0, 256)
+        silu(2, 0)
+        turn(1, 3)
+        w_quantize(512)
+        turn(2, 0)
+        store_result(0, 256, 512)
+        out_quantize(0, 256, 512)
+        silu(2, 3)
+        turn(2, 1)
+        copy_out(1, 2, "S")
+        out_cast(1, 0, 256, "V")
+        copy_out(1, 3, "S")
+        copy_out(2, 1, "V")
+        copy_out(2, 0, "S")
+        multiply(0, 5)
+        out_cast(1, 256, 512, "V")
+        silu(2, 2)
+        multiply(0, 4)
+        out_quantize(1, 0, 256)
+        multiply(1, 5)
+        out_quantize(1, 256, 512)
+        turn(2, 3)
+        turn(2, 2)
+        w_low(768)
+        silu(0, 4)
+        silu(0, 5)
+        turn(0, 4)
+        store_result(0, 0, 256)
+        turn(0, 5)
+        multiply(2, 5)
+        store_result(1, 0, 256)
+        copy_out(2, 3, "S")
+        multiply(1, 4)
+        copy_out(0, 5, "V")
+        copy_out(2, 2, "S")
+        w_quantize(768)
+        silu(1, 5)
+        out_cast(2, 256, 512, "V")
+        copy_out(0, 4, "S")
+        store_codes(0, 0, 512)
+        store_result(1, 256, 512)
+        out_cast(2, 0, 256, "V")
+        silu(1, 4)
+        silu(2, 5)
+        multiply(2, 4)
+        multiply(0, 7)
+        turn(1, 5)
+        store_result(2, 0, 256)
+        turn(1, 4)
+        silu(2, 4)
+        turn(2, 5)
+        multiply(2, 6)
+        store_codes(1, 0, 512)
+        copy_out(1, 5, "S")
+        out_quantize(2, 256, 512)
+        out_quantize(2, 0, 256)
+        silu(0, 7)
+        out_cast(0, 512, 768, "V")
+        multiply(0, 6)
+        turn(2, 4)
+        turn(0, 7)
+        copy_out(1, 4, "V")
+        silu(2, 6)
+        copy_out(2, 4, "S")
+        store_result(2, 256, 512)
+        store_result(0, 512, 768)
+        out_quantize(0, 512, 768)
+        out_cast(1, 512, 768, "V")
+        multiply(2, 7)
+        silu(0, 6)
+        copy_out(2, 5, "V")
+        turn(2, 6)
+        silu(2, 7)
+        store_codes(2, 0, 512)
+        out_quantize(1, 512, 768)
+        store_scales(0, 3, 0, 512, [nc.sync] * 4)
+        store_result(1, 512, 768)
+        out_cast(2, 512, 768, "V")
+        copy_out(0, 7, "S")
+        turn(0, 6)
+        multiply(1, 7)
+        copy_out(2, 6, "V")
+        store_codes(0, 512, 768)
+        store_result(2, 512, 768)
+        copy_out(0, 6, "V")
+        out_cast(2, 768, 896, "V")
+        out_cast(0, 768, 1024, "V")
+        multiply(1, 6)
+        silu(1, 7)
+        turn(2, 7)
+        out_quantize(2, 512, 768)
+        store_codes(1, 512, 768)
+        silu(1, 6)
+        out_quantize(2, 768, 896)
+        turn(1, 7)
+        turn(1, 6)
+        out_quantize(0, 768, 1024)
+        copy_out(2, 7, "S")
+        store_result(2, 768, 896)
+        copy_out(1, 6, "S")
+        copy_out(1, 7, "V")
+        out_cast(2, 896, 1024, "V")
+        store_result(0, 768, 1024)
+        store_codes(2, 512, 768)
+        out_cast(1, 768, 1024, "V")
+        store_result(2, 896, 1024)
+        out_quantize(2, 896, 1024)
+        out_quantize(1, 768, 1024)
+        store_codes(0, 768, 1024)
+        store_result(1, 768, 1024)
+        store_codes(2, 768, 1024)
+        store_codes(1, 768, 1024)
+        store_scales(0, 3, 512, 1024, [nc.sync, nc.scalar, nc.sync, nc.scalar])

@@ -21,10 +21,10 @@ CHUNK = P * PACK
 QUARTER = 256
 HI_MASK_PAIR = 0xFFF0FFF0 - (1 << 32)
 BANKS = {"sum": 4, "turn": 4}
-MID_BUFS = 6
-GROUPS = [(0, 256), (256, 512), (512, 768), (768, 1024)]
-BIAS_TILES = []
-TOKEN_MAJOR = []
+MID_BUFS = 12
+W_PIECES = [[0,128],[128,256],[256,384],[384,512],[512,768],[768,1024]]
+X_PIECES = [[0,256],[256,512],[512,768],[768,1024],[1024,1536]]
+TOKEN_MAJOR = [(0, 1), (1, 1)]
 
 
 def tile_mix_hilo_tm_pl_silu_kernel(tc, w, x, b, out_0, out_1, out_2):
@@ -44,26 +44,30 @@ def tile_mix_hilo_tm_pl_silu_kernel(tc, w, x, b, out_0, out_1, out_2):
         def bank(kind):
             index = bank_count[kind] % BANKS[kind]
             bank_count[kind] = bank_count[kind] + 1
-            return psum.tile([P, PACK, P], F32, name="%s%d" % (kind, index))
+            return psum.tile([P, CHUNK], F32, name="%s%d" % (kind, index))
 
         def load_w(n0, n1):
             raw = keep.tile([P, PACK, n1 - n0], F32, name="w_raw%d" % n0)
             nc.sync.dma_start(out=raw[:], in_=w_rows[:, :, n0:n1])
-            tiles["w_raw", n0] = raw
-            tiles["w_parts", n0] = keep.tile([P, 2, n1 - n0, PACK], BF16, name="w_parts%d" % n0, align_bytes=64)
-            codes = keep.tile([P, 2, n1 - n0], U32, name="w_codes%d" % n0, align_bytes=64)
-            scales = keep.tile([P, 2, n1 - n0], U8, name="w_scales%d" % n0, align_bytes=64)
-            tiles["w_mx", n0] = (codes, scales)
-            for n in range(n0, n1, P):
-                tiles["w_tile", n // P] = (codes, scales, n - n0)
+            for m0, m1 in W_PIECES:
+                if n0 <= m0 < n1:
+                    tiles["w_raw", m0] = raw[:, :, m0 - n0 : m1 - n0]
+                    tiles["w_parts", m0] = keep.tile([P, 2, m1 - m0, PACK], BF16, name="w_parts%d" % m0, align_bytes=64)
+                    codes = keep.tile([P, 2, m1 - m0], U32, name="w_codes%d" % m0, align_bytes=64)
+                    scales = keep.tile([P, 2, m1 - m0], U8, name="w_scales%d" % m0, align_bytes=64)
+                    tiles["w_mx", m0] = (codes, scales)
+                    for n in range(m0, m1, P):
+                        tiles["w_tile", n // P] = (codes, scales, n - m0)
 
         def load_x(t0, t1):
             raw = keep.tile([P, PACK, t1 - t0], F32, name="x_raw%d" % t0)
             nc.sync.dma_start(out=raw[:], in_=x_rows[:, :, t0:t1])
-            tiles["x_raw", t0] = raw
+            for m0, m1 in X_PIECES:
+                if t0 <= m0 < t1:
+                    tiles["x_raw", m0] = raw[:, :, m0 - t0 : m1 - t0]
 
         def w_top(n0, engine):
-            halves = tiles["w_raw", n0][:].bitcast(BF16).rearrange("p j (c i e) -> p c j i e", i=4, e=2)
+            halves = tiles["w_raw", n0].bitcast(BF16).rearrange("p j (c i e) -> p c j i e", i=4, e=2)
             top = tiles["w_parts", n0][:, 0].rearrange("p (c i) j -> p c j i", i=4)
             engines[engine](out=top, in_=halves[:, :, :, :, 1])
 
@@ -75,7 +79,7 @@ def tile_mix_hilo_tm_pl_silu_kernel(tc, w, x, b, out_0, out_1, out_2):
             parts = tiles["w_parts", n0]
             nc.vector.tensor_tensor(
                 out=parts[:, 1].rearrange("p (c i) j -> p c j i", i=4),
-                in0=tiles["w_raw", n0][:].rearrange("p j (c i) -> p c j i", i=4),
+                in0=tiles["w_raw", n0].rearrange("p j (c i) -> p c j i", i=4),
                 in1=parts[:, 0].rearrange("p (c i) j -> p c j i", i=4),
                 op=ALU.subtract,
             )
@@ -97,7 +101,7 @@ def tile_mix_hilo_tm_pl_silu_kernel(tc, w, x, b, out_0, out_1, out_2):
             m1 = m0 + raw.shape[2] // PACK
             engines[engine](
                 out=tiles["x_bf", a][:, :, m0:m1, :].rearrange("p r m j -> p m j r"),
-                in_=raw[:].rearrange("p j (m r) -> p m j r", r=PACK),
+                in_=raw.rearrange("p j (m r) -> p m j r", r=PACK),
             )
 
         def x_quantize(a):
@@ -110,72 +114,71 @@ def tile_mix_hilo_tm_pl_silu_kernel(tc, w, x, b, out_0, out_1, out_2):
 
         def multiply(a, nt):
             x_codes, x_scales = tiles["x_mx", a]
-            w_codes, w_scales, c0 = tiles["w_tile", nt]
             acc = bank("sum")
             tiles["acc", a, nt] = acc
-            if (a, nt) in TOKEN_MAJOR:
-                for r in range(PACK):
-                    for h in range(2):
-                        nc.tensor.matmul_mx(
-                            out=acc[:, r, :],
-                            lhsT=x_codes[:, r * P : (r + 1) * P].bitcast(FP8X4),
-                            lhsT_scale=x_scales[:, r * P : (r + 1) * P],
-                            rhs=w_codes[:, h, c0 : c0 + P].bitcast(FP8X4),
-                            rhs_scale=w_scales[:, h, c0 : c0 + P],
-                            start=(h == 0),
-                            stop=(h == 1),
-                        )
+            if (a, nt // PACK) in TOKEN_MAJOR:
+                r = nt % PACK
+                half = nt // PACK * CHUNK
+                for m0, m1 in W_PIECES:
+                    if half <= m0 < half + CHUNK:
+                        w_codes, w_scales = tiles["w_mx", m0]
+                        for part in range(2):
+                            nc.tensor.matmul_mx(
+                                out=acc[:, m0 - half : m1 - half],
+                                lhsT=x_codes[:, r * P : (r + 1) * P].bitcast(FP8X4),
+                                lhsT_scale=x_scales[:, r * P : (r + 1) * P],
+                                rhs=w_codes[:, part, :].bitcast(FP8X4),
+                                rhs_scale=w_scales[:, part, :],
+                                start=(part == 0),
+                                stop=(part == 1),
+                            )
             else:
-                for h in range(2):
+                w_codes, w_scales, c0 = tiles["w_tile", nt]
+                for part in range(2):
                     nc.tensor.matmul_mx(
-                        out=acc[:].rearrange("p r m -> p (r m)"),
-                        lhsT=w_codes[:, h, c0 : c0 + P].bitcast(FP8X4),
-                        lhsT_scale=w_scales[:, h, c0 : c0 + P],
+                        out=acc[:],
+                        lhsT=w_codes[:, part, c0 : c0 + P].bitcast(FP8X4),
+                        lhsT_scale=w_scales[:, part, c0 : c0 + P],
                         rhs=x_codes[:].bitcast(FP8X4),
                         rhs_scale=x_scales[:],
-                        start=(h == 0),
-                        stop=(h == 1),
+                        start=(part == 0),
+                        stop=(part == 1),
                     )
 
-        def result_tile(a, nt):
-            g0, g1 = [g for g in GROUPS if g[0] <= nt * P < g[1]][0]
-            if ("res", a, g0) not in tiles:
-                tiles["res", a, g0] = keep.tile([P, PACK, g1 - g0], F32, name="res%d_%d" % (a, g0))
-            return tiles["res", a, g0][:, :, nt * P - g0 : (nt + 1) * P - g0]
+        def result_tile(a, h):
+            if ("res", a, h) not in tiles:
+                tiles["res", a, h] = keep.tile([P, PACK, CHUNK], F32, name="res%d_%d" % (a, h))
+            return tiles["res", a, h]
 
         def add_bias(a, nt):
-            mid = keep.tile([P, PACK, P], F32, name="mid", bufs=MID_BUFS)
-            nc.vector.tensor_tensor(
-                out=mid[:],
-                in0=tiles["acc", a, nt][:],
-                in1=bias_rows[:, BIAS_TILES.index(nt), :].unsqueeze(1).to_broadcast([P, PACK, P]),
-                op=ALU.add,
-            )
+            mid = keep.tile([P, CHUNK], F32, name="mid", bufs=MID_BUFS)
+            nc.vector.tensor_tensor(out=mid[:], in0=tiles["acc", a, nt][:], in1=bias_rows[:], op=ALU.add)
             tiles["mid", a, nt] = mid
 
         def silu(a, nt):
-            if (a, nt) in TOKEN_MAJOR:
-                nc.scalar.activation(out=result_tile(a, nt), in_=tiles["mid", a, nt][:], func=SILU)
+            if (a, nt // PACK) in TOKEN_MAJOR:
+                nc.scalar.activation(out=result_tile(a, nt // PACK)[:, nt % PACK, :], in_=tiles["mid", a, nt][:], func=SILU)
             else:
-                mid = keep.tile([P, PACK, P], F32, name="mid", bufs=MID_BUFS)
+                mid = keep.tile([P, CHUNK], F32, name="mid", bufs=MID_BUFS)
                 nc.scalar.activation(out=mid[:], in_=tiles["acc", a, nt][:], func=SILU, bias=bias_cols[:, nt : nt + 1])
                 tiles["mid", a, nt] = mid
 
         def turn(a, nt):
             turned = bank("turn")
-            for r in range(PACK):
-                nc.tensor.transpose(turned[:, r, :], tiles["mid", a, nt][:, r, :], ident[:])
+            h, r = divmod(nt, PACK)
+            for j in range(PACK):
+                nc.tensor.transpose(turned[:, j * P : (j + 1) * P], tiles["mid", a, h * PACK + j][:, r * P : (r + 1) * P], ident[:])
             tiles["turned", a, nt] = turned
 
         def copy_out(a, nt, engine):
-            engines[engine](out=result_tile(a, nt), in_=tiles["turned", a, nt][:])
+            engines[engine](out=result_tile(a, nt // PACK)[:, nt % PACK, :], in_=tiles["turned", a, nt][:])
 
         def out_cast(a, n0, n1, engine):
-            g0, g1 = [g for g in GROUPS if g[0] <= n0 < g[1]][0]
+            h = n0 // CHUNK
             rounded = keep.tile([P, n1 - n0, PACK], BF16, name="rounded%d_%d" % (a, n0), align_bytes=64)
             engines[engine](
                 out=rounded[:].rearrange("p (c i) r -> p c r i", i=4),
-                in_=tiles["res", a, g0][:, :, n0 - g0 : n1 - g0].rearrange("p r (c i) -> p c r i", i=4),
+                in_=tiles["res", a, h][:, :, n0 - h * CHUNK : n1 - h * CHUNK].rearrange("p r (c i) -> p c r i", i=4),
             )
             tiles["rounded", a, n0] = rounded
 
@@ -186,10 +189,9 @@ def tile_mix_hilo_tm_pl_silu_kernel(tc, w, x, b, out_0, out_1, out_2):
                 in_=tiles["rounded", a, n0][:].rearrange("p n r -> p (n r)"),
             )
 
-        def store_result(a, n0, n1):
-            g0, g1 = [g for g in GROUPS if g[0] <= n0 < g[1]][0]
-            rows = out_0[a * CHUNK : (a + 1) * CHUNK, n0:n1].rearrange("(p r) n -> p r n", r=PACK)
-            nc.sync.dma_start(out=rows, in_=tiles["res", a, g0][:, :, n0 - g0 : n1 - g0])
+        def store_result(a, h, r0, r1):
+            rows = out_0[a * CHUNK : (a + 1) * CHUNK, h * CHUNK : (h + 1) * CHUNK].rearrange("(p r) n -> p r n", r=PACK)
+            nc.sync.dma_start(out=rows[:, r0:r1, :], in_=tiles["res", a, h][:, r0:r1, :])
 
         def store_codes(a, n0, n1):
             words = out_1[a].rearrange("p n i -> p (n i)").bitcast(I32)
@@ -205,7 +207,7 @@ def tile_mix_hilo_tm_pl_silu_kernel(tc, w, x, b, out_0, out_1, out_2):
         ident = keep.tile([P, P], F32, name="ident")
         b_raw = keep.tile([P, P], F32, name="b_raw")
         bias_cols = keep.tile([P, M // P], F32, name="bias_cols")
-        bias_rows = keep.tile([P, max(1, len(BIAS_TILES)), P], F32, name="bias_rows")
+        bias_rows = keep.tile([P, CHUNK], F32, name="bias_rows")
         warm = keep.tile([P, 8], F32, name="warm")
 
         def constants():
@@ -217,198 +219,185 @@ def tile_mix_hilo_tm_pl_silu_kernel(tc, w, x, b, out_0, out_1, out_2):
 
         def bias_to_columns():
             turned = bank("turn")
-            nc.tensor.transpose(turned[:, 0, :], b_raw[:], ident[:])
-            nc.scalar.copy(out=bias_cols[:], in_=turned[:, 0, 0 : M // P])
+            nc.tensor.transpose(turned[:, 0:P], b_raw[:], ident[:])
+            nc.scalar.copy(out=bias_cols[:], in_=turned[:, 0 : M // P])
 
         def bias_to_rows():
             turned = bank("turn")
-            for i, nt in enumerate(BIAS_TILES):
-                nc.tensor.transpose(turned[:, i, :], bias_cols[:, nt : nt + 1].to_broadcast([P, P]), ident[:])
-            nc.scalar.copy(out=bias_rows[:], in_=turned[:, 0 : len(BIAS_TILES), :])
+            for j in range(PACK):
+                nc.tensor.transpose(turned[:, j * P : (j + 1) * P], bias_cols[:, PACK + j : PACK + j + 1].to_broadcast([P, P]), ident[:])
+            nc.scalar.copy(out=bias_rows[:], in_=turned[:])
 
         constants()
-        load_w(256, 512)
-        load_w(0, 128)
-        w_top(256, "V")
-        w_top(0, "V")
-        bias_to_columns()
-        load_x(0, 256)
-        w_mask(256)
-        load_x(256, 512)
-        w_mask(0)
-        w_low(256)
-        x_cast(0, "S")
-        w_low(0)
-        load_w(128, 256)
-        load_x(768, 1024)
+        load_w(0, 256)
         w_top(128, "S")
-        x_cast(768, "S")
-        load_x(512, 768)
-        x_cast(256, "V")
-        w_quantize(0)
-        load_x(1024, 1536)
-        x_quantize(0)
-        multiply(0, 0)
+        w_top(0, "V")
+        load_x(0, 512)
+        load_w(256, 512)
+        w_mask(0)
+        w_low(0)
         w_mask(128)
-        w_quantize(256)
+        w_quantize(0)
         w_low(128)
-        x_cast(512, "V")
-        multiply(0, 3)
-        load_w(768, 1024)
-        silu(0, 0)
-        multiply(0, 2)
+        bias_to_columns()
+        x_cast(256, "V")
         w_quantize(128)
-        load_w(512, 768)
-        x_quantize(1)
-        silu(0, 3)
-        silu(0, 2)
+        bias_to_rows()
+        x_cast(0, "S")
+        w_top(256, "S")
+        load_x(512, 1024)
+        x_quantize(0)
+        w_top(384, "V")
+        w_mask(256)
         multiply(0, 1)
-        multiply(1, 0)
-        x_cast(1024, "V")
-        multiply(1, 1)
+        w_mask(384)
+        load_w(512, 1024)
+        w_low(256)
+        w_low(384)
+        multiply(0, 0)
         silu(0, 1)
-        w_top(768, "V")
-        silu(1, 0)
-        turn(0, 3)
-        x_quantize(2)
-        silu(1, 1)
-        copy_out(0, 3, "S")
-        turn(0, 2)
-        w_top(512, "V")
-        turn(1, 0)
-        w_mask(768)
-        turn(0, 0)
-        copy_out(0, 2, "S")
-        multiply(1, 2)
-        w_mask(512)
-        turn(1, 1)
-        copy_out(0, 0, "S")
-        turn(0, 1)
-        silu(1, 2)
-        multiply(2, 1)
-        copy_out(0, 1, "S")
+        w_quantize(384)
+        x_cast(512, "S")
+        w_quantize(256)
+        x_cast(768, "V")
+        multiply(0, 2)
+        multiply(0, 3)
+        silu(0, 0)
+        load_x(1024, 1536)
+        silu(0, 2)
+        x_quantize(1)
+        multiply(1, 1)
         multiply(1, 3)
-        copy_out(1, 1, "S")
-        multiply(2, 3)
-        multiply(2, 0)
-        silu(2, 1)
-        out_cast(0, 256, 512, "V")
-        copy_out(1, 0, "V")
-        multiply(2, 2)
-        turn(1, 2)
-        out_cast(0, 0, 256, "V")
-        silu(1, 3)
-        w_low(512)
-        out_quantize(0, 0, 256)
-        silu(2, 0)
-        turn(1, 3)
-        w_quantize(512)
-        turn(2, 0)
-        store_result(0, 256, 512)
-        out_quantize(0, 256, 512)
-        silu(2, 3)
-        turn(2, 1)
-        copy_out(1, 2, "S")
-        out_cast(1, 0, 256, "V")
-        copy_out(1, 3, "S")
-        copy_out(2, 1, "V")
-        copy_out(2, 0, "S")
-        multiply(0, 5)
-        out_cast(1, 256, 512, "V")
-        silu(2, 2)
-        multiply(0, 4)
-        out_quantize(1, 0, 256)
-        multiply(1, 5)
-        out_quantize(1, 256, 512)
-        turn(2, 3)
-        turn(2, 2)
+        w_top(768, "V")
+        multiply(1, 0)
+        silu(0, 3)
+        w_top(512, "V")
+        turn(0, 3)
+        w_mask(768)
+        silu(1, 1)
+        w_mask(512)
         w_low(768)
-        silu(0, 4)
-        silu(0, 5)
-        turn(0, 4)
-        store_result(0, 0, 256)
-        turn(0, 5)
-        multiply(2, 5)
-        store_result(1, 0, 256)
-        copy_out(2, 3, "S")
-        multiply(1, 4)
-        copy_out(0, 5, "V")
-        copy_out(2, 2, "S")
+        silu(1, 3)
+        x_cast(1024, "V")
+        turn(0, 0)
+        turn(0, 1)
+        silu(1, 0)
+        copy_out(0, 3, "S")
+        multiply(1, 2)
+        copy_out(0, 0, "S")
         w_quantize(768)
-        silu(1, 5)
-        out_cast(2, 256, 512, "V")
-        copy_out(0, 4, "S")
-        store_codes(0, 0, 512)
-        store_result(1, 256, 512)
-        out_cast(2, 0, 256, "V")
-        silu(1, 4)
-        silu(2, 5)
-        multiply(2, 4)
+        turn(0, 2)
+        silu(1, 2)
+        x_quantize(2)
+        copy_out(0, 1, "S")
+        copy_out(0, 2, "S")
+        turn(1, 3)
+        turn(1, 2)
+        turn(1, 1)
+        turn(1, 0)
+        store_result(0, 0, 0, 2)
+        multiply(2, 3)
+        w_low(512)
+        copy_out(1, 0, "V")
+        store_result(0, 0, 2, 4)
+        multiply(2, 0)
+        copy_out(1, 3, "S")
+        multiply(2, 1)
+        copy_out(1, 2, "S")
+        copy_out(1, 1, "S")
+        multiply(2, 2)
+        silu(2, 3)
+        silu(2, 0)
+        w_quantize(512)
+        silu(2, 1)
+        silu(2, 2)
+        multiply(0, 5)
+        out_cast(0, 0, 256, "V")
+        multiply(0, 4)
+        out_cast(0, 256, 512, "V")
+        out_quantize(0, 0, 256)
+        add_bias(0, 5)
+        turn(2, 1)
+        store_result(1, 0, 0, 2)
+        turn(2, 0)
+        turn(2, 3)
+        out_quantize(0, 256, 512)
+        copy_out(2, 1, "V")
+        add_bias(0, 4)
+        out_cast(1, 0, 256, "S")
+        out_cast(1, 256, 512, "V")
+        store_result(1, 0, 2, 4)
+        turn(2, 2)
         multiply(0, 7)
-        turn(1, 5)
-        store_result(2, 0, 256)
-        turn(1, 4)
-        silu(2, 4)
-        turn(2, 5)
-        multiply(2, 6)
-        store_codes(1, 0, 512)
-        copy_out(1, 5, "S")
-        out_quantize(2, 256, 512)
-        out_quantize(2, 0, 256)
-        silu(0, 7)
-        out_cast(0, 512, 768, "V")
         multiply(0, 6)
-        turn(2, 4)
-        turn(0, 7)
-        copy_out(1, 4, "V")
-        silu(2, 6)
-        copy_out(2, 4, "S")
-        store_result(2, 256, 512)
-        store_result(0, 512, 768)
-        out_quantize(0, 512, 768)
-        out_cast(1, 512, 768, "V")
-        multiply(2, 7)
-        silu(0, 6)
-        copy_out(2, 5, "V")
-        turn(2, 6)
-        silu(2, 7)
-        store_codes(2, 0, 512)
-        out_quantize(1, 512, 768)
-        store_scales(0, 3, 0, 512, [nc.sync] * 4)
-        store_result(1, 512, 768)
-        out_cast(2, 512, 768, "V")
-        copy_out(0, 7, "S")
-        turn(0, 6)
-        multiply(1, 7)
-        copy_out(2, 6, "V")
-        store_codes(0, 512, 768)
-        store_result(2, 512, 768)
-        copy_out(0, 6, "V")
-        out_cast(2, 768, 896, "V")
-        out_cast(0, 768, 1024, "V")
+        copy_out(2, 0, "S")
+        multiply(1, 4)
+        multiply(1, 5)
+        add_bias(0, 7)
+        add_bias(0, 6)
+        out_quantize(1, 0, 256)
+        silu(0, 5)
         multiply(1, 6)
+        multiply(1, 7)
+        add_bias(1, 4)
+        silu(0, 4)
+        add_bias(1, 5)
+        multiply(2, 5)
+        add_bias(1, 6)
+        copy_out(2, 3, "S")
+        copy_out(2, 2, "S")
+        add_bias(1, 7)
+        multiply(2, 7)
+        out_cast(2, 0, 256, "V")
+        out_quantize(1, 256, 512)
+        out_cast(2, 256, 512, "V")
+        out_quantize(2, 0, 256)
+        silu(0, 6)
+        silu(0, 7)
+        multiply(2, 6)
+        silu(1, 4)
+        store_codes(0, 0, 512)
+        silu(1, 5)
+        silu(2, 5)
+        silu(2, 7)
+        multiply(2, 4)
+        store_result(2, 0, 0, 2)
+        out_quantize(2, 256, 512)
+        out_cast(0, 512, 768, "V")
+        out_cast(0, 768, 1024, "V")
+        silu(2, 6)
+        silu(2, 4)
         silu(1, 7)
-        turn(2, 7)
-        out_quantize(2, 512, 768)
-        store_codes(1, 512, 768)
-        silu(1, 6)
-        out_quantize(2, 768, 896)
-        turn(1, 7)
-        turn(1, 6)
+        turn(2, 6)
+        out_quantize(0, 512, 768)
         out_quantize(0, 768, 1024)
-        copy_out(2, 7, "S")
-        store_result(2, 768, 896)
-        copy_out(1, 6, "S")
-        copy_out(1, 7, "V")
-        out_cast(2, 896, 1024, "V")
-        store_result(0, 768, 1024)
-        store_codes(2, 512, 768)
+        turn(2, 4)
+        store_result(0, 1, 0, 2)
+        store_result(2, 0, 2, 4)
+        store_result(0, 1, 2, 4)
+        silu(1, 6)
+        turn(2, 7)
+        store_result(1, 1, 0, 2)
+        turn(2, 5)
+        store_codes(1, 0, 512)
         out_cast(1, 768, 1024, "V")
-        store_result(2, 896, 1024)
-        out_quantize(2, 896, 1024)
+        copy_out(2, 5, "V")
+        store_scales(0, 3, 0, 512, [nc.sync] * 4)
+        copy_out(2, 6, "S")
         out_quantize(1, 768, 1024)
-        store_codes(0, 768, 1024)
-        store_result(1, 768, 1024)
-        store_codes(2, 768, 1024)
-        store_codes(1, 768, 1024)
-        store_scales(0, 3, 512, 1024, [nc.sync, nc.scalar, nc.sync, nc.scalar])
+        store_codes(2, 0, 512)
+        copy_out(2, 7, "S")
+        copy_out(2, 4, "S")
+        store_result(1, 1, 2, 4)
+        out_cast(2, 512, 768, "V")
+        store_result(2, 1, 2, 4)
+        out_cast(1, 512, 768, "V")
+        out_cast(2, 768, 1024, "V")
+        out_quantize(1, 512, 768)
+        store_result(2, 1, 0, 2)
+        store_codes(0, 512, 1024)
+        store_codes(1, 512, 1024)
+        out_quantize(2, 512, 768)
+        out_quantize(2, 768, 1024)
+        store_codes(2, 512, 1024)
+        store_scales(0, 3, 512, 1024, [nc.scalar] * 4)

@@ -18,18 +18,24 @@ SILU = mybir.ActivationFunctionType.Silu
 P = 128
 PACK = 4
 CHUNK = P * PACK
-QUARTER = 256
-HI_MASK_PAIR = 0xFFF0FFF0 - (1 << 32)
-BANKS = {"sum": 4, "turn": 4}
+CHUNKS = T // CHUNK
+HALF = M // 2
+QUARTER = M // 4
+LOW_TILES = range(0, 4)
+HIGH_TILES = range(4, 8)
+RUN = 4
+BANKS = 4
 MID_BUFS = 12
-W_PIECES = [[0,128],[128,256],[256,384],[384,512],[512,768],[768,1024]]
-X_PIECES = [[0,256],[256,512],[512,768],[768,1024],[1024,1536]]
-TOKEN_MAJOR = [(0, 1), (1, 1)]
+HI_MASK_PAIR = 0xFFF0FFF0 - (1 << 32)
+
+W_PIECES = {0: 256, 256: 384, 384: 512, 512: 768, 768: 1024}
+X_PIECES = {0: 256, 256: 512, 512: 1024, 1024: 1536}
 
 
 def tile_mix_hilo_tm_pl_silu_kernel(tc, w, x, b, out_0, out_1, out_2):
     nc = tc.nc
-    engines = {"V": nc.vector.tensor_copy, "S": nc.scalar.copy}
+    on_vector = nc.vector.tensor_copy
+    on_scalar = nc.scalar.copy
 
     with ExitStack() as ctx:
         keep = ctx.enter_context(tc.tile_pool(name="keep", bufs=1))
@@ -38,366 +44,279 @@ def tile_mix_hilo_tm_pl_silu_kernel(tc, w, x, b, out_0, out_1, out_2):
 
         w_rows = w.rearrange("(p j) n -> p j n", j=PACK)
         x_rows = x.rearrange("(p j) t -> p j t", j=PACK)
-        tiles = {}
-        bank_count = {"sum": 0, "turn": 0}
+        w_raw, w_parts, w_mx = {}, {}, {}
+        x_raw, x_dealt, x_mx = {}, {}, {}
+        sums, mids, turned, results, rounded = {}, {}, {}, {}, {}
+        banks_taken = {"sum": 0, "turn": 0}
 
-        def bank(kind):
-            index = bank_count[kind] % BANKS[kind]
-            bank_count[kind] = bank_count[kind] + 1
-            return psum.tile([P, CHUNK], F32, name="%s%d" % (kind, index))
+        def next_bank(kind):
+            index = banks_taken[kind] % BANKS
+            banks_taken[kind] = banks_taken[kind] + 1
+            return psum.tile([P, PACK, P], F32, name="%s%d" % (kind, index))
 
-        def load_w(n0, n1):
-            raw = keep.tile([P, PACK, n1 - n0], F32, name="w_raw%d" % n0)
-            nc.sync.dma_start(out=raw[:], in_=w_rows[:, :, n0:n1])
-            for m0, m1 in W_PIECES:
-                if n0 <= m0 < n1:
-                    tiles["w_raw", m0] = raw[:, :, m0 - n0 : m1 - n0]
-                    tiles["w_parts", m0] = keep.tile([P, 2, m1 - m0, PACK], BF16, name="w_parts%d" % m0, align_bytes=64)
-                    codes = keep.tile([P, 2, m1 - m0], U32, name="w_codes%d" % m0, align_bytes=64)
-                    scales = keep.tile([P, 2, m1 - m0], U8, name="w_scales%d" % m0, align_bytes=64)
-                    tiles["w_mx", m0] = (codes, scales)
-                    for n in range(m0, m1, P):
-                        tiles["w_tile", n // P] = (codes, scales, n - m0)
 
-        def load_x(t0, t1):
-            raw = keep.tile([P, PACK, t1 - t0], F32, name="x_raw%d" % t0)
-            nc.sync.dma_start(out=raw[:], in_=x_rows[:, :, t0:t1])
-            for m0, m1 in X_PIECES:
-                if t0 <= m0 < t1:
-                    tiles["x_raw", m0] = raw[:, :, m0 - t0 : m1 - t0]
+        def load(name, rows, pieces, views, c0, c1):
+            raw = keep.tile([P, PACK, c1 - c0], F32, name="%s_raw%d" % (name, c0))
+            nc.sync.dma_start(out=raw[:], in_=rows[:, :, c0:c1])
+            for start in pieces:
+                if c0 <= start < c1:
+                    views[start] = raw[:, :, start - c0 : pieces[start] - c0]
 
-        def w_top(n0, engine):
-            halves = tiles["w_raw", n0].bitcast(BF16).rearrange("p j (c i e) -> p c j i e", i=4, e=2)
-            top = tiles["w_parts", n0][:, 0].rearrange("p (c i) j -> p c j i", i=4)
-            engines[engine](out=top, in_=halves[:, :, :, :, 1])
+        def w_top(n0, copy):
+            parts = keep.tile([P, 2, W_PIECES[n0] - n0, PACK], BF16, name="w_parts%d" % n0, align_bytes=64)
+            halves = w_raw[n0].bitcast(BF16).rearrange("p j (c i e) -> p c j i e", i=RUN, e=2)
+            copy(out=parts[:, 0].rearrange("p (c i) j -> p c j i", i=RUN), in_=halves[:, :, :, :, 1])
+            w_parts[n0] = parts
 
         def w_mask(n0):
-            pairs = tiles["w_parts", n0][:, 0].rearrange("p n j -> p (n j)").bitcast(I32)
+            pairs = w_parts[n0][:, 0].rearrange("p n j -> p (n j)").bitcast(I32)
             nc.vector.tensor_scalar(out=pairs, in0=pairs, scalar1=HI_MASK_PAIR, scalar2=None, op0=ALU.bitwise_and)
 
         def w_low(n0):
-            parts = tiles["w_parts", n0]
             nc.vector.tensor_tensor(
-                out=parts[:, 1].rearrange("p (c i) j -> p c j i", i=4),
-                in0=tiles["w_raw", n0].rearrange("p j (c i) -> p c j i", i=4),
-                in1=parts[:, 0].rearrange("p (c i) j -> p c j i", i=4),
+                out=w_parts[n0][:, 1].rearrange("p (c i) j -> p c j i", i=RUN),
+                in0=w_raw[n0].rearrange("p j (c i) -> p c j i", i=RUN),
+                in1=w_parts[n0][:, 0].rearrange("p (c i) j -> p c j i", i=RUN),
                 op=ALU.subtract,
             )
 
         def w_quantize(n0):
-            codes, scales = tiles["w_mx", n0]
+            width = W_PIECES[n0] - n0
+            codes = keep.tile([P, 2, width], U32, name="w_codes%d" % n0, align_bytes=64)
+            scales = keep.tile([P, 2, width], U8, name="w_scales%d" % n0, align_bytes=64)
             nc.vector.quantize_mx(
                 out=codes[:].rearrange("p h n -> p (h n)").bitcast(FP8X4),
                 scales=scales[:].rearrange("p h n -> p (h n)"),
-                in_=tiles["w_parts", n0][:].rearrange("p h n j -> p (h n j)"),
+                in_=w_parts[n0][:].rearrange("p h n j -> p (h n j)"),
             )
+            for c0 in range(0, width, P):
+                w_mx[(n0 + c0) // P] = (codes[:, :, c0 : c0 + P], scales[:, :, c0 : c0 + P])
 
-        def x_cast(t0, engine):
+        def x_cast(t0, copy):
             a = t0 // CHUNK
-            if ("x_bf", a) not in tiles:
-                tiles["x_bf", a] = keep.tile([P, PACK, P, PACK], BF16, name="x_bf%d" % a, align_bytes=64)
-            raw = tiles["x_raw", t0]
-            m0 = (t0 % CHUNK) // PACK
-            m1 = m0 + raw.shape[2] // PACK
-            engines[engine](
-                out=tiles["x_bf", a][:, :, m0:m1, :].rearrange("p r m j -> p m j r"),
-                in_=raw.rearrange("p j (m r) -> p m j r", r=PACK),
+            if a not in x_dealt:
+                x_dealt[a] = keep.tile([P, PACK, P, PACK], BF16, name="x_dealt%d" % a, align_bytes=64)
+            m0 = (t0 - a * CHUNK) // PACK
+            m1 = (X_PIECES[t0] - a * CHUNK) // PACK
+            copy(
+                out=x_dealt[a][:, :, m0:m1, :].rearrange("p r m j -> p m j r"),
+                in_=x_raw[t0].rearrange("p j (m r) -> p m j r", r=PACK),
             )
 
         def x_quantize(a):
             codes = keep.tile([P, CHUNK], U32, name="x_codes%d" % a, align_bytes=64)
             scales = keep.tile([P, CHUNK], U8, name="x_scales%d" % a, align_bytes=64)
             nc.vector.quantize_mx(
-                out=codes[:].bitcast(FP8X4), scales=scales[:], in_=tiles["x_bf", a][:].rearrange("p r m j -> p (r m j)")
+                out=codes[:].bitcast(FP8X4), scales=scales[:], in_=x_dealt[a][:].rearrange("p r m j -> p (r m j)")
             )
-            tiles["x_mx", a] = (codes, scales)
+            x_mx[a] = (codes, scales)
 
-        def multiply(a, nt):
-            x_codes, x_scales = tiles["x_mx", a]
-            acc = bank("sum")
-            tiles["acc", a, nt] = acc
-            if (a, nt // PACK) in TOKEN_MAJOR:
-                r = nt % PACK
-                half = nt // PACK * CHUNK
-                for m0, m1 in W_PIECES:
-                    if half <= m0 < half + CHUNK:
-                        w_codes, w_scales = tiles["w_mx", m0]
-                        for part in range(2):
-                            nc.tensor.matmul_mx(
-                                out=acc[:, m0 - half : m1 - half],
-                                lhsT=x_codes[:, r * P : (r + 1) * P].bitcast(FP8X4),
-                                lhsT_scale=x_scales[:, r * P : (r + 1) * P],
-                                rhs=w_codes[:, part, :].bitcast(FP8X4),
-                                rhs_scale=w_scales[:, part, :],
-                                start=(part == 0),
-                                stop=(part == 1),
-                            )
-            else:
-                w_codes, w_scales, c0 = tiles["w_tile", nt]
+
+        def result_columns(a, n0, n1):
+            half = n0 // HALF
+            if (a, half) not in results:
+                results[a, half] = keep.tile([P, PACK, HALF], F32, name="result%d_%d" % (a, half))
+            return results[a, half][:, :, n0 - half * HALF : n1 - half * HALF]
+
+        def channel_major_sum(a, nt):
+            x_codes, x_scales = x_mx[a]
+            w_codes, w_scales = w_mx[nt]
+            sums[a, nt] = next_bank("sum")
+            for part in range(2):
+                nc.tensor.matmul_mx(
+                    out=sums[a, nt][:].rearrange("p r m -> p (r m)"),
+                    lhsT=w_codes[:, part, :].bitcast(FP8X4),
+                    lhsT_scale=w_scales[:, part, :],
+                    rhs=x_codes[:].bitcast(FP8X4),
+                    rhs_scale=x_scales[:],
+                    start=(part == 0),
+                    stop=(part == 1),
+                )
+
+        def channel_major_silu(a, nt):
+            mids[a, nt] = keep.tile([P, PACK, P], F32, name="mid", bufs=MID_BUFS)
+            nc.scalar.activation(out=mids[a, nt][:], in_=sums[a, nt][:], func=SILU, bias=bias_cols[:, nt : nt + 1])
+
+        def turn(a, nt):
+            turned[a, nt] = next_bank("turn")
+            for r in range(PACK):
+                nc.tensor.transpose(turned[a, nt][:, r, :], mids[a, nt][:, r, :], ident[:])
+
+        def copy_out(a, nt, copy):
+            copy(out=result_columns(a, nt * P, (nt + 1) * P), in_=turned[a, nt][:])
+
+        def channel_major_in(a, tiles):
+            for nt in tiles:
+                channel_major_sum(a, nt)
+                channel_major_silu(a, nt)
+
+        def channel_major_out(a, tiles):
+            for nt in tiles:
+                turn(a, nt)
+                copy_out(a, nt, on_scalar)
+
+        def token_major_sum(a, nt):
+            x_codes, x_scales = x_mx[a]
+            w_codes, w_scales = w_mx[nt]
+            sums[a, nt] = next_bank("sum")
+            for r in range(PACK):
                 for part in range(2):
                     nc.tensor.matmul_mx(
-                        out=acc[:],
-                        lhsT=w_codes[:, part, c0 : c0 + P].bitcast(FP8X4),
-                        lhsT_scale=w_scales[:, part, c0 : c0 + P],
-                        rhs=x_codes[:].bitcast(FP8X4),
-                        rhs_scale=x_scales[:],
+                        out=sums[a, nt][:, r, :],
+                        lhsT=x_codes[:, r * P : (r + 1) * P].bitcast(FP8X4),
+                        lhsT_scale=x_scales[:, r * P : (r + 1) * P],
+                        rhs=w_codes[:, part, :].bitcast(FP8X4),
+                        rhs_scale=w_scales[:, part, :],
                         start=(part == 0),
                         stop=(part == 1),
                     )
 
-        def result_tile(a, h):
-            if ("res", a, h) not in tiles:
-                tiles["res", a, h] = keep.tile([P, PACK, CHUNK], F32, name="res%d_%d" % (a, h))
-            return tiles["res", a, h]
-
-        def add_bias(a, nt):
-            mid = keep.tile([P, CHUNK], F32, name="mid", bufs=MID_BUFS)
-            nc.vector.tensor_tensor(out=mid[:], in0=tiles["acc", a, nt][:], in1=bias_rows[:], op=ALU.add)
-            tiles["mid", a, nt] = mid
-
-        def silu(a, nt):
-            if (a, nt // PACK) in TOKEN_MAJOR:
-                nc.scalar.activation(out=result_tile(a, nt // PACK)[:, nt % PACK, :], in_=tiles["mid", a, nt][:], func=SILU)
-            else:
-                mid = keep.tile([P, CHUNK], F32, name="mid", bufs=MID_BUFS)
-                nc.scalar.activation(out=mid[:], in_=tiles["acc", a, nt][:], func=SILU, bias=bias_cols[:, nt : nt + 1])
-                tiles["mid", a, nt] = mid
-
-        def turn(a, nt):
-            turned = bank("turn")
-            h, r = divmod(nt, PACK)
-            for j in range(PACK):
-                nc.tensor.transpose(turned[:, j * P : (j + 1) * P], tiles["mid", a, h * PACK + j][:, r * P : (r + 1) * P], ident[:])
-            tiles["turned", a, nt] = turned
-
-        def copy_out(a, nt, engine):
-            engines[engine](out=result_tile(a, nt // PACK)[:, nt % PACK, :], in_=tiles["turned", a, nt][:])
-
-        def out_cast(a, n0, n1, engine):
-            h = n0 // CHUNK
-            rounded = keep.tile([P, n1 - n0, PACK], BF16, name="rounded%d_%d" % (a, n0), align_bytes=64)
-            engines[engine](
-                out=rounded[:].rearrange("p (c i) r -> p c r i", i=4),
-                in_=tiles["res", a, h][:, :, n0 - h * CHUNK : n1 - h * CHUNK].rearrange("p r (c i) -> p c r i", i=4),
+        def token_major_out(a, nt):
+            mids[a, nt] = keep.tile([P, PACK, P], F32, name="mid", bufs=MID_BUFS)
+            bias = bias_rows[:, nt - HIGH_TILES.start, :].unsqueeze(1).to_broadcast([P, PACK, P])
+            nc.vector.tensor_tensor(out=mids[a, nt][:], in0=sums[a, nt][:], in1=bias, op=ALU.add)
+            nc.scalar.activation(
+                out=result_columns(a, nt * P, (nt + 1) * P), in_=mids[a, nt][:], func=SILU, bias=zero[:, 1:2]
             )
-            tiles["rounded", a, n0] = rounded
 
-        def out_quantize(a, n0, n1):
+
+        def out_cast(a, n0, copy):
+            rounded[a, n0] = keep.tile([P, QUARTER, PACK], BF16, name="rounded%d_%d" % (a, n0), align_bytes=64)
+            copy(
+                out=rounded[a, n0][:].rearrange("p (c i) r -> p c r i", i=RUN),
+                in_=result_columns(a, n0, n0 + QUARTER).rearrange("p r (c i) -> p c r i", i=RUN),
+            )
+
+        def out_quantize(a, n0):
             nc.vector.quantize_mx(
-                out=out_codes[:, a, n0:n1].bitcast(FP8X4),
-                scales=out_scales[:, a, n0:n1],
-                in_=tiles["rounded", a, n0][:].rearrange("p n r -> p (n r)"),
+                out=out_codes[:, a, n0 : n0 + QUARTER].bitcast(FP8X4),
+                scales=out_scales[:, a, n0 : n0 + QUARTER],
+                in_=rounded[a, n0][:].rearrange("p n r -> p (n r)"),
             )
 
-        def store_result(a, h, r0, r1):
-            rows = out_0[a * CHUNK : (a + 1) * CHUNK, h * CHUNK : (h + 1) * CHUNK].rearrange("(p r) n -> p r n", r=PACK)
-            nc.sync.dma_start(out=rows[:, r0:r1, :], in_=tiles["res", a, h][:, r0:r1, :])
+        def store_result(a, n0, n1):
+            rows = out_0[a * CHUNK : (a + 1) * CHUNK, n0:n1].rearrange("(p r) n -> p r n", r=PACK)
+            nc.sync.dma_start(out=rows, in_=result_columns(a, n0, n1))
 
-        def store_codes(a, n0, n1):
+        def store_codes(a, n0):
             words = out_1[a].rearrange("p n i -> p (n i)").bitcast(I32)
-            nc.sync.dma_start(out=words[:, n0:n1], in_=out_codes[:, a, n0:n1].bitcast(I32))
+            nc.sync.dma_start(out=words[:, n0 : n0 + HALF], in_=out_codes[:, a, n0 : n0 + HALF].bitcast(I32))
 
-        def store_scales(a0, a1, n0, n1, queues):
+        def store_scales(n0, queue):
             for q in range(4):
-                rows = out_2[a0:a1, 4 * q : 4 * q + 4, n0:n1].rearrange("a r n -> r a n").bitcast(I32)
-                queues[q].dma_start(out=rows, in_=out_scales[32 * q : 32 * q + 4, a0:a1, n0:n1].bitcast(I32))
+                rows = out_2[:, 4 * q : 4 * q + 4, n0 : n0 + HALF].rearrange("a r n -> r a n").bitcast(I32)
+                queue.dma_start(out=rows, in_=out_scales[32 * q : 32 * q + 4, :, n0 : n0 + HALF].bitcast(I32))
 
-        out_codes = keep.tile([P, T // CHUNK, M], U32, name="out_codes", align_bytes=64)
-        out_scales = keep.tile([P, T // CHUNK, M], U8, name="out_scales", align_bytes=64)
+        def planes_of_half(a, n0):
+            for n in (n0, n0 + QUARTER):
+                out_cast(a, n, on_vector)
+            for n in (n0, n0 + QUARTER):
+                out_quantize(a, n)
+
+        out_codes = keep.tile([P, CHUNKS, M], U32, name="out_codes", align_bytes=64)
+        out_scales = keep.tile([P, CHUNKS, M], U8, name="out_scales", align_bytes=64)
         ident = keep.tile([P, P], F32, name="ident")
-        b_raw = keep.tile([P, P], F32, name="b_raw")
+        b_rows = keep.tile([P, P], F32, name="b_rows")
         bias_cols = keep.tile([P, M // P], F32, name="bias_cols")
-        bias_rows = keep.tile([P, CHUNK], F32, name="bias_rows")
-        warm = keep.tile([P, 8], F32, name="warm")
+        bias_rows = keep.tile([P, PACK, P], F32, name="bias_rows")
+        zero = keep.tile([P, 2], F32, name="zero")
 
-        def constants():
-            nc.gpsimd.memset(b_raw[:], 0.0)
-            nc.scalar.dma_start(out=b_raw[0 : M // P, :], in_=b.rearrange("(c n) -> c n", n=P))
-            nc.gpsimd.memset(warm[:, 0:1], 0.0)
-            nc.scalar.activation(out=warm[:, 1:2], in_=warm[:, 0:1], func=SILU)
-            make_identity(nc, ident[:])
 
-        def bias_to_columns():
-            turned = bank("turn")
-            nc.tensor.transpose(turned[:, 0:P], b_raw[:], ident[:])
-            nc.scalar.copy(out=bias_cols[:], in_=turned[:, 0 : M // P])
+        nc.gpsimd.memset(zero[:, 0:1], 0.0)
+        nc.scalar.activation(out=zero[:, 1:2], in_=zero[:, 0:1], func=SILU)
+        make_identity(nc, ident[:])
+        nc.vector.memset(b_rows[:], 0.0)
 
-        def bias_to_rows():
-            turned = bank("turn")
-            for j in range(PACK):
-                nc.tensor.transpose(turned[:, j * P : (j + 1) * P], bias_cols[:, PACK + j : PACK + j + 1].to_broadcast([P, P]), ident[:])
-            nc.scalar.copy(out=bias_rows[:], in_=turned[:])
+        load("w", w_rows, W_PIECES, w_raw, 0, 256)
+        nc.sync.dma_start(out=b_rows[0 : M // P, :], in_=b.rearrange("(c n) -> c n", n=P))
+        load("x", x_rows, X_PIECES, x_raw, 0, 512)
+        load("w", w_rows, W_PIECES, w_raw, 256, 512)
+        load("x", x_rows, X_PIECES, x_raw, 512, 1024)
+        load("w", w_rows, W_PIECES, w_raw, 512, 1024)
+        load("x", x_rows, X_PIECES, x_raw, 1024, 1536)
 
-        constants()
-        load_w(0, 256)
-        w_top(128, "S")
-        w_top(0, "V")
-        load_x(0, 512)
-        load_w(256, 512)
+        bank = next_bank("turn")
+        nc.tensor.transpose(bank[:, 0, :], b_rows[:], ident[:])
+        nc.scalar.copy(out=bias_cols[:], in_=bank[:, 0, 0 : M // P])
+        bank = next_bank("turn")
+        for i, nt in enumerate(HIGH_TILES):
+            nc.tensor.transpose(bank[:, i, :], bias_cols[:, nt : nt + 1].to_broadcast([P, P]), ident[:])
+        nc.scalar.copy(out=bias_rows[:], in_=bank[:])
+
+        w_top(0, on_vector)
         w_mask(0)
         w_low(0)
-        w_mask(128)
+        x_cast(0, on_vector)
+        x_cast(256, on_scalar)
         w_quantize(0)
-        w_low(128)
-        bias_to_columns()
-        x_cast(256, "V")
-        w_quantize(128)
-        bias_to_rows()
-        x_cast(0, "S")
-        w_top(256, "S")
-        load_x(512, 1024)
         x_quantize(0)
-        w_top(384, "V")
+        w_top(256, on_scalar)
+        w_top(384, on_scalar)
         w_mask(256)
-        multiply(0, 1)
-        w_mask(384)
-        load_w(512, 1024)
         w_low(256)
-        w_low(384)
-        multiply(0, 0)
-        silu(0, 1)
-        w_quantize(384)
-        x_cast(512, "S")
+        w_mask(384)
         w_quantize(256)
-        x_cast(768, "V")
-        multiply(0, 2)
-        multiply(0, 3)
-        silu(0, 0)
-        load_x(1024, 1536)
-        silu(0, 2)
+        w_low(384)
+        x_cast(512, on_vector)
+        w_quantize(384)
         x_quantize(1)
-        multiply(1, 1)
-        multiply(1, 3)
-        w_top(768, "V")
-        multiply(1, 0)
-        silu(0, 3)
-        w_top(512, "V")
-        turn(0, 3)
-        w_mask(768)
-        silu(1, 1)
+
+        channel_major_in(0, LOW_TILES[:3])
+        channel_major_out(0, LOW_TILES[:3])
+        store_result(0, 0, QUARTER)
+        w_top(512, on_vector)
+        w_top(768, on_vector)
         w_mask(512)
-        w_low(768)
-        silu(1, 3)
-        x_cast(1024, "V")
-        turn(0, 0)
-        turn(0, 1)
-        silu(1, 0)
-        copy_out(0, 3, "S")
-        multiply(1, 2)
-        copy_out(0, 0, "S")
-        w_quantize(768)
-        turn(0, 2)
-        silu(1, 2)
+        out_cast(0, 0, on_vector)
+        x_cast(1024, on_vector)
+        w_mask(768)
         x_quantize(2)
-        copy_out(0, 1, "S")
-        copy_out(0, 2, "S")
-        turn(1, 3)
-        turn(1, 2)
-        turn(1, 1)
-        turn(1, 0)
-        store_result(0, 0, 0, 2)
-        multiply(2, 3)
         w_low(512)
-        copy_out(1, 0, "V")
-        store_result(0, 0, 2, 4)
-        multiply(2, 0)
-        copy_out(1, 3, "S")
-        multiply(2, 1)
-        copy_out(1, 2, "S")
-        copy_out(1, 1, "S")
-        multiply(2, 2)
-        silu(2, 3)
-        silu(2, 0)
+        channel_major_in(0, LOW_TILES[3:])
+        channel_major_in(1, LOW_TILES)
+        channel_major_out(0, LOW_TILES[3:])
+        store_result(0, QUARTER, HALF)
+        channel_major_out(1, LOW_TILES[:3])
+        turn(1, LOW_TILES[3])
+        copy_out(1, LOW_TILES[3], on_vector)
+        store_result(1, 0, HALF)
+
+        channel_major_in(2, LOW_TILES)
         w_quantize(512)
-        silu(2, 1)
-        silu(2, 2)
-        multiply(0, 5)
-        out_cast(0, 0, 256, "V")
-        multiply(0, 4)
-        out_cast(0, 256, 512, "V")
-        out_quantize(0, 0, 256)
-        add_bias(0, 5)
-        turn(2, 1)
-        store_result(1, 0, 0, 2)
-        turn(2, 0)
-        turn(2, 3)
-        out_quantize(0, 256, 512)
-        copy_out(2, 1, "V")
-        add_bias(0, 4)
-        out_cast(1, 0, 256, "S")
-        out_cast(1, 256, 512, "V")
-        store_result(1, 0, 2, 4)
-        turn(2, 2)
-        multiply(0, 7)
-        multiply(0, 6)
-        copy_out(2, 0, "S")
-        multiply(1, 4)
-        multiply(1, 5)
-        add_bias(0, 7)
-        add_bias(0, 6)
-        out_quantize(1, 0, 256)
-        silu(0, 5)
-        multiply(1, 6)
-        multiply(1, 7)
-        add_bias(1, 4)
-        silu(0, 4)
-        add_bias(1, 5)
-        multiply(2, 5)
-        add_bias(1, 6)
-        copy_out(2, 3, "S")
-        copy_out(2, 2, "S")
-        add_bias(1, 7)
-        multiply(2, 7)
-        out_cast(2, 0, 256, "V")
-        out_quantize(1, 256, 512)
-        out_cast(2, 256, 512, "V")
-        out_quantize(2, 0, 256)
-        silu(0, 6)
-        silu(0, 7)
-        multiply(2, 6)
-        silu(1, 4)
-        store_codes(0, 0, 512)
-        silu(1, 5)
-        silu(2, 5)
-        silu(2, 7)
-        multiply(2, 4)
-        store_result(2, 0, 0, 2)
-        out_quantize(2, 256, 512)
-        out_cast(0, 512, 768, "V")
-        out_cast(0, 768, 1024, "V")
-        silu(2, 6)
-        silu(2, 4)
-        silu(1, 7)
-        turn(2, 6)
-        out_quantize(0, 512, 768)
-        out_quantize(0, 768, 1024)
-        turn(2, 4)
-        store_result(0, 1, 0, 2)
-        store_result(2, 0, 2, 4)
-        store_result(0, 1, 2, 4)
-        silu(1, 6)
-        turn(2, 7)
-        store_result(1, 1, 0, 2)
-        turn(2, 5)
-        store_codes(1, 0, 512)
-        out_cast(1, 768, 1024, "V")
-        copy_out(2, 5, "V")
-        store_scales(0, 3, 0, 512, [nc.sync] * 4)
-        copy_out(2, 6, "S")
-        out_quantize(1, 768, 1024)
-        store_codes(2, 0, 512)
-        copy_out(2, 7, "S")
-        copy_out(2, 4, "S")
-        store_result(1, 1, 2, 4)
-        out_cast(2, 512, 768, "V")
-        store_result(2, 1, 2, 4)
-        out_cast(1, 512, 768, "V")
-        out_cast(2, 768, 1024, "V")
-        out_quantize(1, 512, 768)
-        store_result(2, 1, 0, 2)
-        store_codes(0, 512, 1024)
-        store_codes(1, 512, 1024)
-        out_quantize(2, 512, 768)
-        out_quantize(2, 768, 1024)
-        store_codes(2, 512, 1024)
-        store_scales(0, 3, 512, 1024, [nc.scalar] * 4)
+        out_quantize(0, 0)
+        out_cast(0, QUARTER, on_vector)
+        w_low(768)
+        out_quantize(0, QUARTER)
+        w_quantize(768)
+        store_codes(0, 0)
+        token_major_sum(0, HIGH_TILES[0])
+        channel_major_out(2, LOW_TILES)
+        store_result(2, 0, HALF)
+
+        token_major_out(0, HIGH_TILES[0])
+        for nt in HIGH_TILES[1:]:
+            token_major_sum(0, nt)
+            token_major_out(0, nt)
+        store_result(0, HALF, M)
+        for nt in HIGH_TILES:
+            token_major_sum(1, nt)
+            token_major_out(1, nt)
+        store_result(1, HALF, M)
+
+        channel_major_in(2, HIGH_TILES)
+        channel_major_out(2, HIGH_TILES)
+        for a in (1, 2):
+            planes_of_half(a, 0)
+            store_codes(a, 0)
+        store_scales(0, nc.sync)
+        store_result(2, HALF, HALF + QUARTER)
+        store_result(2, HALF + QUARTER, M)
+        for a in (0, 1):
+            planes_of_half(a, HALF)
+            store_codes(a, HALF)
+        out_cast(2, HALF, on_scalar)
+        out_cast(2, HALF + QUARTER, on_vector)
+        out_quantize(2, HALF)
+        out_quantize(2, HALF + QUARTER)
+        store_codes(2, HALF)
+        store_scales(HALF, nc.scalar)

@@ -21,15 +21,11 @@ CHUNK = P * PACK
 CHUNKS = T // CHUNK
 HALF = M // 2
 QUARTER = M // 4
-LOW_TILES = range(0, 4)
-HIGH_TILES = range(4, 8)
+TILES = M // P
 RUN = 4
-BANKS = 4
+BANKS = 8
 MID_BUFS = 12
 HI_MASK_PAIR = 0xFFF0FFF0 - (1 << 32)
-
-W_PIECES = {0: 256, 256: 384, 384: 512, 512: 768, 768: 1024}
-X_PIECES = {0: 256, 256: 512, 512: 1024, 1024: 1536}
 
 
 def tile_mix_hilo_tm_pl_silu_kernel(tc, w, x, b, out_0, out_1, out_2):
@@ -44,63 +40,65 @@ def tile_mix_hilo_tm_pl_silu_kernel(tc, w, x, b, out_0, out_1, out_2):
 
         w_rows = w.rearrange("(p j) n -> p j n", j=PACK)
         x_rows = x.rearrange("(p j) t -> p j t", j=PACK)
-        w_raw, w_parts, w_mx = {}, {}, {}
+        w_raw, w_parts, w_codes, w_scales = {}, {}, {}, {}
         x_raw, x_dealt, x_mx = {}, {}, {}
         sums, mids, turned, results, rounded = {}, {}, {}, {}, {}
-        banks_taken = {"sum": 0, "turn": 0}
+        banks_taken = []
 
-        def next_bank(kind):
-            index = banks_taken[kind] % BANKS
-            banks_taken[kind] = banks_taken[kind] + 1
-            return psum.tile([P, PACK, P], F32, name="%s%d" % (kind, index))
+        def next_bank():
+            index = len(banks_taken) % BANKS
+            banks_taken.append(index)
+            return psum.tile([P, PACK, P], F32, name="bank%d" % index)
 
-
-        def load(name, rows, pieces, views, c0, c1):
+        def load(name, rows, loaded, c0, c1):
             raw = keep.tile([P, PACK, c1 - c0], F32, name="%s_raw%d" % (name, c0))
             nc.sync.dma_start(out=raw[:], in_=rows[:, :, c0:c1])
-            for start in pieces:
-                if c0 <= start < c1:
-                    views[start] = raw[:, :, start - c0 : pieces[start] - c0]
+            loaded[c0, c1] = raw
 
-        def w_top(n0, copy):
-            parts = keep.tile([P, 2, W_PIECES[n0] - n0, PACK], BF16, name="w_parts%d" % n0, align_bytes=64)
-            halves = w_raw[n0].bitcast(BF16).rearrange("p j (c i e) -> p c j i e", i=RUN, e=2)
-            copy(out=parts[:, 0].rearrange("p (c i) j -> p c j i", i=RUN), in_=halves[:, :, :, :, 1])
-            w_parts[n0] = parts
+        def columns(loaded, c0, c1):
+            for (l0, l1), raw in loaded.items():
+                if l0 <= c0 and c1 <= l1:
+                    return raw[:, :, c0 - l0 : c1 - l0]
+
+        def w_top(n0, n1, copy):
+            for part in range(2):
+                w_parts[part, n0] = keep.tile([P, n1 - n0, PACK], BF16, name="w_part%d_%d" % (part, n0), align_bytes=64)
+            halves = columns(w_raw, n0, n1).bitcast(BF16).rearrange("p j (c i e) -> p c j i e", i=RUN, e=2)
+            copy(out=w_parts[0, n0][:].rearrange("p (c i) j -> p c j i", i=RUN), in_=halves[:, :, :, :, 1])
 
         def w_mask(n0):
-            pairs = w_parts[n0][:, 0].rearrange("p n j -> p (n j)").bitcast(I32)
+            pairs = w_parts[0, n0][:].rearrange("p n j -> p (n j)").bitcast(I32)
             nc.vector.tensor_scalar(out=pairs, in0=pairs, scalar1=HI_MASK_PAIR, scalar2=None, op0=ALU.bitwise_and)
 
-        def w_low(n0):
+        def w_low(n0, n1):
             nc.vector.tensor_tensor(
-                out=w_parts[n0][:, 1].rearrange("p (c i) j -> p c j i", i=RUN),
-                in0=w_raw[n0].rearrange("p j (c i) -> p c j i", i=RUN),
-                in1=w_parts[n0][:, 0].rearrange("p (c i) j -> p c j i", i=RUN),
+                out=w_parts[1, n0][:].rearrange("p (c i) j -> p c j i", i=RUN),
+                in0=columns(w_raw, n0, n1).rearrange("p j (c i) -> p c j i", i=RUN),
+                in1=w_parts[0, n0][:].rearrange("p (c i) j -> p c j i", i=RUN),
                 op=ALU.subtract,
             )
 
-        def w_quantize(n0):
-            width = W_PIECES[n0] - n0
-            codes = keep.tile([P, 2, width], U32, name="w_codes%d" % n0, align_bytes=64)
-            scales = keep.tile([P, 2, width], U8, name="w_scales%d" % n0, align_bytes=64)
+        def w_quantize(part, n0, n1):
+            half = n0 // HALF
+            if (part, half) not in w_codes:
+                w_codes[part, half] = keep.tile([P, HALF], U32, name="w_codes%d_%d" % (part, half), align_bytes=64)
+                w_scales[part, half] = keep.tile([P, HALF], U8, name="w_scales%d_%d" % (part, half), align_bytes=64)
+            cols = slice(n0 - half * HALF, n1 - half * HALF)
             nc.vector.quantize_mx(
-                out=codes[:].rearrange("p h n -> p (h n)").bitcast(FP8X4),
-                scales=scales[:].rearrange("p h n -> p (h n)"),
-                in_=w_parts[n0][:].rearrange("p h n j -> p (h n j)"),
+                out=w_codes[part, half][:, cols].bitcast(FP8X4),
+                scales=w_scales[part, half][:, cols],
+                in_=w_parts[part, n0][:].rearrange("p n j -> p (n j)"),
             )
-            for c0 in range(0, width, P):
-                w_mx[(n0 + c0) // P] = (codes[:, :, c0 : c0 + P], scales[:, :, c0 : c0 + P])
 
-        def x_cast(t0, copy):
+        def x_cast(t0, t1, copy):
             a = t0 // CHUNK
             if a not in x_dealt:
                 x_dealt[a] = keep.tile([P, PACK, P, PACK], BF16, name="x_dealt%d" % a, align_bytes=64)
             m0 = (t0 - a * CHUNK) // PACK
-            m1 = (X_PIECES[t0] - a * CHUNK) // PACK
+            m1 = (t1 - a * CHUNK) // PACK
             copy(
                 out=x_dealt[a][:, :, m0:m1, :].rearrange("p r m j -> p m j r"),
-                in_=x_raw[t0].rearrange("p j (m r) -> p m j r", r=PACK),
+                in_=columns(x_raw, t0, t1).rearrange("p j (m r) -> p m j r", r=PACK),
             )
 
         def x_quantize(a):
@@ -111,212 +109,240 @@ def tile_mix_hilo_tm_pl_silu_kernel(tc, w, x, b, out_0, out_1, out_2):
             )
             x_mx[a] = (codes, scales)
 
+        def result_of(a):
+            if a not in results:
+                results[a] = keep.tile([P, PACK, M], F32, name="result%d" % a)
+            return results[a]
 
-        def result_columns(a, n0, n1):
-            half = n0 // HALF
-            if (a, half) not in results:
-                results[a, half] = keep.tile([P, PACK, HALF], F32, name="result%d_%d" % (a, half))
-            return results[a, half][:, :, n0 - half * HALF : n1 - half * HALF]
-
-        def channel_major_sum(a, nt):
+        def cm_sum(a, nt):
             x_codes, x_scales = x_mx[a]
-            w_codes, w_scales = w_mx[nt]
-            sums[a, nt] = next_bank("sum")
+            half = nt * P // HALF
+            cols = slice(nt * P - half * HALF, (nt + 1) * P - half * HALF)
+            sums[a, nt] = next_bank()
             for part in range(2):
                 nc.tensor.matmul_mx(
                     out=sums[a, nt][:].rearrange("p r m -> p (r m)"),
-                    lhsT=w_codes[:, part, :].bitcast(FP8X4),
-                    lhsT_scale=w_scales[:, part, :],
+                    lhsT=w_codes[part, half][:, cols].bitcast(FP8X4),
+                    lhsT_scale=w_scales[part, half][:, cols],
                     rhs=x_codes[:].bitcast(FP8X4),
                     rhs_scale=x_scales[:],
                     start=(part == 0),
                     stop=(part == 1),
                 )
 
-        def channel_major_silu(a, nt):
+        def cm_silu(a, nt):
             mids[a, nt] = keep.tile([P, PACK, P], F32, name="mid", bufs=MID_BUFS)
             nc.scalar.activation(out=mids[a, nt][:], in_=sums[a, nt][:], func=SILU, bias=bias_cols[:, nt : nt + 1])
 
         def turn(a, nt):
-            turned[a, nt] = next_bank("turn")
+            turned[a, nt] = next_bank()
             for r in range(PACK):
                 nc.tensor.transpose(turned[a, nt][:, r, :], mids[a, nt][:, r, :], ident[:])
 
         def copy_out(a, nt, copy):
-            copy(out=result_columns(a, nt * P, (nt + 1) * P), in_=turned[a, nt][:])
+            copy(out=result_of(a)[:, :, nt * P : (nt + 1) * P], in_=turned[a, nt][:])
 
-        def channel_major_in(a, tiles):
+        def cm_in(a, tiles):
             for nt in tiles:
-                channel_major_sum(a, nt)
-                channel_major_silu(a, nt)
+                cm_sum(a, nt)
+                cm_silu(a, nt)
 
-        def channel_major_out(a, tiles):
+        def cm_out(a, tiles, copy):
             for nt in tiles:
                 turn(a, nt)
-                copy_out(a, nt, on_scalar)
+                copy_out(a, nt, copy)
 
-        def token_major_sum(a, nt):
+        def tm_sum(a, r, half):
             x_codes, x_scales = x_mx[a]
-            w_codes, w_scales = w_mx[nt]
-            sums[a, nt] = next_bank("sum")
-            for r in range(PACK):
-                for part in range(2):
-                    nc.tensor.matmul_mx(
-                        out=sums[a, nt][:, r, :],
-                        lhsT=x_codes[:, r * P : (r + 1) * P].bitcast(FP8X4),
-                        lhsT_scale=x_scales[:, r * P : (r + 1) * P],
-                        rhs=w_codes[:, part, :].bitcast(FP8X4),
-                        rhs_scale=w_scales[:, part, :],
-                        start=(part == 0),
-                        stop=(part == 1),
-                    )
+            sums[a, r, half] = next_bank()
+            for part in range(2):
+                nc.tensor.matmul_mx(
+                    out=sums[a, r, half][:].rearrange("p i n -> p (i n)"),
+                    lhsT=x_codes[:, r * P : (r + 1) * P].bitcast(FP8X4),
+                    lhsT_scale=x_scales[:, r * P : (r + 1) * P],
+                    rhs=w_codes[part, half][:].bitcast(FP8X4),
+                    rhs_scale=w_scales[part, half][:],
+                    start=(part == 0),
+                    stop=(part == 1),
+                )
 
-        def token_major_out(a, nt):
-            mids[a, nt] = keep.tile([P, PACK, P], F32, name="mid", bufs=MID_BUFS)
-            bias = bias_rows[:, nt - HIGH_TILES.start, :].unsqueeze(1).to_broadcast([P, PACK, P])
-            nc.vector.tensor_tensor(out=mids[a, nt][:], in0=sums[a, nt][:], in1=bias, op=ALU.add)
+        def tm_add(a, r, half):
+            mids[a, r, half] = keep.tile([P, PACK, P], F32, name="mid", bufs=MID_BUFS)
+            nc.vector.tensor_tensor(out=mids[a, r, half][:], in0=sums[a, r, half][:], in1=bias_rows[half][:], op=ALU.add)
+
+        def tm_silu(a, r, half):
             nc.scalar.activation(
-                out=result_columns(a, nt * P, (nt + 1) * P), in_=mids[a, nt][:], func=SILU, bias=zero[:, 1:2]
+                out=result_of(a)[:, r, half * HALF : (half + 1) * HALF],
+                in_=mids[a, r, half][:].rearrange("p i n -> p (i n)"),
+                func=SILU,
+                bias=zero[:, 1:2],
             )
 
-
-        def out_cast(a, n0, copy):
-            rounded[a, n0] = keep.tile([P, QUARTER, PACK], BF16, name="rounded%d_%d" % (a, n0), align_bytes=64)
+        def out_cast(a, n0, n1, copy):
+            rounded[a, n0] = keep.tile([P, n1 - n0, PACK], BF16, name="rounded%d_%d" % (a, n0), align_bytes=64)
             copy(
                 out=rounded[a, n0][:].rearrange("p (c i) r -> p c r i", i=RUN),
-                in_=result_columns(a, n0, n0 + QUARTER).rearrange("p r (c i) -> p c r i", i=RUN),
+                in_=result_of(a)[:, :, n0:n1].rearrange("p r (c i) -> p c r i", i=RUN),
             )
 
-        def out_quantize(a, n0):
+        def out_cast_gpsimd(a, n0, n1, name):
+            rounded[a, n0] = keep.tile([P, n1 - n0, PACK], BF16, name=name, align_bytes=64)
+            nc.gpsimd.tensor_scalar(
+                out=rounded[a, n0][:],
+                in0=result_of(a)[:, :, n0:n1].rearrange("p r n -> p n r"),
+                scalar1=1.0,
+                scalar2=-0.0,
+                op0=ALU.mult,
+                op1=ALU.add,
+            )
+
+        def out_quantize(a, n0, n1):
             nc.vector.quantize_mx(
-                out=out_codes[:, a, n0 : n0 + QUARTER].bitcast(FP8X4),
-                scales=out_scales[:, a, n0 : n0 + QUARTER],
+                out=out_codes[:, a, n0:n1].bitcast(FP8X4),
+                scales=out_scales[:, a, n0:n1],
                 in_=rounded[a, n0][:].rearrange("p n r -> p (n r)"),
             )
 
-        def store_result(a, n0, n1):
+        def store_result(a, n0, n1, r0=0, r1=PACK):
             rows = out_0[a * CHUNK : (a + 1) * CHUNK, n0:n1].rearrange("(p r) n -> p r n", r=PACK)
-            nc.sync.dma_start(out=rows, in_=result_columns(a, n0, n1))
+            nc.sync.dma_start(out=rows[:, r0:r1, :], in_=result_of(a)[:, r0:r1, n0:n1])
 
-        def store_codes(a, n0):
+        def store_codes(a, n0, n1):
             words = out_1[a].rearrange("p n i -> p (n i)").bitcast(I32)
-            nc.sync.dma_start(out=words[:, n0 : n0 + HALF], in_=out_codes[:, a, n0 : n0 + HALF].bitcast(I32))
+            nc.sync.dma_start(out=words[:, n0:n1], in_=out_codes[:, a, n0:n1].bitcast(I32))
 
-        def store_scales(n0, queue):
+        def store_scales(a0, a1, n0, n1, queues):
             for q in range(4):
-                rows = out_2[:, 4 * q : 4 * q + 4, n0 : n0 + HALF].rearrange("a r n -> r a n").bitcast(I32)
-                queue.dma_start(out=rows, in_=out_scales[32 * q : 32 * q + 4, :, n0 : n0 + HALF].bitcast(I32))
+                rows = out_2[a0:a1, 4 * q : 4 * q + 4, n0:n1].rearrange("a r n -> r a n").bitcast(I32)
+                queues[q].dma_start(out=rows, in_=out_scales[32 * q : 32 * q + 4, a0:a1, n0:n1].bitcast(I32))
 
-        def planes_of_half(a, n0):
-            for n in (n0, n0 + QUARTER):
-                out_cast(a, n, on_vector)
-            for n in (n0, n0 + QUARTER):
-                out_quantize(a, n)
+        def planes(a, n0, n1):
+            mid = (n0 + n1) // 2
+            out_cast(a, n0, mid, on_vector)
+            out_cast(a, mid, n1, on_vector)
+            out_quantize(a, n0, mid)
+            out_quantize(a, mid, n1)
 
         out_codes = keep.tile([P, CHUNKS, M], U32, name="out_codes", align_bytes=64)
         out_scales = keep.tile([P, CHUNKS, M], U8, name="out_scales", align_bytes=64)
         ident = keep.tile([P, P], F32, name="ident")
         b_rows = keep.tile([P, P], F32, name="b_rows")
-        bias_cols = keep.tile([P, M // P], F32, name="bias_cols")
-        bias_rows = keep.tile([P, PACK, P], F32, name="bias_rows")
+        bias_cols = keep.tile([P, TILES], F32, name="bias_cols")
+        bias_rows = [keep.tile([P, PACK, P], F32, name="bias_rows%d" % half) for half in range(2)]
         zero = keep.tile([P, 2], F32, name="zero")
 
+        def bias_columns():
+            bank = next_bank()
+            nc.tensor.transpose(bank[:, 0, :], b_rows[:], ident[:])
+            nc.scalar.copy(out=bias_cols[:], in_=bank[:, 0, 0:TILES])
+
+        def bias_spread(half):
+            bank = next_bank()
+            for i in range(PACK):
+                nt = half * PACK + i
+                nc.tensor.transpose(bank[:, i, :], bias_cols[:, nt : nt + 1].to_broadcast([P, P]), ident[:])
+            nc.scalar.copy(out=bias_rows[half][:], in_=bank[:])
 
         nc.gpsimd.memset(zero[:, 0:1], 0.0)
         nc.scalar.activation(out=zero[:, 1:2], in_=zero[:, 0:1], func=SILU)
         make_identity(nc, ident[:])
         nc.vector.memset(b_rows[:], 0.0)
 
-        load("w", w_rows, W_PIECES, w_raw, 0, 256)
-        nc.sync.dma_start(out=b_rows[0 : M // P, :], in_=b.rearrange("(c n) -> c n", n=P))
-        load("x", x_rows, X_PIECES, x_raw, 0, 512)
-        load("w", w_rows, W_PIECES, w_raw, 256, 512)
-        load("x", x_rows, X_PIECES, x_raw, 512, 1024)
-        load("w", w_rows, W_PIECES, w_raw, 512, 1024)
-        load("x", x_rows, X_PIECES, x_raw, 1024, 1536)
 
-        bank = next_bank("turn")
-        nc.tensor.transpose(bank[:, 0, :], b_rows[:], ident[:])
-        nc.scalar.copy(out=bias_cols[:], in_=bank[:, 0, 0 : M // P])
-        bank = next_bank("turn")
-        for i, nt in enumerate(HIGH_TILES):
-            nc.tensor.transpose(bank[:, i, :], bias_cols[:, nt : nt + 1].to_broadcast([P, P]), ident[:])
-        nc.scalar.copy(out=bias_rows[:], in_=bank[:])
+        load("w", w_rows, w_raw, 0, 256)
+        nc.sync.dma_start(out=b_rows[0:TILES, :], in_=b.rearrange("(c n) -> c n", n=P))
+        load("x", x_rows, x_raw, 0, 512)
+        load("w", w_rows, w_raw, 256, 512)
+        load("x", x_rows, x_raw, 512, 1024)
+        load("w", w_rows, w_raw, 512, 1024)
+        load("x", x_rows, x_raw, 1024, 1536)
 
-        w_top(0, on_vector)
+        bias_columns()
+        bias_spread(1)
+
+        w_top(0, 256, on_vector)
         w_mask(0)
-        w_low(0)
-        x_cast(0, on_vector)
-        x_cast(256, on_scalar)
-        w_quantize(0)
+        w_low(0, 256)
+        x_cast(0, 256, on_vector)
+        x_cast(256, 512, on_scalar)
+        w_quantize(0, 0, 256)
+        w_quantize(1, 0, 256)
         x_quantize(0)
-        w_top(256, on_scalar)
-        w_top(384, on_scalar)
+        w_top(256, 384, on_scalar)
+        w_top(384, 512, on_scalar)
+        bias_spread(0)
         w_mask(256)
-        w_low(256)
+        w_low(256, 384)
         w_mask(384)
-        w_quantize(256)
-        w_low(384)
-        x_cast(512, on_vector)
-        w_quantize(384)
+        w_quantize(0, 256, 384)
+        w_low(384, 512)
+        w_quantize(1, 256, 384)
+        w_quantize(0, 384, 512)
+        w_quantize(1, 384, 512)
+        x_cast(512, 1024, on_vector)
         x_quantize(1)
 
-        channel_major_in(0, LOW_TILES[:3])
-        channel_major_out(0, LOW_TILES[:3])
-        store_result(0, 0, QUARTER)
-        w_top(512, on_vector)
-        w_top(768, on_vector)
+        cm_in(0, (0, 1, 2))
+        cm_out(0, (0, 1), on_scalar)
+        store_result(0, 0, 256)
+        w_top(512, 768, on_vector)
+        w_top(768, 1024, on_vector)
         w_mask(512)
-        out_cast(0, 0, on_vector)
-        x_cast(1024, on_vector)
         w_mask(768)
-        x_quantize(2)
-        w_low(512)
-        channel_major_in(0, LOW_TILES[3:])
-        channel_major_in(1, LOW_TILES)
-        channel_major_out(0, LOW_TILES[3:])
-        store_result(0, QUARTER, HALF)
-        channel_major_out(1, LOW_TILES[:3])
-        turn(1, LOW_TILES[3])
-        copy_out(1, LOW_TILES[3], on_vector)
-        store_result(1, 0, HALF)
+        w_low(512, 768)
+        w_low(768, 1024)
+        for part in range(2):
+            w_quantize(part, 512, 768)
+            w_quantize(part, 768, 1024)
+        x_cast(1024, 1536, on_vector)
+        cm_in(0, (3,))
+        cm_out(0, (2,), on_scalar)
+        cm_in(1, (0, 1))
+        cm_out(0, (3,), on_scalar)
+        store_result(0, 256, 512)
+        cm_in(1, (2, 3))
+        cm_out(1, (0, 1), on_scalar)
+        store_result(1, 0, 256)
+        cm_out(1, (2, 3), on_scalar)
+        store_result(1, 256, 512)
 
-        channel_major_in(2, LOW_TILES)
-        w_quantize(512)
-        out_quantize(0, 0)
-        out_cast(0, QUARTER, on_vector)
-        w_low(768)
-        out_quantize(0, QUARTER)
-        w_quantize(768)
-        store_codes(0, 0)
-        token_major_sum(0, HIGH_TILES[0])
-        channel_major_out(2, LOW_TILES)
-        store_result(2, 0, HALF)
-
-        token_major_out(0, HIGH_TILES[0])
-        for nt in HIGH_TILES[1:]:
-            token_major_sum(0, nt)
-            token_major_out(0, nt)
-        store_result(0, HALF, M)
-        for nt in HIGH_TILES:
-            token_major_sum(1, nt)
-            token_major_out(1, nt)
-        store_result(1, HALF, M)
-
-        channel_major_in(2, HIGH_TILES)
-        channel_major_out(2, HIGH_TILES)
-        for a in (1, 2):
-            planes_of_half(a, 0)
-            store_codes(a, 0)
-        store_scales(0, nc.sync)
-        store_result(2, HALF, HALF + QUARTER)
-        store_result(2, HALF + QUARTER, M)
+        out_cast(0, 0, 256, on_scalar)
         for a in (0, 1):
-            planes_of_half(a, HALF)
-            store_codes(a, HALF)
-        out_cast(2, HALF, on_scalar)
-        out_cast(2, HALF + QUARTER, on_vector)
-        out_quantize(2, HALF)
-        out_quantize(2, HALF + QUARTER)
-        store_codes(2, HALF)
-        store_scales(HALF, nc.scalar)
+            for r in range(PACK):
+                tm_sum(a, r, 1)
+                tm_add(a, r, 1)
+                tm_silu(a, r, 1)
+                if a == 0 and r == 0:
+                    x_quantize(2)
+                    out_cast_gpsimd(1, 0, 512, "x_dealt2")
+                    out_cast_gpsimd(0, 256, 512, "rounded0_256")
+                if r % 2:
+                    store_result(a, HALF, M, r - 1, r + 1)
+        out_cast_gpsimd(0, 512, 768, "rounded0_512")
+        out_cast_gpsimd(0, 768, 1024, "rounded0_768")
+        for r in range(PACK):
+            for half in range(2):
+                tm_sum(2, r, half)
+                tm_add(2, r, half)
+                tm_silu(2, r, half)
+            store_result(2, 0, M, r, r + 1)
+        for n0 in (0, 256, 512):
+            out_cast(2, n0, n0 + QUARTER, on_scalar)
+        for n0 in range(0, M, QUARTER):
+            out_quantize(0, n0, n0 + QUARTER)
+        store_codes(0, 0, M)
+        out_cast(1, 512, 768, on_vector)
+        out_cast(1, 768, 1024, on_vector)
+        out_quantize(1, 0, 512)
+        out_quantize(1, 512, 768)
+        out_quantize(1, 768, 1024)
+        store_scales(0, 2, 0, M, [nc.sync] * 4)
+        store_codes(1, 0, M)
+        out_cast(2, 768, 1024, on_vector)
+        out_quantize(2, 0, 256)
+        out_quantize(2, 256, 512)
+        store_codes(2, 0, 512)
+        out_quantize(2, 768, 1024)
+        out_quantize(2, 512, 768)
+        store_codes(2, 512, 1024)
+        store_scales(2, 3, 0, M, [nc.scalar, nc.scalar, nc.sync, nc.sync])

@@ -90,24 +90,26 @@ def tile_mix_hilo_tm_pl_silu_kernel(tc, w, x, b, out_0, out_1, out_2):
                 in_=w_parts[part, n0][:].rearrange("p n j -> p (n j)"),
             )
 
-        def x_cast(t0, t1, copy):
-            a = t0 // CHUNK
-            if a not in x_dealt:
-                x_dealt[a] = keep.tile([P, PACK, P, PACK], BF16, name="x_dealt%d" % a, align_bytes=64)
-            m0 = (t0 - a * CHUNK) // PACK
-            m1 = (t1 - a * CHUNK) // PACK
+        def x_cast_slots(a, h, copy, name=None):
+            x_dealt[a, h] = keep.tile([P, 2, P, PACK], BF16, name=name or "x_dealt%d_%d" % (a, h), align_bytes=64)
             copy(
-                out=x_dealt[a][:, :, m0:m1, :].rearrange("p r m j -> p m j r"),
-                in_=columns(x_raw, t0, t1).rearrange("p j (m r) -> p m j r", r=PACK),
+                out=x_dealt[a, h][:].rearrange("p r m j -> p m j r"),
+                in_=columns(x_raw, a * CHUNK, (a + 1) * CHUNK).rearrange("p j (m r) -> p m j r", r=PACK)[
+                    :, :, :, 2 * h : 2 * h + 2
+                ],
             )
 
-        def x_quantize(a):
-            codes = keep.tile([P, CHUNK], U32, name="x_codes%d" % a, align_bytes=64)
-            scales = keep.tile([P, CHUNK], U8, name="x_scales%d" % a, align_bytes=64)
+        def x_quantize(a, h):
+            if a not in x_mx:
+                codes = keep.tile([P, CHUNK], U32, name="x_codes%d" % a, align_bytes=64)
+                scales = keep.tile([P, CHUNK], U8, name="x_scales%d" % a, align_bytes=64)
+                x_mx[a] = (codes, scales)
+            codes, scales = x_mx[a]
             nc.vector.quantize_mx(
-                out=codes[:].bitcast(FP8X4), scales=scales[:], in_=x_dealt[a][:].rearrange("p r m j -> p (r m j)")
+                out=codes[:, 2 * h * P : (2 * h + 2) * P].bitcast(FP8X4),
+                scales=scales[:, 2 * h * P : (2 * h + 2) * P],
+                in_=x_dealt[a, h][:].rearrange("p r m j -> p (r m j)"),
             )
-            x_mx[a] = (codes, scales)
 
         def result_of(a):
             if a not in results:
@@ -129,6 +131,54 @@ def tile_mix_hilo_tm_pl_silu_kernel(tc, w, x, b, out_0, out_1, out_2):
                     start=(part == 0),
                     stop=(part == 1),
                 )
+
+        def cm_sum_slots(a, nt, h):
+            x_codes, x_scales = x_mx[a]
+            cols = slice(nt * P, (nt + 1) * P)
+            tokens = slice(2 * h * P, (2 * h + 2) * P)
+            if h == 0:
+                sums[a, nt] = next_bank()
+            for part in range(2):
+                nc.tensor.matmul_mx(
+                    out=sums[a, nt][:].rearrange("p r m -> p (r m)")[:, tokens],
+                    lhsT=w_codes[part, 0][:, cols].bitcast(FP8X4),
+                    lhsT_scale=w_scales[part, 0][:, cols],
+                    rhs=x_codes[:, tokens].bitcast(FP8X4),
+                    rhs_scale=x_scales[:, tokens],
+                    start=(part == 0 and h == 0),
+                    stop=(part == 1 and h == 1),
+                )
+
+        def pair_sum(a, h, n0):
+            x_codes, x_scales = x_mx[a]
+            half = n0 // HALF
+            cols = slice(n0 - half * HALF, n0 - half * HALF + QUARTER)
+            sums[a, h, n0, 2] = next_bank()
+            for i in range(2):
+                r = 2 * h + i
+                for part in range(2):
+                    nc.tensor.matmul_mx(
+                        out=sums[a, h, n0, 2][:].rearrange("p i n -> p (i n)")[:, i * QUARTER : (i + 1) * QUARTER],
+                        lhsT=x_codes[:, r * P : (r + 1) * P].bitcast(FP8X4),
+                        lhsT_scale=x_scales[:, r * P : (r + 1) * P],
+                        rhs=w_codes[part, half][:, cols].bitcast(FP8X4),
+                        rhs_scale=w_scales[part, half][:, cols],
+                        start=(part == 0),
+                        stop=(part == 1),
+                    )
+
+        def pair_out(a, h, n0):
+            mid = keep.tile([P, PACK, P], F32, name="mid", bufs=MID_BUFS)
+            pair = mid[:].rearrange("p (i c) n -> p i (c n)", i=2)
+            nc.vector.tensor_tensor(
+                out=pair,
+                in0=sums[a, h, n0, 2][:].rearrange("p (i c) n -> p i (c n)", i=2),
+                in1=bias_rows[:, n0 : n0 + QUARTER].unsqueeze(1).to_broadcast([P, 2, QUARTER]),
+                op=ALU.add,
+            )
+            nc.scalar.activation(
+                out=result_of(a)[:, 2 * h : 2 * h + 2, n0 : n0 + QUARTER], in_=pair, func=SILU, bias=zero[:, 1:2]
+            )
 
         def cm_silu(a, nt):
             mids[a, nt] = keep.tile([P, PACK, P], F32, name="mid", bufs=MID_BUFS)
@@ -168,7 +218,12 @@ def tile_mix_hilo_tm_pl_silu_kernel(tc, w, x, b, out_0, out_1, out_2):
 
         def tm_add(a, r, half):
             mids[a, r, half] = keep.tile([P, PACK, P], F32, name="mid", bufs=MID_BUFS)
-            nc.vector.tensor_tensor(out=mids[a, r, half][:], in0=sums[a, r, half][:], in1=bias_rows[half][:], op=ALU.add)
+            nc.vector.tensor_tensor(
+                out=mids[a, r, half][:].rearrange("p i n -> p (i n)"),
+                in0=sums[a, r, half][:].rearrange("p i n -> p (i n)"),
+                in1=bias_rows[:, half * HALF : (half + 1) * HALF],
+                op=ALU.add,
+            )
 
         def tm_silu(a, r, half):
             nc.scalar.activation(
@@ -199,7 +254,7 @@ def tile_mix_hilo_tm_pl_silu_kernel(tc, w, x, b, out_0, out_1, out_2):
         def out_quantize(a, n0, n1):
             nc.vector.quantize_mx(
                 out=out_codes[:, a, n0:n1].bitcast(FP8X4),
-                scales=out_scales[:, a, n0:n1],
+                scales=scale_plane(a)[:, n0:n1],
                 in_=rounded[a, n0][:].rearrange("p n r -> p (n r)"),
             )
 
@@ -212,131 +267,151 @@ def tile_mix_hilo_tm_pl_silu_kernel(tc, w, x, b, out_0, out_1, out_2):
             nc.sync.dma_start(out=words[:, n0:n1], in_=out_codes[:, a, n0:n1].bitcast(I32))
 
         def store_scales(a0, a1, n0, n1, queues):
-            for q in range(4):
-                rows = out_2[a0:a1, 4 * q : 4 * q + 4, n0:n1].rearrange("a r n -> r a n").bitcast(I32)
-                queues[q].dma_start(out=rows, in_=out_scales[32 * q : 32 * q + 4, a0:a1, n0:n1].bitcast(I32))
-
-        def planes(a, n0, n1):
-            mid = (n0 + n1) // 2
-            out_cast(a, n0, mid, on_vector)
-            out_cast(a, mid, n1, on_vector)
-            out_quantize(a, n0, mid)
-            out_quantize(a, mid, n1)
+            for r in range(4):
+                rows = out_2[a0:a1, r:16:4, n0:n1].rearrange("a q n -> q a n").bitcast(I32)
+                queues[r].dma_start(out=rows, in_=out_scales[a0][r:P:32, :, n0:n1].bitcast(I32))
 
         out_codes = keep.tile([P, CHUNKS, M], U32, name="out_codes", align_bytes=64)
-        out_scales = keep.tile([P, CHUNKS, M], U8, name="out_scales", align_bytes=64)
+        out_scales = {
+            0: keep.tile([P, 1, M], U8, name="out_scales0", align_bytes=64),
+            1: keep.tile([P, 2, M], U8, name="out_scales1", align_bytes=64),
+        }
+
+        def scale_plane(a):
+            return out_scales[0][:, 0, :] if a == 0 else out_scales[1][:, a - 1, :]
+
         ident = keep.tile([P, P], F32, name="ident")
-        b_rows = keep.tile([P, P], F32, name="b_rows")
+        b_dealt = keep.tile([P, TILES], F32, name="b_dealt")
         bias_cols = keep.tile([P, TILES], F32, name="bias_cols")
-        bias_rows = [keep.tile([P, PACK, P], F32, name="bias_rows%d" % half) for half in range(2)]
+        bias_rows = keep.tile([P, M], F32, name="bias_rows")
         zero = keep.tile([P, 2], F32, name="zero")
 
-        def bias_columns():
-            bank = next_bank()
-            nc.tensor.transpose(bank[:, 0, :], b_rows[:], ident[:])
-            nc.scalar.copy(out=bias_cols[:], in_=bank[:, 0, 0:TILES])
-
-        def bias_spread(half):
+        def bias_spread(g):
             bank = next_bank()
             for i in range(PACK):
-                nt = half * PACK + i
-                nc.tensor.transpose(bank[:, i, :], bias_cols[:, nt : nt + 1].to_broadcast([P, P]), ident[:])
-            nc.scalar.copy(out=bias_rows[half][:], in_=bank[:])
+                c = g * PACK + i
+                nc.tensor.transpose(bank[:, i, :], b_dealt[:, c : c + 1].to_broadcast([P, P]), ident[:])
+            nc.scalar.copy(
+                out=bias_rows[:].rearrange("p (m c) -> p m c", c=TILES)[:, :, g * PACK : (g + 1) * PACK],
+                in_=bank[:].rearrange("p i m -> p m i"),
+            )
+
+        def bias_columns(n0, n1):
+            bank = next_bank()
+            for nt in range(n0, n1):
+                nc.tensor.transpose(bank[:, nt - n0, :], bias_rows[:, nt * P : (nt + 1) * P], ident[:])
+            nc.scalar.copy(out=bias_cols[:, n0:n1], in_=bank[:, 0 : n1 - n0, 0])
 
         nc.gpsimd.memset(zero[:, 0:1], 0.0)
         nc.scalar.activation(out=zero[:, 1:2], in_=zero[:, 0:1], func=SILU)
         make_identity(nc, ident[:])
-        nc.vector.memset(b_rows[:], 0.0)
-
 
         load("w", w_rows, w_raw, 0, 256)
-        nc.sync.dma_start(out=b_rows[0:TILES, :], in_=b.rearrange("(c n) -> c n", n=P))
+        nc.sync.dma_start(out=b_dealt[:], in_=b.rearrange("(p c) -> p c", c=TILES))
         load("x", x_rows, x_raw, 0, 512)
         load("w", w_rows, w_raw, 256, 512)
+        load("w", w_rows, w_raw, 512, 768)
         load("x", x_rows, x_raw, 512, 1024)
-        load("w", w_rows, w_raw, 512, 1024)
+        load("w", w_rows, w_raw, 768, 1024)
         load("x", x_rows, x_raw, 1024, 1536)
 
-        bias_columns()
-        bias_spread(1)
-
-        w_top(0, 256, on_vector)
-        w_mask(0)
-        w_low(0, 256)
-        x_cast(0, 256, on_vector)
-        x_cast(256, 512, on_scalar)
-        w_quantize(0, 0, 256)
-        w_quantize(1, 0, 256)
-        x_quantize(0)
-        w_top(256, 384, on_scalar)
-        w_top(384, 512, on_scalar)
+        w_top(0, 128, on_vector)
+        w_top(128, 256, on_vector)
         bias_spread(0)
-        w_mask(256)
-        w_low(256, 384)
+        bias_spread(1)
+        x_cast_slots(0, 1, on_scalar)
+        bias_columns(0, 4)
+        w_top(384, 512, on_scalar)
+        w_mask(0)
+        w_mask(128)
+        w_low(0, 128)
+        w_low(128, 256)
+        w_quantize(0, 0, 128)
+        x_cast_slots(0, 0, on_vector)
+        w_quantize(1, 0, 128)
+        w_quantize(0, 128, 256)
+        x_quantize(0, 0)
+        w_quantize(1, 128, 256)
+        cm_sum_slots(0, 0, 0)
+        cm_sum_slots(0, 1, 0)
+        x_quantize(0, 1)
+        w_top(256, 384, on_vector)
         w_mask(384)
-        w_quantize(0, 256, 384)
+        w_mask(256)
         w_low(384, 512)
-        w_quantize(1, 256, 384)
+        w_low(256, 384)
+        w_top(512, 768, on_scalar)
+        for nt in (0, 1):
+            cm_sum_slots(0, nt, 1)
+            cm_silu(0, nt)
+        w_quantize(0, 256, 384)
         w_quantize(0, 384, 512)
+        w_quantize(1, 256, 384)
         w_quantize(1, 384, 512)
-        x_cast(512, 1024, on_vector)
-        x_quantize(1)
 
-        cm_in(0, (0, 1, 2))
-        cm_out(0, (0, 1), on_scalar)
-        store_result(0, 0, 256)
-        w_top(512, 768, on_vector)
-        w_top(768, 1024, on_vector)
         w_mask(512)
-        w_mask(768)
+        x_cast_slots(1, 0, on_vector)
+        x_cast_slots(1, 1, on_vector)
+        x_quantize(1, 0)
+        x_quantize(1, 1)
         w_low(512, 768)
+        w_top(768, 1024, on_vector)
+        w_quantize(0, 512, 768)
+        w_mask(768)
+        w_quantize(1, 512, 768)
         w_low(768, 1024)
-        for part in range(2):
-            w_quantize(part, 512, 768)
-            w_quantize(part, 768, 1024)
-        x_cast(1024, 1536, on_vector)
-        cm_in(0, (3,))
-        cm_out(0, (2,), on_scalar)
-        cm_in(1, (0, 1))
-        cm_out(0, (3,), on_scalar)
-        store_result(0, 256, 512)
-        cm_in(1, (2, 3))
-        cm_out(1, (0, 1), on_scalar)
-        store_result(1, 0, 256)
-        cm_out(1, (2, 3), on_scalar)
-        store_result(1, 256, 512)
+        w_quantize(0, 768, 1024)
+        w_quantize(1, 768, 1024)
+        x_cast_slots(2, 0, on_vector)
+        x_cast_slots(2, 1, on_vector)
+        x_quantize(2, 0)
+        x_quantize(2, 1)
 
-        out_cast(0, 0, 256, on_scalar)
+        order = [(a, nt) for a in (0, 1) for nt in range(4)]
+        for i, (a, nt) in enumerate(order):
+            if i + 2 < len(order):
+                cm_in(order[i + 2][0], (order[i + 2][1],))
+            if i == 7:
+                tm_sum(0, 0, 1)
+            cm_out(a, (nt,), on_scalar)
+            if nt % 2:
+                store_result(a, (nt - 1) * P, (nt + 1) * P)
+            if i == 1:
+                out_cast(0, 0, 128, on_scalar)
+
+        def bank(a, r, half):
+            if (a, r, half) not in sums:
+                tm_sum(a, r, half)
+            tm_add(a, r, half)
+            tm_silu(a, r, half)
+
+        out_cast(0, 128, 256, on_scalar)
+        out_cast_gpsimd(0, 256, 512, "x_dealt2_1")
+        out_cast_gpsimd(1, 0, 512, "rounded1_0")
         for a in (0, 1):
             for r in range(PACK):
-                tm_sum(a, r, 1)
-                tm_add(a, r, 1)
-                tm_silu(a, r, 1)
-                if a == 0 and r == 0:
-                    x_quantize(2)
-                    out_cast_gpsimd(1, 0, 512, "x_dealt2")
-                    out_cast_gpsimd(0, 256, 512, "rounded0_256")
+                bank(a, r, 1)
                 if r % 2:
                     store_result(a, HALF, M, r - 1, r + 1)
-        out_cast_gpsimd(0, 512, 768, "rounded0_512")
-        out_cast_gpsimd(0, 768, 1024, "rounded0_768")
+        out_cast_gpsimd(0, 512, 1024, "rounded0_512")
         for r in range(PACK):
             for half in range(2):
-                tm_sum(2, r, half)
-                tm_add(2, r, half)
-                tm_silu(2, r, half)
+                bank(2, r, half)
             store_result(2, 0, M, r, r + 1)
-        for n0 in (0, 256, 512):
-            out_cast(2, n0, n0 + QUARTER, on_scalar)
-        for n0 in range(0, M, QUARTER):
-            out_quantize(0, n0, n0 + QUARTER)
+        out_quantize(0, 256, 512)
+        out_quantize(0, 0, 128)
+        out_quantize(0, 128, 256)
+        out_quantize(0, 512, 1024)
         store_codes(0, 0, M)
+        out_cast(2, 0, 256, on_scalar)
+        store_scales(0, 1, 0, M, [nc.scalar] * 4)
+        out_cast(2, 256, 512, on_scalar)
+        out_cast(2, 512, 768, on_scalar)
         out_cast(1, 512, 768, on_vector)
         out_cast(1, 768, 1024, on_vector)
         out_quantize(1, 0, 512)
         out_quantize(1, 512, 768)
         out_quantize(1, 768, 1024)
-        store_scales(0, 2, 0, M, [nc.sync] * 4)
         store_codes(1, 0, M)
         out_cast(2, 768, 1024, on_vector)
         out_quantize(2, 0, 256)
@@ -345,4 +420,4 @@ def tile_mix_hilo_tm_pl_silu_kernel(tc, w, x, b, out_0, out_1, out_2):
         out_quantize(2, 768, 1024)
         out_quantize(2, 512, 768)
         store_codes(2, 512, 1024)
-        store_scales(2, 3, 0, M, [nc.scalar, nc.scalar, nc.sync, nc.sync])
+        store_scales(1, 3, 0, M, [nc.scalar, nc.scalar, nc.sync, nc.sync])

@@ -60,21 +60,25 @@ def tile_mix_hilo_tm_pl_silu_kernel(tc, w, x, b, out_0, out_1, out_2):
                 if l0 <= c0 and c1 <= l1:
                     return raw[:, :, c0 - l0 : c1 - l0]
 
-        def w_top(n0, n1, copy):
-            for part in range(2):
-                w_parts[part, n0] = keep.tile([P, n1 - n0, PACK], BF16, name="w_part%d_%d" % (part, n0), align_bytes=64)
-            halves = columns(w_raw, n0, n1).bitcast(BF16).rearrange("p j (c i e) -> p c j i e", i=RUN, e=2)
-            copy(out=w_parts[0, n0][:].rearrange("p (c i) j -> p c j i", i=RUN), in_=halves[:, :, :, :, 1])
+        def w_part(part, n0, n1):
+            q0 = n0 // QUARTER * QUARTER
+            if (part, q0) not in w_parts:
+                w_parts[part, q0] = keep.tile([P, QUARTER, PACK], BF16, name="w_part%d_%d" % (part, q0), align_bytes=64)
+            return w_parts[part, q0][:, n0 - q0 : n1 - q0, :]
 
-        def w_mask(n0):
-            pairs = w_parts[0, n0][:].rearrange("p n j -> p (n j)").bitcast(I32)
+        def w_top(n0, n1, copy):
+            halves = columns(w_raw, n0, n1).bitcast(BF16).rearrange("p j (c i e) -> p c j i e", i=RUN, e=2)
+            copy(out=w_part(0, n0, n1).rearrange("p (c i) j -> p c j i", i=RUN), in_=halves[:, :, :, :, 1])
+
+        def w_mask(n0, n1):
+            pairs = w_part(0, n0, n1).rearrange("p n j -> p (n j)").bitcast(I32)
             nc.vector.tensor_scalar(out=pairs, in0=pairs, scalar1=HI_MASK_PAIR, scalar2=None, op0=ALU.bitwise_and)
 
         def w_low(n0, n1):
             nc.vector.tensor_tensor(
-                out=w_parts[1, n0][:].rearrange("p (c i) j -> p c j i", i=RUN),
+                out=w_part(1, n0, n1).rearrange("p (c i) j -> p c j i", i=RUN),
                 in0=columns(w_raw, n0, n1).rearrange("p j (c i) -> p c j i", i=RUN),
-                in1=w_parts[0, n0][:].rearrange("p (c i) j -> p c j i", i=RUN),
+                in1=w_part(0, n0, n1).rearrange("p (c i) j -> p c j i", i=RUN),
                 op=ALU.subtract,
             )
 
@@ -87,15 +91,16 @@ def tile_mix_hilo_tm_pl_silu_kernel(tc, w, x, b, out_0, out_1, out_2):
             nc.vector.quantize_mx(
                 out=w_codes[part, half][:, cols].bitcast(FP8X4),
                 scales=w_scales[part, half][:, cols],
-                in_=w_parts[part, n0][:].rearrange("p n j -> p (n j)"),
+                in_=w_part(part, n0, n1).rearrange("p n j -> p (n j)"),
             )
 
-        def x_cast_slots(a, h, copy, name=None):
-            x_dealt[a, h] = keep.tile([P, 2, P, PACK], BF16, name=name or "x_dealt%d_%d" % (a, h), align_bytes=64)
+        def x_cast_slots(a, h, copy, m0=0, m1=P):
+            if (a, h) not in x_dealt:
+                x_dealt[a, h] = keep.tile([P, 2, P, PACK], BF16, name="x_dealt%d_%d" % (a, h), align_bytes=64)
             copy(
-                out=x_dealt[a, h][:].rearrange("p r m j -> p m j r"),
+                out=x_dealt[a, h][:, :, m0:m1, :].rearrange("p r m j -> p m j r"),
                 in_=columns(x_raw, a * CHUNK, (a + 1) * CHUNK).rearrange("p j (m r) -> p m j r", r=PACK)[
-                    :, :, :, 2 * h : 2 * h + 2
+                    :, m0:m1, :, 2 * h : 2 * h + 2
                 ],
             )
 
@@ -233,17 +238,23 @@ def tile_mix_hilo_tm_pl_silu_kernel(tc, w, x, b, out_0, out_1, out_2):
                 bias=zero[:, 1:2],
             )
 
-        def out_cast(a, n0, n1, copy):
-            rounded[a, n0] = keep.tile([P, n1 - n0, PACK], BF16, name="rounded%d_%d" % (a, n0), align_bytes=64)
+        def rounded_tile(a, n0, n1, name=None):
+            rounded[a, n0, n1] = keep.tile([P, n1 - n0, PACK], BF16, name=name or "rounded%d_%d" % (a, n0), align_bytes=64)
+
+        def rounded_of(a, n0, n1):
+            for (ra, r0, r1), tile in rounded.items():
+                if ra == a and r0 <= n0 and n1 <= r1:
+                    return tile[:, n0 - r0 : n1 - r0, :]
+
+        def out_cast(a, n0, n1, copy, run=RUN):
             copy(
-                out=rounded[a, n0][:].rearrange("p (c i) r -> p c r i", i=RUN),
-                in_=result_of(a)[:, :, n0:n1].rearrange("p r (c i) -> p c r i", i=RUN),
+                out=rounded_of(a, n0, n1).rearrange("p (c i) r -> p c r i", i=run),
+                in_=result_of(a)[:, :, n0:n1].rearrange("p r (c i) -> p c r i", i=run),
             )
 
-        def out_cast_gpsimd(a, n0, n1, name):
-            rounded[a, n0] = keep.tile([P, n1 - n0, PACK], BF16, name=name, align_bytes=64)
+        def out_cast_gpsimd(a, n0, n1):
             nc.gpsimd.tensor_scalar(
-                out=rounded[a, n0][:],
+                out=rounded_of(a, n0, n1),
                 in0=result_of(a)[:, :, n0:n1].rearrange("p r n -> p n r"),
                 scalar1=1.0,
                 scalar2=-0.0,
@@ -255,7 +266,7 @@ def tile_mix_hilo_tm_pl_silu_kernel(tc, w, x, b, out_0, out_1, out_2):
             nc.vector.quantize_mx(
                 out=out_codes[:, a, n0:n1].bitcast(FP8X4),
                 scales=scale_plane(a)[:, n0:n1],
-                in_=rounded[a, n0][:].rearrange("p n r -> p (n r)"),
+                in_=rounded_of(a, n0, n1).rearrange("p n r -> p (n r)"),
             )
 
         def store_result(a, n0, n1, r0=0, r1=PACK):
@@ -319,37 +330,33 @@ def tile_mix_hilo_tm_pl_silu_kernel(tc, w, x, b, out_0, out_1, out_2):
         w_top(128, 256, on_vector)
         bias_spread(0)
         bias_spread(1)
-        x_cast_slots(0, 1, on_scalar)
+        x_cast_slots(0, 1, on_scalar, 32, P)
         bias_columns(0, 4)
         w_top(384, 512, on_scalar)
-        w_mask(0)
-        w_mask(128)
+        w_mask(0, 128)
+        w_mask(128, 256)
         w_low(0, 128)
         w_low(128, 256)
-        w_quantize(0, 0, 128)
+        w_quantize(0, 0, 256)
         x_cast_slots(0, 0, on_vector)
-        w_quantize(1, 0, 128)
-        w_quantize(0, 128, 256)
+        w_quantize(1, 0, 256)
+        x_cast_slots(0, 1, on_vector, 0, 32)
         x_quantize(0, 0)
-        w_quantize(1, 128, 256)
         cm_sum_slots(0, 0, 0)
         cm_sum_slots(0, 1, 0)
         x_quantize(0, 1)
         w_top(256, 384, on_vector)
-        w_mask(384)
-        w_mask(256)
+        w_mask(384, 512)
+        w_mask(256, 384)
         w_low(384, 512)
         w_low(256, 384)
         w_top(512, 768, on_scalar)
         for nt in (0, 1):
             cm_sum_slots(0, nt, 1)
             cm_silu(0, nt)
-        w_quantize(0, 256, 384)
-        w_quantize(0, 384, 512)
-        w_quantize(1, 256, 384)
-        w_quantize(1, 384, 512)
-
-        w_mask(512)
+        w_quantize(0, 256, 512)
+        w_quantize(1, 256, 512)
+        w_mask(512, 768)
         x_cast_slots(1, 0, on_vector)
         x_cast_slots(1, 1, on_vector)
         x_quantize(1, 0)
@@ -357,7 +364,7 @@ def tile_mix_hilo_tm_pl_silu_kernel(tc, w, x, b, out_0, out_1, out_2):
         w_low(512, 768)
         w_top(768, 1024, on_vector)
         w_quantize(0, 512, 768)
-        w_mask(768)
+        w_mask(768, 1024)
         w_quantize(1, 512, 768)
         w_low(768, 1024)
         w_quantize(0, 768, 1024)
@@ -367,9 +374,14 @@ def tile_mix_hilo_tm_pl_silu_kernel(tc, w, x, b, out_0, out_1, out_2):
         x_quantize(2, 0)
         x_quantize(2, 1)
 
+        rounded_tile(0, 0, 256)
         order = [(a, nt) for a in (0, 1) for nt in range(4)]
         for i, (a, nt) in enumerate(order):
-            if i + 2 < len(order):
+            if i == 2:
+                cm_sum_slots(1, 0, 0)
+                cm_sum_slots(1, 0, 1)
+                cm_silu(1, 0)
+            elif i + 2 < len(order):
                 cm_in(order[i + 2][0], (order[i + 2][1],))
             if i == 7:
                 tm_sum(0, 0, 1)
@@ -377,7 +389,7 @@ def tile_mix_hilo_tm_pl_silu_kernel(tc, w, x, b, out_0, out_1, out_2):
             if nt % 2:
                 store_result(a, (nt - 1) * P, (nt + 1) * P)
             if i == 1:
-                out_cast(0, 0, 128, on_scalar)
+                out_cast(0, 0, 128, on_scalar, RUN)
 
         def bank(a, r, half):
             if (a, r, half) not in sums:
@@ -385,39 +397,42 @@ def tile_mix_hilo_tm_pl_silu_kernel(tc, w, x, b, out_0, out_1, out_2):
             tm_add(a, r, half)
             tm_silu(a, r, half)
 
-        out_cast(0, 128, 256, on_scalar)
-        out_cast_gpsimd(0, 256, 512, "x_dealt2_1")
-        out_cast_gpsimd(1, 0, 512, "rounded1_0")
+        rounded_tile(0, 256, 512, "x_dealt2_1")
+        rounded_tile(0, 512, 1024)
+        rounded_tile(1, 0, 512)
+        rounded_tile(1, 512, 1024)
+        rounded_tile(2, 0, 512)
+        rounded_tile(2, 512, 768)
+        rounded_tile(2, 768, 1024)
+        out_cast_gpsimd(0, 256, 512)
+        out_cast_gpsimd(1, 0, 512)
         for a in (0, 1):
             for r in range(PACK):
                 bank(a, r, 1)
                 if r % 2:
                     store_result(a, HALF, M, r - 1, r + 1)
-        out_cast_gpsimd(0, 512, 1024, "rounded0_512")
+        out_cast_gpsimd(0, 512, 1024)
+        out_cast_gpsimd(1, 512, 640)
         for r in range(PACK):
             for half in range(2):
                 bank(2, r, half)
             store_result(2, 0, M, r, r + 1)
+        out_cast(2, 0, 512, on_scalar, RUN)
+        out_cast(2, 768, 1024, on_scalar, RUN)
+        out_cast(0, 128, 256, on_vector)
         out_quantize(0, 256, 512)
-        out_quantize(0, 0, 128)
-        out_quantize(0, 128, 256)
         out_quantize(0, 512, 1024)
+        out_quantize(0, 0, 256)
+        store_scales(0, 1, 0, M, [nc.sync] * 4)
         store_codes(0, 0, M)
-        out_cast(2, 0, 256, on_scalar)
-        store_scales(0, 1, 0, M, [nc.scalar] * 4)
-        out_cast(2, 256, 512, on_scalar)
-        out_cast(2, 512, 768, on_scalar)
-        out_cast(1, 512, 768, on_vector)
-        out_cast(1, 768, 1024, on_vector)
+        out_cast(1, 640, 1024, on_vector)
         out_quantize(1, 0, 512)
-        out_quantize(1, 512, 768)
-        out_quantize(1, 768, 1024)
+        out_quantize(1, 512, 1024)
         store_codes(1, 0, M)
-        out_cast(2, 768, 1024, on_vector)
-        out_quantize(2, 0, 256)
-        out_quantize(2, 256, 512)
-        store_codes(2, 0, 512)
-        out_quantize(2, 768, 1024)
+        out_cast(2, 512, 768, on_vector)
+        out_quantize(2, 0, 512)
         out_quantize(2, 512, 768)
-        store_codes(2, 512, 1024)
+        store_codes(2, 0, 768)
+        out_quantize(2, 768, 1024)
+        store_codes(2, 768, 1024)
         store_scales(1, 3, 0, M, [nc.scalar, nc.scalar, nc.sync, nc.sync])

@@ -51,7 +51,7 @@ def tile_mix_hilo_tm_pl_silu_kernel(tc, w, x, b, out_0, out_1, out_2):
             return psum.tile([P, PACK, P], F32, name="bank%d" % index)
 
         def load(name, rows, loaded, c0, c1):
-            raw = keep.tile([P, PACK, c1 - c0], F32, name="%s_raw%d" % (name, c0))
+            raw = keep.tile([P, PACK, c1 - c0], F32, name="%s_raw%d" % (name, c0), align_bytes=256)
             nc.sync.dma_start(out=raw[:], in_=rows[:, :, c0:c1])
             loaded[c0, c1] = raw
 
@@ -118,7 +118,7 @@ def tile_mix_hilo_tm_pl_silu_kernel(tc, w, x, b, out_0, out_1, out_2):
 
         def result_of(a):
             if a not in results:
-                results[a] = keep.tile([P, PACK, M], F32, name="result%d" % a)
+                results[a] = keep.tile([P, PACK, M], F32, name="result%d" % a, align_bytes=256)
             return results[a]
 
         def cm_sum(a, nt):
@@ -282,10 +282,10 @@ def tile_mix_hilo_tm_pl_silu_kernel(tc, w, x, b, out_0, out_1, out_2):
                 rows = out_2[a0:a1, r:16:4, n0:n1].rearrange("a q n -> q a n").bitcast(I32)
                 queues[r].dma_start(out=rows, in_=out_scales[a0][r:P:32, :, n0:n1].bitcast(I32))
 
-        out_codes = keep.tile([P, CHUNKS, M], U32, name="out_codes", align_bytes=64)
+        out_codes = keep.tile([P, CHUNKS, M], U32, name="out_codes", align_bytes=256)
         out_scales = {
-            0: keep.tile([P, 1, M], U8, name="out_scales0", align_bytes=64),
-            1: keep.tile([P, 2, M], U8, name="out_scales1", align_bytes=64),
+            0: keep.tile([P, 1, M], U8, name="out_scales0", align_bytes=256),
+            1: keep.tile([P, 2, M], U8, name="out_scales1", align_bytes=256),
         }
 
         def scale_plane(a):

@@ -141,7 +141,8 @@ def tile_mix_hilo_tm_pl_silu_kernel(tc, w, x, b, out_0, out_1, out_2):
             x_codes, x_scales = x_mx[a]
             cols = slice(nt * P, (nt + 1) * P)
             tokens = slice(2 * h * P, (2 * h + 2) * P)
-            if h == 0:
+            first = (a, nt) not in sums
+            if first:
                 sums[a, nt] = next_bank()
             for part in range(2):
                 nc.tensor.matmul_mx(
@@ -150,8 +151,8 @@ def tile_mix_hilo_tm_pl_silu_kernel(tc, w, x, b, out_0, out_1, out_2):
                     lhsT_scale=w_scales[part, 0][:, cols],
                     rhs=x_codes[:, tokens].bitcast(FP8X4),
                     rhs_scale=x_scales[:, tokens],
-                    start=(part == 0 and h == 0),
-                    stop=(part == 1 and h == 1),
+                    start=(part == 0 and first),
+                    stop=(part == 1 and not first),
                 )
 
         def pair_sum(a, h, n0):
@@ -207,10 +208,11 @@ def tile_mix_hilo_tm_pl_silu_kernel(tc, w, x, b, out_0, out_1, out_2):
                 turn(a, nt)
                 copy_out(a, nt, copy)
 
-        def tm_sum(a, r, half):
+        def tm_sum(a, r, half, parts=(0, 1)):
             x_codes, x_scales = x_mx[a]
-            sums[a, r, half] = next_bank()
-            for part in range(2):
+            if 0 in parts:
+                sums[a, r, half] = next_bank()
+            for part in parts:
                 nc.tensor.matmul_mx(
                     out=sums[a, r, half][:].rearrange("p i n -> p (i n)"),
                     lhsT=x_codes[:, r * P : (r + 1) * P].bitcast(FP8X4),
@@ -330,7 +332,7 @@ def tile_mix_hilo_tm_pl_silu_kernel(tc, w, x, b, out_0, out_1, out_2):
         w_top(128, 256, on_vector)
         bias_spread(0)
         bias_spread(1)
-        x_cast_slots(0, 1, on_scalar, 32, P)
+        x_cast_slots(0, 1, on_scalar)
         bias_columns(0, 4)
         w_top(384, 512, on_scalar)
         w_mask(0, 128)
@@ -340,39 +342,36 @@ def tile_mix_hilo_tm_pl_silu_kernel(tc, w, x, b, out_0, out_1, out_2):
         w_quantize(0, 0, 256)
         x_cast_slots(0, 0, on_vector)
         w_quantize(1, 0, 256)
-        x_cast_slots(0, 1, on_vector, 0, 32)
+        w_top(256, 384, on_vector)
         x_quantize(0, 0)
         cm_sum_slots(0, 0, 0)
         cm_sum_slots(0, 1, 0)
-        x_quantize(0, 1)
-        w_top(256, 384, on_vector)
-        w_mask(384, 512)
         w_mask(256, 384)
-        w_low(384, 512)
+        w_mask(384, 512)
+        x_quantize(0, 1)
         w_low(256, 384)
+        w_low(384, 512)
         w_top(512, 768, on_scalar)
         for nt in (0, 1):
             cm_sum_slots(0, nt, 1)
             cm_silu(0, nt)
+        x_cast_slots(1, 1, on_scalar, 0, 48)
         w_quantize(0, 256, 512)
         w_quantize(1, 256, 512)
         w_mask(512, 768)
         x_cast_slots(1, 0, on_vector)
-        x_cast_slots(1, 1, on_vector)
+        x_cast_slots(1, 1, on_vector, 48, P)
         x_quantize(1, 0)
         x_quantize(1, 1)
-        w_low(512, 768)
         w_top(768, 1024, on_vector)
-        w_quantize(0, 512, 768)
+        w_low(512, 768)
         w_mask(768, 1024)
+        w_quantize(0, 512, 768)
         w_quantize(1, 512, 768)
         w_low(768, 1024)
         w_quantize(0, 768, 1024)
-        w_quantize(1, 768, 1024)
         x_cast_slots(2, 0, on_vector)
-        x_cast_slots(2, 1, on_vector)
-        x_quantize(2, 0)
-        x_quantize(2, 1)
+        w_quantize(1, 768, 1024)
 
         rounded_tile(0, 0, 256)
         order = [(a, nt) for a in (0, 1) for nt in range(4)]
@@ -383,17 +382,21 @@ def tile_mix_hilo_tm_pl_silu_kernel(tc, w, x, b, out_0, out_1, out_2):
                 cm_silu(1, 0)
             elif i + 2 < len(order):
                 cm_in(order[i + 2][0], (order[i + 2][1],))
+            if i == 3:
+                x_cast_slots(2, 1, on_scalar, 0, 32)
             if i == 7:
-                tm_sum(0, 0, 1)
+                for r in range(2):
+                    tm_sum(0, r, 1, (0,))
             cm_out(a, (nt,), on_scalar)
             if nt % 2:
                 store_result(a, (nt - 1) * P, (nt + 1) * P)
-            if i == 1:
-                out_cast(0, 0, 128, on_scalar, RUN)
+        x_cast_slots(2, 1, on_vector, 32, P)
+        x_quantize(2, 0)
+        x_quantize(2, 1)
+        out_cast(0, 0, 128, on_scalar, RUN)
 
         def bank(a, r, half):
-            if (a, r, half) not in sums:
-                tm_sum(a, r, half)
+            tm_sum(a, r, half, (1,) if (a, r, half) in sums else (0, 1))
             tm_add(a, r, half)
             tm_silu(a, r, half)
 
@@ -412,7 +415,7 @@ def tile_mix_hilo_tm_pl_silu_kernel(tc, w, x, b, out_0, out_1, out_2):
                 if r % 2:
                     store_result(a, HALF, M, r - 1, r + 1)
         out_cast_gpsimd(0, 512, 1024)
-        out_cast_gpsimd(1, 512, 640)
+        out_cast_gpsimd(1, 512, 704)
         for r in range(PACK):
             for half in range(2):
                 bank(2, r, half)
@@ -425,14 +428,14 @@ def tile_mix_hilo_tm_pl_silu_kernel(tc, w, x, b, out_0, out_1, out_2):
         out_quantize(0, 0, 256)
         store_scales(0, 1, 0, M, [nc.sync] * 4)
         store_codes(0, 0, M)
-        out_cast(1, 640, 1024, on_vector)
+        out_cast(1, 704, 1024, on_vector)
         out_quantize(1, 0, 512)
         out_quantize(1, 512, 1024)
         store_codes(1, 0, M)
         out_cast(2, 512, 768, on_vector)
         out_quantize(2, 0, 512)
+        store_codes(2, 0, 512)
         out_quantize(2, 512, 768)
-        store_codes(2, 0, 768)
         out_quantize(2, 768, 1024)
-        store_codes(2, 768, 1024)
-        store_scales(1, 3, 0, M, [nc.scalar, nc.scalar, nc.sync, nc.sync])
+        store_codes(2, 512, 1024)
+        store_scales(1, 3, 0, M, [nc.sync] * 4)

@@ -24,7 +24,14 @@ QUARTER = M // 4
 TILES = M // P
 RUN = 4
 BANKS = 8
-MID_BUFS = 12
+MID_BUFS = 6
+SCALE_GROUPS = ((0, 1), (1, 3))
+S_EARLY = 128
+G_START = 128
+G_END = 768
+S_LAST = 768
+X2_AFTER = 2
+PANEL_BANKS = 4
 HI_MASK_PAIR = 0xFFF0FFF0 - (1 << 32)
 
 
@@ -33,6 +40,9 @@ def tile_mix_hilo_tm_pl_silu_kernel(tc, w, x, b, out_0, out_1, out_2):
     on_vector = nc.vector.tensor_copy
     on_scalar = nc.scalar.copy
 
+    def on_gpsimd(out, in_):
+        nc.gpsimd.tensor_scalar(out=out, in0=in_, scalar1=1.0, scalar2=-0.0, op0=ALU.mult, op1=ALU.add)
+
     with ExitStack() as ctx:
         keep = ctx.enter_context(tc.tile_pool(name="keep", bufs=1))
         psum = ctx.enter_context(tc.psum_pool(name="psum", bufs=1))
@@ -40,15 +50,26 @@ def tile_mix_hilo_tm_pl_silu_kernel(tc, w, x, b, out_0, out_1, out_2):
 
         w_rows = w.rearrange("(p j) n -> p j n", j=PACK)
         x_rows = x.rearrange("(p j) t -> p j t", j=PACK)
-        w_raw, w_parts, w_codes, w_scales = {}, {}, {}, {}
-        x_raw, x_dealt, x_mx = {}, {}, {}
-        sums, mids, turned, results, rounded = {}, {}, {}, {}, {}
+        w_raw, x_raw, staged, w_mx, x_mx, sums, results = {}, {}, {}, {}, {}, {}, {}
         banks_taken = []
 
+        strip_banks = []
+
         def next_bank():
-            index = len(banks_taken) % BANKS
+            index = len(banks_taken) % PANEL_BANKS
             banks_taken.append(index)
-            return psum.tile([P, PACK, P], F32, name="bank%d" % index)
+            return psum.tile([P, HALF], F32, name="bank%d" % index)
+
+        def next_strip_bank():
+            i = len(strip_banks)
+            if i < BANKS - PANEL_BANKS:
+                index = PANEL_BANKS + i
+            elif i < BANKS:
+                index = (len(banks_taken) + i - (BANKS - PANEL_BANKS)) % PANEL_BANKS
+            else:
+                index = strip_banks[i - BANKS]
+            strip_banks.append(index)
+            return psum.tile([P, HALF], F32, name="bank%d" % index)
 
         def load(name, rows, loaded, c0, c1):
             raw = keep.tile([P, PACK, c1 - c0], F32, name="%s_raw%d" % (name, c0), align_bytes=256)
@@ -60,60 +81,65 @@ def tile_mix_hilo_tm_pl_silu_kernel(tc, w, x, b, out_0, out_1, out_2):
                 if l0 <= c0 and c1 <= l1:
                     return raw[:, :, c0 - l0 : c1 - l0]
 
-        def w_part(part, n0, n1):
-            q0 = n0 // QUARTER * QUARTER
-            if (part, q0) not in w_parts:
-                w_parts[part, q0] = keep.tile([P, QUARTER, PACK], BF16, name="w_part%d_%d" % (part, q0), align_bytes=64)
-            return w_parts[part, q0][:, n0 - q0 : n1 - q0, :]
+        def stage(kind, c0, c1, buffer=None):
+            staged[kind, c0, c1] = keep.tile([P, c1 - c0, PACK], BF16, name=buffer or "%s_%d" % (kind, c0), align_bytes=64)
 
-        def w_top(n0, n1, copy):
-            halves = columns(w_raw, n0, n1).bitcast(BF16).rearrange("p j (c i e) -> p c j i e", i=RUN, e=2)
-            copy(out=w_part(0, n0, n1).rearrange("p (c i) j -> p c j i", i=RUN), in_=halves[:, :, :, :, 1])
+        def staged_cols(kind, c0, c1):
+            for (k, l0, l1), tile in staged.items():
+                if k == kind and l0 <= c0 and c1 <= l1:
+                    return tile[:, c0 - l0 : c1 - l0, :]
+
+        def in_runs(view, run):
+            return view.rearrange("p (c i) j -> p c j i", i=run) if run > 1 else view
+
+        def rows_in_runs(view, run):
+            return view.rearrange("p j (c i) -> p c j i", i=run) if run > 1 else view.rearrange("p j c -> p c j")
+
+        def w_top(n0, n1, copy, run=RUN):
+            upper = columns(w_raw, n0, n1).bitcast(BF16).rearrange("p j (n e) -> p j n e", e=2)[:, :, :, 1]
+            copy(out=in_runs(staged_cols("hi", n0, n1), run), in_=rows_in_runs(upper, run))
 
         def w_mask(n0, n1):
-            pairs = w_part(0, n0, n1).rearrange("p n j -> p (n j)").bitcast(I32)
+            pairs = staged_cols("hi", n0, n1).rearrange("p n j -> p (n j)").bitcast(I32)
             nc.vector.tensor_scalar(out=pairs, in0=pairs, scalar1=HI_MASK_PAIR, scalar2=None, op0=ALU.bitwise_and)
 
-        def w_low(n0, n1):
-            nc.vector.tensor_tensor(
-                out=w_part(1, n0, n1).rearrange("p (c i) j -> p c j i", i=RUN),
-                in0=columns(w_raw, n0, n1).rearrange("p j (c i) -> p c j i", i=RUN),
-                in1=w_part(0, n0, n1).rearrange("p (c i) j -> p c j i", i=RUN),
+        def w_low(n0, n1, engine, run=RUN):
+            engine.tensor_tensor(
+                out=in_runs(staged_cols("lo", n0, n1), run),
+                in0=rows_in_runs(columns(w_raw, n0, n1), run),
+                in1=in_runs(staged_cols("hi", n0, n1), run),
                 op=ALU.subtract,
             )
 
         def w_quantize(part, n0, n1):
             half = n0 // HALF
-            if (part, half) not in w_codes:
-                w_codes[part, half] = keep.tile([P, HALF], U32, name="w_codes%d_%d" % (part, half), align_bytes=64)
-                w_scales[part, half] = keep.tile([P, HALF], U8, name="w_scales%d_%d" % (part, half), align_bytes=64)
+            if (part, half) not in w_mx:
+                codes = keep.tile([P, HALF], U32, name="w_codes_%s%d" % (part, half), align_bytes=64)
+                scales = keep.tile([P, HALF], U8, name="w_scales_%s%d" % (part, half), align_bytes=64)
+                w_mx[part, half] = (codes, scales)
+            codes, scales = w_mx[part, half]
             cols = slice(n0 - half * HALF, n1 - half * HALF)
             nc.vector.quantize_mx(
-                out=w_codes[part, half][:, cols].bitcast(FP8X4),
-                scales=w_scales[part, half][:, cols],
-                in_=w_part(part, n0, n1).rearrange("p n j -> p (n j)"),
+                out=codes[:, cols].bitcast(FP8X4),
+                scales=scales[:, cols],
+                in_=staged_cols(part, n0, n1).rearrange("p n j -> p (n j)"),
             )
 
-        def x_cast_slots(a, h, copy, m0=0, m1=P):
-            if (a, h) not in x_dealt:
-                x_dealt[a, h] = keep.tile([P, 2, P, PACK], BF16, name="x_dealt%d_%d" % (a, h), align_bytes=64)
-            copy(
-                out=x_dealt[a, h][:, :, m0:m1, :].rearrange("p r m j -> p m j r"),
-                in_=columns(x_raw, a * CHUNK, (a + 1) * CHUNK).rearrange("p j (m r) -> p m j r", r=PACK)[
-                    :, m0:m1, :, 2 * h : 2 * h + 2
-                ],
-            )
+        def x_round(a, h, copy, m0=0, m1=P):
+            dealt = staged_cols("x%d" % a, 2 * h * P, (2 * h + 2) * P).rearrange("p (r m) j -> p m j r", r=2)
+            tokens = columns(x_raw, a * CHUNK + PACK * m0, a * CHUNK + PACK * m1).rearrange("p j (m r) -> p m j r", r=PACK)
+            copy(out=dealt[:, m0:m1], in_=tokens[:, :, :, 2 * h : 2 * h + 2])
 
-        def x_quantize(a, h):
+        def x_quantize(a, r0, r1):
             if a not in x_mx:
                 codes = keep.tile([P, CHUNK], U32, name="x_codes%d" % a, align_bytes=64)
                 scales = keep.tile([P, CHUNK], U8, name="x_scales%d" % a, align_bytes=64)
                 x_mx[a] = (codes, scales)
             codes, scales = x_mx[a]
             nc.vector.quantize_mx(
-                out=codes[:, 2 * h * P : (2 * h + 2) * P].bitcast(FP8X4),
-                scales=scales[:, 2 * h * P : (2 * h + 2) * P],
-                in_=x_dealt[a, h][:].rearrange("p r m j -> p (r m j)"),
+                out=codes[:, r0 * P : r1 * P].bitcast(FP8X4),
+                scales=scales[:, r0 * P : r1 * P],
+                in_=staged_cols("x%d" % a, r0 * P, r1 * P).rearrange("p c j -> p (c j)"),
             )
 
         def result_of(a):
@@ -121,157 +147,49 @@ def tile_mix_hilo_tm_pl_silu_kernel(tc, w, x, b, out_0, out_1, out_2):
                 results[a] = keep.tile([P, PACK, M], F32, name="result%d" % a, align_bytes=256)
             return results[a]
 
-        def cm_sum(a, nt):
-            x_codes, x_scales = x_mx[a]
-            half = nt * P // HALF
-            cols = slice(nt * P - half * HALF, (nt + 1) * P - half * HALF)
-            sums[a, nt] = next_bank()
-            for part in range(2):
-                nc.tensor.matmul_mx(
-                    out=sums[a, nt][:].rearrange("p r m -> p (r m)"),
-                    lhsT=w_codes[part, half][:, cols].bitcast(FP8X4),
-                    lhsT_scale=w_scales[part, half][:, cols],
-                    rhs=x_codes[:].bitcast(FP8X4),
-                    rhs_scale=x_scales[:],
-                    start=(part == 0),
-                    stop=(part == 1),
-                )
-
-        def cm_sum_slots(a, nt, h):
-            x_codes, x_scales = x_mx[a]
-            cols = slice(nt * P, (nt + 1) * P)
-            tokens = slice(2 * h * P, (2 * h + 2) * P)
-            first = (a, nt) not in sums
-            if first:
-                sums[a, nt] = next_bank()
-            for part in range(2):
-                nc.tensor.matmul_mx(
-                    out=sums[a, nt][:].rearrange("p r m -> p (r m)")[:, tokens],
-                    lhsT=w_codes[part, 0][:, cols].bitcast(FP8X4),
-                    lhsT_scale=w_scales[part, 0][:, cols],
-                    rhs=x_codes[:, tokens].bitcast(FP8X4),
-                    rhs_scale=x_scales[:, tokens],
-                    start=(part == 0 and first),
-                    stop=(part == 1 and not first),
-                )
-
-        def pair_sum(a, h, n0):
+        def strip_sum(a, r0, r1, n0, n1):
             x_codes, x_scales = x_mx[a]
             half = n0 // HALF
-            cols = slice(n0 - half * HALF, n0 - half * HALF + QUARTER)
-            sums[a, h, n0, 2] = next_bank()
-            for i in range(2):
-                r = 2 * h + i
-                for part in range(2):
+            cols = slice(n0 - half * HALF, n1 - half * HALF)
+            bank = next_strip_bank()
+            sums[a, r0, n0] = bank
+            width = n1 - n0
+            for r in range(r0, r1):
+                for part in ("hi", "lo"):
+                    codes, scales = w_mx[part, half]
                     nc.tensor.matmul_mx(
-                        out=sums[a, h, n0, 2][:].rearrange("p i n -> p (i n)")[:, i * QUARTER : (i + 1) * QUARTER],
+                        out=bank[:, (r - r0) * width : (r - r0 + 1) * width],
                         lhsT=x_codes[:, r * P : (r + 1) * P].bitcast(FP8X4),
                         lhsT_scale=x_scales[:, r * P : (r + 1) * P],
-                        rhs=w_codes[part, half][:, cols].bitcast(FP8X4),
-                        rhs_scale=w_scales[part, half][:, cols],
-                        start=(part == 0),
-                        stop=(part == 1),
+                        rhs=codes[:, cols].bitcast(FP8X4),
+                        rhs_scale=scales[:, cols],
+                        start=(part == "hi"),
+                        stop=(part == "lo"),
                     )
 
-        def pair_out(a, h, n0):
-            mid = keep.tile([P, PACK, P], F32, name="mid", bufs=MID_BUFS)
-            pair = mid[:].rearrange("p (i c) n -> p i (c n)", i=2)
+        def strip_add(a, r0, r1, n0, n1):
             nc.vector.tensor_tensor(
-                out=pair,
-                in0=sums[a, h, n0, 2][:].rearrange("p (i c) n -> p i (c n)", i=2),
-                in1=bias_rows[:, n0 : n0 + QUARTER].unsqueeze(1).to_broadcast([P, 2, QUARTER]),
-                op=ALU.add,
-            )
-            nc.scalar.activation(
-                out=result_of(a)[:, 2 * h : 2 * h + 2, n0 : n0 + QUARTER], in_=pair, func=SILU, bias=zero[:, 1:2]
-            )
-
-        def cm_silu(a, nt):
-            mids[a, nt] = keep.tile([P, PACK, P], F32, name="mid", bufs=MID_BUFS)
-            nc.scalar.activation(out=mids[a, nt][:], in_=sums[a, nt][:], func=SILU, bias=bias_cols[:, nt : nt + 1])
-
-        def turn(a, nt):
-            turned[a, nt] = next_bank()
-            for r in range(PACK):
-                nc.tensor.transpose(turned[a, nt][:, r, :], mids[a, nt][:, r, :], ident[:])
-
-        def copy_out(a, nt, copy):
-            copy(out=result_of(a)[:, :, nt * P : (nt + 1) * P], in_=turned[a, nt][:])
-
-        def cm_in(a, tiles):
-            for nt in tiles:
-                cm_sum(a, nt)
-                cm_silu(a, nt)
-
-        def cm_out(a, tiles, copy):
-            for nt in tiles:
-                turn(a, nt)
-                copy_out(a, nt, copy)
-
-        def tm_sum(a, r, half, parts=(0, 1)):
-            x_codes, x_scales = x_mx[a]
-            if 0 in parts:
-                sums[a, r, half] = next_bank()
-            for part in parts:
-                nc.tensor.matmul_mx(
-                    out=sums[a, r, half][:].rearrange("p i n -> p (i n)"),
-                    lhsT=x_codes[:, r * P : (r + 1) * P].bitcast(FP8X4),
-                    lhsT_scale=x_scales[:, r * P : (r + 1) * P],
-                    rhs=w_codes[part, half][:].bitcast(FP8X4),
-                    rhs_scale=w_scales[part, half][:],
-                    start=(part == 0),
-                    stop=(part == 1),
-                )
-
-        def tm_add(a, r, half):
-            mids[a, r, half] = keep.tile([P, PACK, P], F32, name="mid", bufs=MID_BUFS)
-            nc.vector.tensor_tensor(
-                out=mids[a, r, half][:].rearrange("p i n -> p (i n)"),
-                in0=sums[a, r, half][:].rearrange("p i n -> p (i n)"),
-                in1=bias_rows[:, half * HALF : (half + 1) * HALF],
+                out=result_of(a)[:, r0:r1, n0:n1],
+                in0=sums[a, r0, n0][:, 0 : (r1 - r0) * (n1 - n0)].rearrange("p (r n) -> p r n", r=r1 - r0),
+                in1=bias_rows[:, n0:n1].unsqueeze(1).to_broadcast([P, r1 - r0, n1 - n0]),
                 op=ALU.add,
             )
 
-        def tm_silu(a, r, half):
-            nc.scalar.activation(
-                out=result_of(a)[:, r, half * HALF : (half + 1) * HALF],
-                in_=mids[a, r, half][:].rearrange("p i n -> p (i n)"),
-                func=SILU,
-                bias=zero[:, 1:2],
-            )
+        def strip_silu(a, r0, r1, n0, n1):
+            strip = result_of(a)[:, r0:r1, n0:n1]
+            nc.scalar.activation(out=strip, in_=strip, func=SILU, bias=zero[:, 1:2])
 
-        def rounded_tile(a, n0, n1, name=None):
-            rounded[a, n0, n1] = keep.tile([P, n1 - n0, PACK], BF16, name=name or "rounded%d_%d" % (a, n0), align_bytes=64)
-
-        def rounded_of(a, n0, n1):
-            for (ra, r0, r1), tile in rounded.items():
-                if ra == a and r0 <= n0 and n1 <= r1:
-                    return tile[:, n0 - r0 : n1 - r0, :]
-
-        def out_cast(a, n0, n1, copy, run=RUN):
-            copy(
-                out=rounded_of(a, n0, n1).rearrange("p (c i) r -> p c r i", i=run),
-                in_=result_of(a)[:, :, n0:n1].rearrange("p r (c i) -> p c r i", i=run),
-            )
-
-        def out_cast_gpsimd(a, n0, n1):
-            nc.gpsimd.tensor_scalar(
-                out=rounded_of(a, n0, n1),
-                in0=result_of(a)[:, :, n0:n1].rearrange("p r n -> p n r"),
-                scalar1=1.0,
-                scalar2=-0.0,
-                op0=ALU.mult,
-                op1=ALU.add,
-            )
+        def out_round(a, n0, n1, copy, run=RUN):
+            copy(out=in_runs(staged_cols("out%d" % a, n0, n1), run), in_=rows_in_runs(result_of(a)[:, :, n0:n1], run))
 
         def out_quantize(a, n0, n1):
             nc.vector.quantize_mx(
                 out=out_codes[:, a, n0:n1].bitcast(FP8X4),
                 scales=scale_plane(a)[:, n0:n1],
-                in_=rounded_of(a, n0, n1).rearrange("p n r -> p (n r)"),
+                in_=staged_cols("out%d" % a, n0, n1).rearrange("p n r -> p (n r)"),
             )
 
-        def store_result(a, n0, n1, r0=0, r1=PACK):
+        def store_result(a, r0, r1, n0, n1):
             rows = out_0[a * CHUNK : (a + 1) * CHUNK, n0:n1].rearrange("(p r) n -> p r n", r=PACK)
             nc.sync.dma_start(out=rows[:, r0:r1, :], in_=result_of(a)[:, r0:r1, n0:n1])
 
@@ -279,163 +197,213 @@ def tile_mix_hilo_tm_pl_silu_kernel(tc, w, x, b, out_0, out_1, out_2):
             words = out_1[a].rearrange("p n i -> p (n i)").bitcast(I32)
             nc.sync.dma_start(out=words[:, n0:n1], in_=out_codes[:, a, n0:n1].bitcast(I32))
 
-        def store_scales(a0, a1, n0, n1, queues):
+        def store_scales(a0, a1, queue):
             for r in range(4):
-                rows = out_2[a0:a1, r:16:4, n0:n1].rearrange("a q n -> q a n").bitcast(I32)
-                queues[r].dma_start(out=rows, in_=out_scales[a0][r:P:32, :, n0:n1].bitcast(I32))
+                rows = out_2[a0:a1, r:16:4, :].rearrange("a q n -> q a n").bitcast(I32)
+                queue.dma_start(out=rows, in_=out_scales[a0][r:P:32, :, :].bitcast(I32))
 
         out_codes = keep.tile([P, CHUNKS, M], U32, name="out_codes", align_bytes=256)
-        out_scales = {
-            0: keep.tile([P, 1, M], U8, name="out_scales0", align_bytes=256),
-            1: keep.tile([P, 2, M], U8, name="out_scales1", align_bytes=256),
-        }
+        out_scales = {a0: keep.tile([P, a1 - a0, M], U8, name="out_scales%d" % a0, align_bytes=256) for a0, a1 in SCALE_GROUPS}
 
         def scale_plane(a):
-            return out_scales[0][:, 0, :] if a == 0 else out_scales[1][:, a - 1, :]
+            for a0, a1 in SCALE_GROUPS:
+                if a0 <= a < a1:
+                    return out_scales[a0][:, a - a0, :]
 
         ident = keep.tile([P, P], F32, name="ident")
         b_dealt = keep.tile([P, TILES], F32, name="b_dealt")
-        bias_cols = keep.tile([P, TILES], F32, name="bias_cols")
         bias_rows = keep.tile([P, M], F32, name="bias_rows")
         zero = keep.tile([P, 2], F32, name="zero")
 
-        def bias_spread(g):
+        def bias_spread(g, copy):
             bank = next_bank()
             for i in range(PACK):
                 c = g * PACK + i
-                nc.tensor.transpose(bank[:, i, :], b_dealt[:, c : c + 1].to_broadcast([P, P]), ident[:])
-            nc.scalar.copy(
+                nc.tensor.transpose(bank[:, i * P : (i + 1) * P], b_dealt[:, c : c + 1].to_broadcast([P, P]), ident[:])
+            copy(
                 out=bias_rows[:].rearrange("p (m c) -> p m c", c=TILES)[:, :, g * PACK : (g + 1) * PACK],
-                in_=bank[:].rearrange("p i m -> p m i"),
+                in_=bank[:].rearrange("p (i m) -> p m i", i=PACK),
             )
 
-        def bias_columns(n0, n1):
-            bank = next_bank()
-            for nt in range(n0, n1):
-                nc.tensor.transpose(bank[:, nt - n0, :], bias_rows[:, nt * P : (nt + 1) * P], ident[:])
-            nc.scalar.copy(out=bias_cols[:, n0:n1], in_=bank[:, 0 : n1 - n0, 0])
+        bias_cols = keep.tile([P, HALF // P], F32, name="bias_cols")
+        mids, turned = {}, {}
 
+        def bias_columns():
+            bank = next_bank()
+            for nt in range(HALF // P):
+                nc.tensor.transpose(bank[:, nt * P : (nt + 1) * P], bias_rows[:, nt * P : (nt + 1) * P], ident[:])
+            nc.scalar.copy(out=bias_cols[:], in_=bank[:].rearrange("p (i m) -> p i m", m=P)[:, :, 0])
+
+        def panel_sum(a, nt, r0=0, r1=PACK):
+            x_codes, x_scales = x_mx[a]
+            if r0 == 0:
+                sums["panel", a, nt] = next_bank()
+            tokens = slice(r0 * P, r1 * P)
+            half = nt * P // HALF
+            cols = slice(nt * P - half * HALF, (nt + 1) * P - half * HALF)
+            for part in ("hi", "lo"):
+                codes, scales = w_mx[part, half]
+                nc.tensor.matmul_mx(
+                    out=sums["panel", a, nt][:, tokens],
+                    lhsT=codes[:, cols].bitcast(FP8X4),
+                    lhsT_scale=scales[:, cols],
+                    rhs=x_codes[:, tokens].bitcast(FP8X4),
+                    rhs_scale=x_scales[:, tokens],
+                    start=(part == "hi" and r0 == 0),
+                    stop=(part == "lo" and r1 == PACK),
+                )
+
+        def panel_silu(a, nt):
+            mids[a, nt] = keep.tile([P, CHUNK], F32, name="mid", bufs=MID_BUFS)
+            nc.scalar.activation(out=mids[a, nt][:], in_=sums["panel", a, nt][:], func=SILU, bias=bias_cols[:, nt : nt + 1])
+
+        def panel_turn(a, nt):
+            turned[a, nt] = next_bank()
+            for r in range(PACK):
+                nc.tensor.transpose(turned[a, nt][:, r * P : (r + 1) * P], mids[a, nt][:, r * P : (r + 1) * P], ident[:])
+
+        def panel_out(a, nt, copy):
+            copy(out=result_of(a)[:, :, nt * P : (nt + 1) * P], in_=turned[a, nt][:].rearrange("p (r n) -> p r n", r=PACK))
+
+        nc.sync.dma_start(out=b_dealt[:], in_=b.rearrange("(p c) -> p c", c=TILES))
         nc.gpsimd.memset(zero[:, 0:1], 0.0)
         nc.scalar.activation(out=zero[:, 1:2], in_=zero[:, 0:1], func=SILU)
         make_identity(nc, ident[:])
 
         load("w", w_rows, w_raw, 0, 256)
-        nc.sync.dma_start(out=b_dealt[:], in_=b.rearrange("(p c) -> p c", c=TILES))
-        load("x", x_rows, x_raw, 0, 512)
+        load("x", x_rows, x_raw, 0, 256)
+        load("x", x_rows, x_raw, 256, 512)
         load("w", w_rows, w_raw, 256, 512)
         load("w", w_rows, w_raw, 512, 768)
         load("x", x_rows, x_raw, 512, 1024)
         load("w", w_rows, w_raw, 768, 1024)
         load("x", x_rows, x_raw, 1024, 1536)
 
+        for q in range(4):
+            stage("hi", q * QUARTER, (q + 1) * QUARTER)
+            stage("lo", q * QUARTER, (q + 1) * QUARTER)
+        for a in range(CHUNKS):
+            for h in range(2):
+                stage("x%d" % a, 2 * h * P, (2 * h + 2) * P)
+
+        def strip_out(a, r0, r1, n0, n1):
+            strip_add(a, r0, r1, n0, n1)
+            strip_silu(a, r0, r1, n0, n1)
+
+        bias_spread(0, on_scalar)
+        bias_spread(1, on_scalar)
         w_top(0, 128, on_vector)
         w_top(128, 256, on_vector)
-        bias_spread(0)
-        bias_spread(1)
-        x_cast_slots(0, 1, on_scalar)
-        bias_columns(0, 4)
-        w_top(384, 512, on_scalar)
+        x_round(0, 0, on_scalar, 0, 64)
+        x_round(0, 1, on_scalar, 0, 64)
+        bias_columns()
+        x_round(0, 0, on_scalar, 64, P)
         w_mask(0, 128)
         w_mask(128, 256)
-        w_low(0, 128)
-        w_low(128, 256)
-        w_quantize(0, 0, 256)
-        x_cast_slots(0, 0, on_vector)
-        w_quantize(1, 0, 256)
+        w_low(0, 128, nc.vector)
+        w_low(128, 256, nc.vector)
+        w_quantize("hi", 0, 256)
+        x_round(0, 1, on_vector, 64, P)
+        w_quantize("lo", 0, 256)
+        w_top(384, 512, on_scalar)
+        w_top(512, 768, on_scalar)
+        x_quantize(0, 0, 2)
+        panel_sum(0, 0, 0, 2)
         w_top(256, 384, on_vector)
-        x_quantize(0, 0)
-        cm_sum_slots(0, 0, 0)
-        cm_sum_slots(0, 1, 0)
+        x_quantize(0, 2, 4)
+        panel_sum(0, 0, 2, 4)
+        panel_sum(0, 1)
         w_mask(256, 384)
         w_mask(384, 512)
-        x_quantize(0, 1)
-        w_low(256, 384)
-        w_low(384, 512)
-        w_top(512, 768, on_scalar)
-        for nt in (0, 1):
-            cm_sum_slots(0, nt, 1)
-            cm_silu(0, nt)
-        x_cast_slots(1, 1, on_scalar, 0, 48)
-        w_quantize(0, 256, 512)
-        w_quantize(1, 256, 512)
+        w_low(256, 384, nc.vector)
+        w_low(384, 512, nc.vector)
+        w_quantize("hi", 256, 512)
         w_mask(512, 768)
-        x_cast_slots(1, 0, on_vector)
-        x_cast_slots(1, 1, on_vector, 48, P)
-        x_quantize(1, 0)
-        x_quantize(1, 1)
+        w_quantize("lo", 256, 512)
+        x_round(1, 0, on_vector)
+        x_round(1, 1, on_vector)
+        x_quantize(1, 0, 2)
+        x_quantize(1, 2, 4)
         w_top(768, 1024, on_vector)
-        w_low(512, 768)
+        w_low(512, 768, nc.vector)
         w_mask(768, 1024)
-        w_quantize(0, 512, 768)
-        w_quantize(1, 512, 768)
-        w_low(768, 1024)
-        w_quantize(0, 768, 1024)
-        x_cast_slots(2, 0, on_vector)
-        w_quantize(1, 768, 1024)
+        w_quantize("hi", 512, 768)
+        w_quantize("lo", 512, 768)
+        w_low(768, 1024, nc.vector)
+        w_quantize("hi", 768, 1024)
+        x_round(2, 0, on_vector)
+        w_quantize("lo", 768, 1024)
 
-        rounded_tile(0, 0, 256)
-        order = [(a, nt) for a in (0, 1) for nt in range(4)]
-        for i, (a, nt) in enumerate(order):
-            if i == 2:
-                cm_sum_slots(1, 0, 0)
-                cm_sum_slots(1, 0, 1)
-                cm_silu(1, 0)
-            elif i + 2 < len(order):
-                cm_in(order[i + 2][0], (order[i + 2][1],))
-            if i == 3:
-                x_cast_slots(2, 1, on_scalar, 0, 32)
-            if i == 7:
-                for r in range(2):
-                    tm_sum(0, r, 1, (0,))
-            cm_out(a, (nt,), on_scalar)
+        panels = [(0, nt) for nt in range(4)] + [(1, 0), (1, 1)]
+        strips = [(1, 0, 2, 256, 512), (1, 2, 4, 256, 512)]
+        strips += [(0, r, r + 2, n0, n0 + QUARTER) for n0 in (512, 768) for r in (0, 2)]
+        strips += [(1, r, r + 1, HALF, M) for r in range(PACK)]
+        strips += [(2, r, r + 1, half * HALF, (half + 1) * HALF) for r in range(PACK) for half in range(2)]
+        stage("out0", 0, G_START)
+        panel_silu(0, 0)
+        for i, (a, nt) in enumerate(panels):
+            if i + 1 < len(panels):
+                if i > 0:
+                    panel_sum(*panels[i + 1])
+                panel_silu(*panels[i + 1])
+            else:
+                out_round(0, 0, S_EARLY, on_scalar)
+            if i == len(panels) - 1:
+                strip_sum(*strips[2])
+            panel_turn(a, nt)
+            panel_out(a, nt, on_scalar)
+            if i == X2_AFTER:
+                x_round(2, 1, on_scalar)
+                strip_sum(*strips[0])
+                strip_sum(*strips[1])
             if nt % 2:
-                store_result(a, (nt - 1) * P, (nt + 1) * P)
-        x_cast_slots(2, 1, on_vector, 32, P)
-        x_quantize(2, 0)
-        x_quantize(2, 1)
-        out_cast(0, 0, 128, on_scalar, RUN)
+                store_result(a, 0, PACK, (nt - 1) * P, (nt + 1) * P)
+        x_quantize(2, 0, 2)
+        x_quantize(2, 2, 4)
 
-        def bank(a, r, half):
-            tm_sum(a, r, half, (1,) if (a, r, half) in sums else (0, 1))
-            tm_add(a, r, half)
-            tm_silu(a, r, half)
+        stage("out0", G_START, 512, "x2_0")
+        stage("out1", 0, 512)
+        stage("out0", 512, 1024)
+        stage("out1", 512, 1024)
+        stage("out2", 0, 512)
+        stage("out2", 512, 1024)
+        out_round(0, G_START, 512, on_gpsimd, 1)
+        for i, strip in enumerate(strips):
+            a, r0, r1, n0, n1 = strip
+            if (a, r0, n0) not in sums:
+                strip_sum(*strip)
+            strip_out(*strip)
+            if r1 - r0 == 2:
+                if r1 == PACK:
+                    store_result(a, 0, PACK, n0, n1)
+            elif a < 2 and r0 % 2:
+                store_result(a, r0 - 1, r1, HALF, M)
+            elif a == 2 and r1 == PACK:
+                store_result(2, r0, r1, n0, n1)
+            elif a == 2 and n0:
+                store_result(2, r0, r1, 0, M)
+            if i == 1:
+                out_round(1, 0, 512, on_gpsimd, 1)
+            if i == 5:
+                out_round(0, 512, 1024, on_gpsimd, 1)
+            if i == 9:
+                out_round(1, 512, G_END, on_gpsimd, 1)
 
-        rounded_tile(0, 256, 512, "x_dealt2_1")
-        rounded_tile(0, 512, 1024)
-        rounded_tile(1, 0, 512)
-        rounded_tile(1, 512, 1024)
-        rounded_tile(2, 0, 512)
-        rounded_tile(2, 512, 768)
-        rounded_tile(2, 768, 1024)
-        out_cast_gpsimd(0, 256, 512)
-        out_cast_gpsimd(1, 0, 512)
-        for a in (0, 1):
-            for r in range(PACK):
-                bank(a, r, 1)
-                if r % 2:
-                    store_result(a, HALF, M, r - 1, r + 1)
-        out_cast_gpsimd(0, 512, 1024)
-        out_cast_gpsimd(1, 512, 704)
-        for r in range(PACK):
-            for half in range(2):
-                bank(2, r, half)
-            store_result(2, 0, M, r, r + 1)
-        out_cast(2, 0, 512, on_scalar, RUN)
-        out_cast(2, 768, 1024, on_scalar, RUN)
-        out_cast(0, 128, 256, on_vector)
-        out_quantize(0, 256, 512)
+        out_round(2, 0, 512, on_scalar)
+        out_round(2, S_LAST, 1024, on_scalar)
+        out_quantize(0, G_START, 512)
         out_quantize(0, 512, 1024)
-        out_quantize(0, 0, 256)
-        store_scales(0, 1, 0, M, [nc.sync] * 4)
+        out_quantize(0, 0, G_START)
         store_codes(0, 0, M)
-        out_cast(1, 704, 1024, on_vector)
+        store_scales(0, 1, nc.sync)
+        out_round(1, G_END, 1024, on_vector)
         out_quantize(1, 0, 512)
         out_quantize(1, 512, 1024)
         store_codes(1, 0, M)
-        out_cast(2, 512, 768, on_vector)
+        out_round(2, 512, S_LAST, on_vector)
         out_quantize(2, 0, 512)
-        store_codes(2, 0, 512)
         out_quantize(2, 512, 768)
+        store_codes(2, 0, 768)
         out_quantize(2, 768, 1024)
-        store_codes(2, 512, 1024)
-        store_scales(1, 3, 0, M, [nc.sync] * 4)
+        store_codes(2, 768, 1024)
+        store_scales(1, 3, nc.sync)

@@ -26,12 +26,13 @@ RUN = 4
 BANKS = 8
 MID_BUFS = 6
 SCALE_GROUPS = ((0, 1), (1, 3))
+PANEL_BANKS = 4
+PANELS = 4
 S_EARLY = 128
-G_START = 128
 G_END = 768
 S_LAST = 768
-X2_AFTER = 2
-PANEL_BANKS = 4
+S_X2 = 128
+S_X1 = 32
 HI_MASK_PAIR = 0xFFF0FFF0 - (1 << 32)
 
 
@@ -221,18 +222,18 @@ def tile_mix_hilo_tm_pl_silu_kernel(tc, w, x, b, out_0, out_1, out_2):
                 c = g * PACK + i
                 nc.tensor.transpose(bank[:, i * P : (i + 1) * P], b_dealt[:, c : c + 1].to_broadcast([P, P]), ident[:])
             copy(
-                out=bias_rows[:].rearrange("p (m c) -> p m c", c=TILES)[:, :, g * PACK : (g + 1) * PACK],
+                out=bias_rows[:, g * HALF : (g + 1) * HALF].rearrange("p (m c) -> p m c", c=PACK),
                 in_=bank[:].rearrange("p (i m) -> p m i", i=PACK),
             )
 
-        bias_cols = keep.tile([P, HALF // P], F32, name="bias_cols")
+        bias_cols = keep.tile([P, PANELS], F32, name="bias_cols")
         mids, turned = {}, {}
 
-        def bias_columns():
+        def bias_columns(t0, t1):
             bank = next_bank()
-            for nt in range(HALF // P):
-                nc.tensor.transpose(bank[:, nt * P : (nt + 1) * P], bias_rows[:, nt * P : (nt + 1) * P], ident[:])
-            nc.scalar.copy(out=bias_cols[:], in_=bank[:].rearrange("p (i m) -> p i m", m=P)[:, :, 0])
+            for nt in range(t0, t1):
+                nc.tensor.transpose(bank[:, (nt - t0) * P : (nt - t0 + 1) * P], bias_rows[:, nt * P : (nt + 1) * P], ident[:])
+            nc.scalar.copy(out=bias_cols[:, t0:t1], in_=bank[:].rearrange("p (i m) -> p i m", m=P)[:, 0 : t1 - t0, 0])
 
         def panel_sum(a, nt, r0=0, r1=PACK):
             x_codes, x_scales = x_mx[a]
@@ -265,12 +266,13 @@ def tile_mix_hilo_tm_pl_silu_kernel(tc, w, x, b, out_0, out_1, out_2):
         def panel_out(a, nt, copy):
             copy(out=result_of(a)[:, :, nt * P : (nt + 1) * P], in_=turned[a, nt][:].rearrange("p (r n) -> p r n", r=PACK))
 
-        nc.sync.dma_start(out=b_dealt[:], in_=b.rearrange("(p c) -> p c", c=TILES))
+        nc.scalar.dma_start(out=b_dealt[:].rearrange("p (g c) -> p g c", c=PACK), in_=b.rearrange("(g p c) -> p g c", p=P, c=PACK))
         nc.gpsimd.memset(zero[:, 0:1], 0.0)
         nc.scalar.activation(out=zero[:, 1:2], in_=zero[:, 0:1], func=SILU)
         make_identity(nc, ident[:])
 
-        load("w", w_rows, w_raw, 0, 256)
+        load("w", w_rows, w_raw, 0, 128)
+        load("w", w_rows, w_raw, 128, 256)
         load("x", x_rows, x_raw, 0, 256)
         load("x", x_rows, x_raw, 256, 512)
         load("w", w_rows, w_raw, 256, 512)
@@ -279,33 +281,35 @@ def tile_mix_hilo_tm_pl_silu_kernel(tc, w, x, b, out_0, out_1, out_2):
         load("w", w_rows, w_raw, 768, 1024)
         load("x", x_rows, x_raw, 1024, 1536)
 
-        for q in range(4):
-            stage("hi", q * QUARTER, (q + 1) * QUARTER)
-            stage("lo", q * QUARTER, (q + 1) * QUARTER)
-        for a in range(CHUNKS):
-            for h in range(2):
-                stage("x%d" % a, 2 * h * P, (2 * h + 2) * P)
+        for part in ("hi", "lo"):
+            stage(part, 0, 256)
+            stage(part, 256, 512)
+            stage(part, 512, 1024)
+        stage("x0", 0, 2 * P)
+        stage("x0", 2 * P, 4 * P)
+        stage("x1", 0, CHUNK)
+        stage("x2", 0, CHUNK)
 
         def strip_out(a, r0, r1, n0, n1):
             strip_add(a, r0, r1, n0, n1)
             strip_silu(a, r0, r1, n0, n1)
 
         bias_spread(0, on_scalar)
-        bias_spread(1, on_scalar)
         w_top(0, 128, on_vector)
         w_top(128, 256, on_vector)
         x_round(0, 0, on_scalar, 0, 64)
         x_round(0, 1, on_scalar, 0, 64)
-        bias_columns()
-        x_round(0, 0, on_scalar, 64, P)
+        x_round(0, 1, on_scalar, 64, P)
+        bias_columns(0, 4)
         w_mask(0, 128)
         w_mask(128, 256)
         w_low(0, 128, nc.vector)
         w_low(128, 256, nc.vector)
         w_quantize("hi", 0, 256)
-        x_round(0, 1, on_vector, 64, P)
+        x_round(0, 0, on_vector, 64, P)
         w_quantize("lo", 0, 256)
         w_top(384, 512, on_scalar)
+        bias_spread(1, on_scalar)
         w_top(512, 768, on_scalar)
         x_quantize(0, 0, 2)
         panel_sum(0, 0, 0, 2)
@@ -320,70 +324,71 @@ def tile_mix_hilo_tm_pl_silu_kernel(tc, w, x, b, out_0, out_1, out_2):
         w_quantize("hi", 256, 512)
         w_mask(512, 768)
         w_quantize("lo", 256, 512)
-        x_round(1, 0, on_vector)
-        x_round(1, 1, on_vector)
-        x_quantize(1, 0, 2)
-        x_quantize(1, 2, 4)
-        w_top(768, 1024, on_vector)
-        w_low(512, 768, nc.vector)
-        w_mask(768, 1024)
-        w_quantize("hi", 512, 768)
-        w_quantize("lo", 512, 768)
-        w_low(768, 1024, nc.vector)
-        w_quantize("hi", 768, 1024)
-        x_round(2, 0, on_vector)
-        w_quantize("lo", 768, 1024)
+        w_low(512, 640, nc.vector)
+        panel_silu(0, 0)
 
         panels = [(0, nt) for nt in range(4)] + [(1, 0), (1, 1)]
         strips = [(1, 0, 2, 256, 512), (1, 2, 4, 256, 512)]
-        strips += [(0, r, r + 2, n0, n0 + QUARTER) for n0 in (512, 768) for r in (0, 2)]
-        strips += [(1, r, r + 1, HALF, M) for r in range(PACK)]
+        strips += [(a, r, r + 1, HALF, M) for a in range(2) for r in range(PACK)]
         strips += [(2, r, r + 1, half * HALF, (half + 1) * HALF) for r in range(PACK) for half in range(2)]
-        stage("out0", 0, G_START)
-        panel_silu(0, 0)
-        for i, (a, nt) in enumerate(panels):
+
+        def panel_step(i):
+            a, nt = panels[i]
             if i + 1 < len(panels):
                 if i > 0:
                     panel_sum(*panels[i + 1])
                 panel_silu(*panels[i + 1])
             else:
                 out_round(0, 0, S_EARLY, on_scalar)
-            if i == len(panels) - 1:
-                strip_sum(*strips[2])
             panel_turn(a, nt)
             panel_out(a, nt, on_scalar)
-            if i == X2_AFTER:
-                x_round(2, 1, on_scalar)
-                strip_sum(*strips[0])
-                strip_sum(*strips[1])
             if nt % 2:
                 store_result(a, 0, PACK, (nt - 1) * P, (nt + 1) * P)
-        x_quantize(2, 0, 2)
-        x_quantize(2, 2, 4)
 
-        stage("out0", G_START, 512, "x2_0")
-        stage("out1", 0, 512)
-        stage("out0", 512, 1024)
-        stage("out1", 512, 1024)
+        panel_step(0)
+        if S_X1:
+            x_round(1, 1, on_scalar, 0, S_X1)
+        x_round(1, 0, on_vector)
+        x_round(1, 1, on_vector, S_X1, P)
+        w_top(768, 1024, on_vector)
+        x_quantize(1, 0, PACK)
+        w_low(640, 768, nc.vector)
+        w_mask(768, 1024)
+        x_round(2, 0, on_vector)
+        w_low(768, 1024, nc.vector)
+        w_quantize("hi", 512, 1024)
+        if S_X2 < P:
+            x_round(2, 1, on_vector, S_X2, P)
+        w_quantize("lo", 512, 1024)
+        panel_step(1)
+        panel_step(2)
+        x_round(2, 1, on_scalar, 0, S_X2)
+        x_quantize(2, 0, PACK)
+        panel_step(3)
+        strip_sum(*strips[0])
+        panel_step(4)
+        strip_sum(*strips[1])
+        stage("out0", 0, M, "lo_512")
+        panel_step(5)
+
+        stage("out1", 0, M)
         stage("out2", 0, 512)
         stage("out2", 512, 1024)
-        out_round(0, G_START, 512, on_gpsimd, 1)
+        out_round(0, S_EARLY, 512, on_gpsimd, 1)
         for i, strip in enumerate(strips):
             a, r0, r1, n0, n1 = strip
             if (a, r0, n0) not in sums:
                 strip_sum(*strip)
             strip_out(*strip)
-            if r1 - r0 == 2:
-                if r1 == PACK:
-                    store_result(a, 0, PACK, n0, n1)
+            if i == 1:
+                store_result(1, 0, PACK, 256, 512)
+                out_round(1, 0, 512, on_gpsimd, 1)
             elif a < 2 and r0 % 2:
-                store_result(a, r0 - 1, r1, HALF, M)
+                store_result(a, r0 - 1, r1, n0, n1)
             elif a == 2 and r1 == PACK:
                 store_result(2, r0, r1, n0, n1)
             elif a == 2 and n0:
                 store_result(2, r0, r1, 0, M)
-            if i == 1:
-                out_round(1, 0, 512, on_gpsimd, 1)
             if i == 5:
                 out_round(0, 512, 1024, on_gpsimd, 1)
             if i == 9:
@@ -391,14 +396,11 @@ def tile_mix_hilo_tm_pl_silu_kernel(tc, w, x, b, out_0, out_1, out_2):
 
         out_round(2, 0, 512, on_scalar)
         out_round(2, S_LAST, 1024, on_scalar)
-        out_quantize(0, G_START, 512)
-        out_quantize(0, 512, 1024)
-        out_quantize(0, 0, G_START)
+        out_round(1, G_END, 1024, on_vector)
+        out_quantize(0, 0, M)
         store_codes(0, 0, M)
         store_scales(0, 1, nc.sync)
-        out_round(1, G_END, 1024, on_vector)
-        out_quantize(1, 0, 512)
-        out_quantize(1, 512, 1024)
+        out_quantize(1, 0, M)
         store_codes(1, 0, M)
         out_round(2, 512, S_LAST, on_vector)
         out_quantize(2, 0, 512)

@@ -22,17 +22,17 @@ CHUNKS = T // CHUNK
 HALF = M // 2
 QUARTER = M // 4
 TILES = M // P
-RUN = 4
+RUN = 2
 BANKS = 8
 MID_BUFS = 6
 SCALE_GROUPS = ((0, 1), (1, 3))
 PANEL_BANKS = 4
 PANELS = 4
 S_EARLY = 128
-G_END = 768
+G_END = 704
 S_LAST = 768
 S_X2 = 128
-S_X1 = 32
+S_X1 = 64
 HI_MASK_PAIR = 0xFFF0FFF0 - (1 << 32)
 
 
@@ -338,7 +338,9 @@ def tile_mix_hilo_tm_pl_silu_kernel(tc, w, x, b, out_0, out_1, out_2):
                 if i > 0:
                     panel_sum(*panels[i + 1])
                 panel_silu(*panels[i + 1])
-            else:
+                if i == 0:
+                    x_round(1, 1, on_scalar, 0, S_X1)
+            elif S_EARLY:
                 out_round(0, 0, S_EARLY, on_scalar)
             panel_turn(a, nt)
             panel_out(a, nt, on_scalar)
@@ -346,10 +348,9 @@ def tile_mix_hilo_tm_pl_silu_kernel(tc, w, x, b, out_0, out_1, out_2):
                 store_result(a, 0, PACK, (nt - 1) * P, (nt + 1) * P)
 
         panel_step(0)
-        if S_X1:
-            x_round(1, 1, on_scalar, 0, S_X1)
         x_round(1, 0, on_vector)
-        x_round(1, 1, on_vector, S_X1, P)
+        if S_X1 < P:
+            x_round(1, 1, on_vector, S_X1, P)
         w_top(768, 1024, on_vector)
         x_quantize(1, 0, PACK)
         w_low(640, 768, nc.vector)

@@ -27,12 +27,10 @@ BANKS = 8
 MID_BUFS = 6
 SCALE_GROUPS = ((0, 1), (1, 3))
 PANEL_BANKS = 4
-PANELS = 4
-S_EARLY = 128
-G_END = 704
+PANELS = 6
+G_END = 544
 S_LAST = 768
-S_X2 = 128
-S_X1 = 64
+S_W3 = 832
 HI_MASK_PAIR = 0xFFF0FFF0 - (1 << 32)
 
 
@@ -277,14 +275,13 @@ def tile_mix_hilo_tm_pl_silu_kernel(tc, w, x, b, out_0, out_1, out_2):
         load("x", x_rows, x_raw, 256, 512)
         load("w", w_rows, w_raw, 256, 512)
         load("w", w_rows, w_raw, 512, 768)
-        load("x", x_rows, x_raw, 512, 1024)
         load("w", w_rows, w_raw, 768, 1024)
+        load("x", x_rows, x_raw, 512, 1024)
         load("x", x_rows, x_raw, 1024, 1536)
 
         for part in ("hi", "lo"):
-            stage(part, 0, 256)
-            stage(part, 256, 512)
-            stage(part, 512, 1024)
+            for q in range(4):
+                stage(part, q * QUARTER, (q + 1) * QUARTER)
         stage("x0", 0, 2 * P)
         stage("x0", 2 * P, 4 * P)
         stage("x1", 0, CHUNK)
@@ -293,6 +290,16 @@ def tile_mix_hilo_tm_pl_silu_kernel(tc, w, x, b, out_0, out_1, out_2):
         def strip_out(a, r0, r1, n0, n1):
             strip_add(a, r0, r1, n0, n1)
             strip_silu(a, r0, r1, n0, n1)
+
+        def panel_in(nt):
+            panel_sum(0, nt)
+            panel_silu(0, nt)
+
+        def panel_back(nt):
+            panel_turn(0, nt)
+            panel_out(0, nt, on_scalar)
+            if nt % 2:
+                store_result(0, 0, PACK, (nt - 1) * P, (nt + 1) * P)
 
         bias_spread(0, on_scalar)
         w_top(0, 128, on_vector)
@@ -324,89 +331,75 @@ def tile_mix_hilo_tm_pl_silu_kernel(tc, w, x, b, out_0, out_1, out_2):
         w_quantize("hi", 256, 512)
         w_mask(512, 768)
         w_quantize("lo", 256, 512)
-        w_low(512, 640, nc.vector)
         panel_silu(0, 0)
-
-        panels = [(0, nt) for nt in range(4)] + [(1, 0), (1, 1)]
-        strips = [(1, 0, 2, 256, 512), (1, 2, 4, 256, 512)]
-        strips += [(a, r, r + 1, HALF, M) for a in range(2) for r in range(PACK)]
-        strips += [(2, r, r + 1, half * HALF, (half + 1) * HALF) for r in range(PACK) for half in range(2)]
-
-        def panel_step(i):
-            a, nt = panels[i]
-            if i + 1 < len(panels):
-                if i > 0:
-                    panel_sum(*panels[i + 1])
-                panel_silu(*panels[i + 1])
-                if i == 0:
-                    x_round(1, 1, on_scalar, 0, S_X1)
-            elif S_EARLY:
-                out_round(0, 0, S_EARLY, on_scalar)
-            panel_turn(a, nt)
-            panel_out(a, nt, on_scalar)
-            if nt % 2:
-                store_result(a, 0, PACK, (nt - 1) * P, (nt + 1) * P)
-
-        panel_step(0)
-        x_round(1, 0, on_vector)
-        if S_X1 < P:
-            x_round(1, 1, on_vector, S_X1, P)
-        w_top(768, 1024, on_vector)
-        x_quantize(1, 0, PACK)
-        w_low(640, 768, nc.vector)
+        panel_silu(0, 1)
+        bias_columns(4, PANELS)
+        w_top(S_W3, 1024, on_scalar)
+        if S_W3 > 768:
+            w_top(768, S_W3, on_vector)
+        w_low(512, 768, nc.vector)
+        w_quantize("hi", 512, 768)
         w_mask(768, 1024)
-        x_round(2, 0, on_vector)
+        w_quantize("lo", 512, 768)
         w_low(768, 1024, nc.vector)
-        w_quantize("hi", 512, 1024)
-        if S_X2 < P:
-            x_round(2, 1, on_vector, S_X2, P)
-        w_quantize("lo", 512, 1024)
-        panel_step(1)
-        panel_step(2)
-        x_round(2, 1, on_scalar, 0, S_X2)
-        x_quantize(2, 0, PACK)
-        panel_step(3)
-        strip_sum(*strips[0])
-        panel_step(4)
-        strip_sum(*strips[1])
-        stage("out0", 0, M, "lo_512")
-        panel_step(5)
+        w_quantize("hi", 768, 1024)
+        x_round(1, 0, on_vector)
+        w_quantize("lo", 768, 1024)
+        x_round(1, 1, on_vector)
+        x_round(2, 0, on_vector)
+        x_quantize(1, 0, PACK)
 
+        strips = [(0, 0, 2, 768, M), (0, 2, 4, 768, M)]
+        strips += [(a, r, r + 1, half * HALF, (half + 1) * HALF) for a in (1, 2) for r in range(PACK) for half in range(2)]
+        panel_back(0)
+        panel_in(2)
+        panel_back(1)
+        panel_in(3)
+        panel_back(2)
+        panel_sum(0, 4)
+        panel_sum(0, 5)
+        x_round(2, 1, on_scalar)
+        x_quantize(2, 0, PACK)
+        panel_silu(0, 4)
+        panel_silu(0, 5)
+        panel_back(3)
+        strip_sum(*strips[0])
+        strip_sum(*strips[1])
+        panel_back(4)
+        panel_back(5)
+
+        stage("out0", 0, M, "x1_0")
         stage("out1", 0, M)
         stage("out2", 0, 512)
         stage("out2", 512, 1024)
-        out_round(0, S_EARLY, 512, on_gpsimd, 1)
+        out_round(0, 0, 512, on_gpsimd, 1)
         for i, strip in enumerate(strips):
             a, r0, r1, n0, n1 = strip
             if (a, r0, n0) not in sums:
                 strip_sum(*strip)
             strip_out(*strip)
             if i == 1:
-                store_result(1, 0, PACK, 256, 512)
-                out_round(1, 0, 512, on_gpsimd, 1)
-            elif a < 2 and r0 % 2:
-                store_result(a, r0 - 1, r1, n0, n1)
-            elif a == 2 and r1 == PACK:
-                store_result(2, r0, r1, n0, n1)
-            elif a == 2 and n0:
-                store_result(2, r0, r1, 0, M)
-            if i == 5:
-                out_round(0, 512, 1024, on_gpsimd, 1)
+                store_result(0, 0, PACK, 768, M)
+                out_round(0, 512, M, on_gpsimd, 1)
+            elif a and n0:
+                store_result(a, r0, r1, 0, M)
             if i == 9:
-                out_round(1, 512, G_END, on_gpsimd, 1)
+                out_round(1, 0, G_END, on_gpsimd, 1)
 
         out_round(2, 0, 512, on_scalar)
         out_round(2, S_LAST, 1024, on_scalar)
-        out_round(1, G_END, 1024, on_vector)
         out_quantize(0, 0, M)
         store_codes(0, 0, M)
         store_scales(0, 1, nc.sync)
-        out_quantize(1, 0, M)
+        out_round(1, G_END, 1024, on_vector)
+        out_quantize(1, 0, 512)
+        out_quantize(1, 512, M)
         store_codes(1, 0, M)
         out_round(2, 512, S_LAST, on_vector)
         out_quantize(2, 0, 512)
+        store_codes(2, 0, 512)
         out_quantize(2, 512, 768)
-        store_codes(2, 0, 768)
+        store_codes(2, 512, 768)
         out_quantize(2, 768, 1024)
         store_codes(2, 768, 1024)
         store_scales(1, 3, nc.sync)

from contextlib import ExitStack

import concourse.mybir as mybir
from concourse.masks import make_identity

K, M, T = 512, 1024, 1536
FLOPS = 2 * 2 * K * M * T

F32 = mybir.dt.float32
BF16 = mybir.dt.bfloat16
I32 = mybir.dt.int32
U32 = mybir.dt.uint32
U8 = mybir.dt.uint8
FP8X4 = mybir.dt.float8_e4m3fn_x4
ALU = mybir.AluOpType
SILU = mybir.ActivationFunctionType.Silu

P = 128
PACK = 4
CHUNK = P * PACK
CHUNKS = T // CHUNK
HALF = M // 2
QUARTER = M // 4
TILES = M // P
RUN = 2
BANKS = 8
MID_BUFS = 6
SCALE_GROUPS = ((0, 1), (1, 3))
PANEL_BANKS = 4
PANELS = 6
G_END = 544
S_LAST = 768
S_W3 = 832
HI_MASK_PAIR = 0xFFF0FFF0 - (1 << 32)


def tile_mix_hilo_tm_pl_silu_kernel(tc, w, x, b, out_0, out_1, out_2):
    nc = tc.nc
    on_vector = nc.vector.tensor_copy
    on_scalar = nc.scalar.copy

    def on_gpsimd(out, in_):
        nc.gpsimd.tensor_scalar(out=out, in0=in_, scalar1=1.0, scalar2=-0.0, op0=ALU.mult, op1=ALU.add)

    with ExitStack() as ctx:
        keep = ctx.enter_context(tc.tile_pool(name="keep", bufs=1))
        psum = ctx.enter_context(tc.psum_pool(name="psum", bufs=1))
        ctx.enter_context(tc.manual_schedule())

        w_rows = w.rearrange("(p j) n -> p j n", j=PACK)
        x_rows = x.rearrange("(p j) t -> p j t", j=PACK)
        w_raw, x_raw, staged, w_mx, x_mx, sums, results = {}, {}, {}, {}, {}, {}, {}
        banks_taken = []

        strip_banks = []

        def next_bank():
            index = len(banks_taken) % PANEL_BANKS
            banks_taken.append(index)
            return psum.tile([P, HALF], F32, name="bank%d" % index)

        def next_strip_bank():
            i = len(strip_banks)
            if i < BANKS - PANEL_BANKS:
                index = PANEL_BANKS + i
            elif i < BANKS:
                index = (len(banks_taken) + i - (BANKS - PANEL_BANKS)) % PANEL_BANKS
            else:
                index = strip_banks[i - BANKS]
            strip_banks.append(index)
            return psum.tile([P, HALF], F32, name="bank%d" % index)

        def load(name, rows, loaded, c0, c1):
            raw = keep.tile([P, PACK, c1 - c0], F32, name="%s_raw%d" % (name, c0), align_bytes=256)
            nc.sync.dma_start(out=raw[:], in_=rows[:, :, c0:c1])
            loaded[c0, c1] = raw

        def columns(loaded, c0, c1):
            for (l0, l1), raw in loaded.items():
                if l0 <= c0 and c1 <= l1:
                    return raw[:, :, c0 - l0 : c1 - l0]

        def stage(kind, c0, c1, buffer=None):
            staged[kind, c0, c1] = keep.tile([P, c1 - c0, PACK], BF16, name=buffer or "%s_%d" % (kind, c0), align_bytes=64)

        def staged_cols(kind, c0, c1):
            for (k, l0, l1), tile in staged.items():
                if k == kind and l0 <= c0 and c1 <= l1:
                    return tile[:, c0 - l0 : c1 - l0, :]

        def in_runs(view, run):
            return view.rearrange("p (c i) j -> p c j i", i=run) if run > 1 else view

        def rows_in_runs(view, run):
            return view.rearrange("p j (c i) -> p c j i", i=run) if run > 1 else view.rearrange("p j c -> p c j")

        def w_top(n0, n1, copy, run=RUN):
            upper = columns(w_raw, n0, n1).bitcast(BF16).rearrange("p j (n e) -> p j n e", e=2)[:, :, :, 1]
            copy(out=in_runs(staged_cols("hi", n0, n1), run), in_=rows_in_runs(upper, run))

        def w_mask(n0, n1):
            pairs = staged_cols("hi", n0, n1).rearrange("p n j -> p (n j)").bitcast(I32)
            nc.vector.tensor_scalar(out=pairs, in0=pairs, scalar1=HI_MASK_PAIR, scalar2=None, op0=ALU.bitwise_and)

        def w_low(n0, n1, engine, run=RUN):
            engine.tensor_tensor(
                out=in_runs(staged_cols("lo", n0, n1), run),
                in0=rows_in_runs(columns(w_raw, n0, n1), run),
                in1=in_runs(staged_cols("hi", n0, n1), run),
                op=ALU.subtract,
            )

        def w_quantize(part, n0, n1):
            half = n0 // HALF
            if (part, half) not in w_mx:
                codes = keep.tile([P, HALF], U32, name="w_codes_%s%d" % (part, half), align_bytes=64)
                scales = keep.tile([P, HALF], U8, name="w_scales_%s%d" % (part, half), align_bytes=64)
                w_mx[part, half] = (codes, scales)
            codes, scales = w_mx[part, half]
            cols = slice(n0 - half * HALF, n1 - half * HALF)
            nc.vector.quantize_mx(
                out=codes[:, cols].bitcast(FP8X4),
                scales=scales[:, cols],
                in_=staged_cols(part, n0, n1).rearrange("p n j -> p (n j)"),
            )

        def x_round(a, h, copy, m0=0, m1=P):
            dealt = staged_cols("x%d" % a, 2 * h * P, (2 * h + 2) * P).rearrange("p (r m) j -> p m j r", r=2)
            tokens = columns(x_raw, a * CHUNK + PACK * m0, a * CHUNK + PACK * m1).rearrange("p j (m r) -> p m j r", r=PACK)
            copy(out=dealt[:, m0:m1], in_=tokens[:, :, :, 2 * h : 2 * h + 2])

        def x_quantize(a, r0, r1):
            if a not in x_mx:
                codes = keep.tile([P, CHUNK], U32, name="x_codes%d" % a, align_bytes=64)
                scales = keep.tile([P, CHUNK], U8, name="x_scales%d" % a, align_bytes=64)
                x_mx[a] = (codes, scales)
            codes, scales = x_mx[a]
            nc.vector.quantize_mx(
                out=codes[:, r0 * P : r1 * P].bitcast(FP8X4),
                scales=scales[:, r0 * P : r1 * P],
                in_=staged_cols("x%d" % a, r0 * P, r1 * P).rearrange("p c j -> p (c j)"),
            )

        def result_of(a):
            if a not in results:
                results[a] = keep.tile([P, PACK, M], F32, name="result%d" % a, align_bytes=256)
            return results[a]

        def strip_sum(a, r0, r1, n0, n1):
            x_codes, x_scales = x_mx[a]
            half = n0 // HALF
            cols = slice(n0 - half * HALF, n1 - half * HALF)
            bank = next_strip_bank()
            sums[a, r0, n0] = bank
            width = n1 - n0
            for r in range(r0, r1):
                for part in ("hi", "lo"):
                    codes, scales = w_mx[part, half]
                    nc.tensor.matmul_mx(
                        out=bank[:, (r - r0) * width : (r - r0 + 1) * width],
                        lhsT=x_codes[:, r * P : (r + 1) * P].bitcast(FP8X4),
                        lhsT_scale=x_scales[:, r * P : (r + 1) * P],
                        rhs=codes[:, cols].bitcast(FP8X4),
                        rhs_scale=scales[:, cols],
                        start=(part == "hi"),
                        stop=(part == "lo"),
                    )

        def strip_add(a, r0, r1, n0, n1):
            nc.vector.tensor_tensor(
                out=result_of(a)[:, r0:r1, n0:n1],
                in0=sums[a, r0, n0][:, 0 : (r1 - r0) * (n1 - n0)].rearrange("p (r n) -> p r n", r=r1 - r0),
                in1=bias_rows[:, n0:n1].unsqueeze(1).to_broadcast([P, r1 - r0, n1 - n0]),
                op=ALU.add,
            )

        def strip_silu(a, r0, r1, n0, n1):
            strip = result_of(a)[:, r0:r1, n0:n1]
            nc.scalar.activation(out=strip, in_=strip, func=SILU, bias=zero[:, 1:2])

        def out_round(a, n0, n1, copy, run=RUN):
            copy(out=in_runs(staged_cols("out%d" % a, n0, n1), run), in_=rows_in_runs(result_of(a)[:, :, n0:n1], run))

        def out_quantize(a, n0, n1):
            nc.vector.quantize_mx(
                out=out_codes[:, a, n0:n1].bitcast(FP8X4),
                scales=scale_plane(a)[:, n0:n1],
                in_=staged_cols("out%d" % a, n0, n1).rearrange("p n r -> p (n r)"),
            )

        def store_result(a, r0, r1, n0, n1):
            rows = out_0[a * CHUNK : (a + 1) * CHUNK, n0:n1].rearrange("(p r) n -> p r n", r=PACK)
            nc.sync.dma_start(out=rows[:, r0:r1, :], in_=result_of(a)[:, r0:r1, n0:n1])

        def store_codes(a, n0, n1):
            words = out_1[a].rearrange("p n i -> p (n i)").bitcast(I32)
            nc.sync.dma_start(out=words[:, n0:n1], in_=out_codes[:, a, n0:n1].bitcast(I32))

        def store_scales(a0, a1, queue):
            for r in range(4):
                rows = out_2[a0:a1, r:16:4, :].rearrange("a q n -> q a n").bitcast(I32)
                queue.dma_start(out=rows, in_=out_scales[a0][r:P:32, :, :].bitcast(I32))

        out_codes = keep.tile([P, CHUNKS, M], U32, name="out_codes", align_bytes=256)
        out_scales = {a0: keep.tile([P, a1 - a0, M], U8, name="out_scales%d" % a0, align_bytes=256) for a0, a1 in SCALE_GROUPS}

        def scale_plane(a):
            for a0, a1 in SCALE_GROUPS:
                if a0 <= a < a1:
                    return out_scales[a0][:, a - a0, :]

        ident = keep.tile([P, P], F32, name="ident")
        b_dealt = keep.tile([P, TILES], F32, name="b_dealt")
        bias_rows = keep.tile([P, M], F32, name="bias_rows")
        zero = keep.tile([P, 2], F32, name="zero")

        def bias_spread(g, copy):
            bank = next_bank()
            for i in range(PACK):
                c = g * PACK + i
                nc.tensor.transpose(bank[:, i * P : (i + 1) * P], b_dealt[:, c : c + 1].to_broadcast([P, P]), ident[:])
            copy(
                out=bias_rows[:, g * HALF : (g + 1) * HALF].rearrange("p (m c) -> p m c", c=PACK),
                in_=bank[:].rearrange("p (i m) -> p m i", i=PACK),
            )

        bias_cols = keep.tile([P, PANELS], F32, name="bias_cols")
        mids, turned = {}, {}

        def bias_columns(t0, t1):
            bank = next_bank()
            for nt in range(t0, t1):
                nc.tensor.transpose(bank[:, (nt - t0) * P : (nt - t0 + 1) * P], bias_rows[:, nt * P : (nt + 1) * P], ident[:])
            nc.scalar.copy(out=bias_cols[:, t0:t1], in_=bank[:].rearrange("p (i m) -> p i m", m=P)[:, 0 : t1 - t0, 0])

        def panel_sum(a, nt, r0=0, r1=PACK):
            x_codes, x_scales = x_mx[a]
            if r0 == 0:
                sums["panel", a, nt] = next_bank()
            tokens = slice(r0 * P, r1 * P)
            half = nt * P // HALF
            cols = slice(nt * P - half * HALF, (nt + 1) * P - half * HALF)
            for part in ("hi", "lo"):
                codes, scales = w_mx[part, half]
                nc.tensor.matmul_mx(
                    out=sums["panel", a, nt][:, tokens],
                    lhsT=codes[:, cols].bitcast(FP8X4),
                    lhsT_scale=scales[:, cols],
                    rhs=x_codes[:, tokens].bitcast(FP8X4),
                    rhs_scale=x_scales[:, tokens],
                    start=(part == "hi" and r0 == 0),
                    stop=(part == "lo" and r1 == PACK),
                )

        def panel_silu(a, nt):
            mids[a, nt] = keep.tile([P, CHUNK], F32, name="mid", bufs=MID_BUFS)
            nc.scalar.activation(out=mids[a, nt][:], in_=sums["panel", a, nt][:], func=SILU, bias=bias_cols[:, nt : nt + 1])

        def panel_turn(a, nt):
            turned[a, nt] = next_bank()
            for r in range(PACK):
                nc.tensor.transpose(turned[a, nt][:, r * P : (r + 1) * P], mids[a, nt][:, r * P : (r + 1) * P], ident[:])

        def panel_out(a, nt, copy):
            copy(out=result_of(a)[:, :, nt * P : (nt + 1) * P], in_=turned[a, nt][:].rearrange("p (r n) -> p r n", r=PACK))

        nc.scalar.dma_start(out=b_dealt[:].rearrange("p (g c) -> p g c", c=PACK), in_=b.rearrange("(g p c) -> p g c", p=P, c=PACK))
        nc.gpsimd.memset(zero[:, 0:1], 0.0)
        nc.scalar.activation(out=zero[:, 1:2], in_=zero[:, 0:1], func=SILU)
        make_identity(nc, ident[:])

        load("w", w_rows, w_raw, 0, 128)
        load("w", w_rows, w_raw, 128, 256)
        load("x", x_rows, x_raw, 0, 256)
        load("x", x_rows, x_raw, 256, 512)
        load("w", w_rows, w_raw, 256, 512)
        load("w", w_rows, w_raw, 512, 768)
        load("w", w_rows, w_raw, 768, 1024)
        load("x", x_rows, x_raw, 512, 1024)
        load("x", x_rows, x_raw, 1024, 1536)

        for part in ("hi", "lo"):
            for q in range(4):
                stage(part, q * QUARTER, (q + 1) * QUARTER)
        stage("x0", 0, 2 * P)
        stage("x0", 2 * P, 4 * P)
        stage("x1", 0, CHUNK)
        stage("x2", 0, CHUNK)

        def strip_out(a, r0, r1, n0, n1):
            strip_add(a, r0, r1, n0, n1)
            strip_silu(a, r0, r1, n0, n1)

        def panel_in(nt):
            panel_sum(0, nt)
            panel_silu(0, nt)

        def panel_back(nt):
            panel_turn(0, nt)
            panel_out(0, nt, on_scalar)
            if nt % 2:
                store_result(0, 0, PACK, (nt - 1) * P, (nt + 1) * P)

        bias_spread(0, on_scalar)
        w_top(0, 128, on_vector)
        w_top(128, 256, on_vector)
        x_round(0, 0, on_scalar, 0, 64)
        x_round(0, 1, on_scalar, 0, 64)
        x_round(0, 1, on_scalar, 64, P)
        bias_columns(0, 4)
        w_mask(0, 128)
        w_mask(128, 256)
        w_low(0, 128, nc.vector)
        w_low(128, 256, nc.vector)
        w_quantize("hi", 0, 256)
        x_round(0, 0, on_vector, 64, P)
        w_quantize("lo", 0, 256)
        w_top(384, 512, on_scalar)
        bias_spread(1, on_scalar)
        w_top(512, 768, on_scalar)
        x_quantize(0, 0, 2)
        panel_sum(0, 0, 0, 2)
        w_top(256, 384, on_vector)
        x_quantize(0, 2, 4)
        panel_sum(0, 0, 2, 4)
        panel_sum(0, 1)
        w_mask(256, 384)
        w_mask(384, 512)
        w_low(256, 384, nc.vector)
        w_low(384, 512, nc.vector)
        w_quantize("hi", 256, 512)
        w_mask(512, 768)
        w_quantize("lo", 256, 512)
        panel_silu(0, 0)
        panel_silu(0, 1)
        bias_columns(4, PANELS)
        w_top(S_W3, 1024, on_scalar)
        if S_W3 > 768:
            w_top(768, S_W3, on_vector)
        w_low(512, 768, nc.vector)
        w_quantize("hi", 512, 768)
        w_mask(768, 1024)
        w_quantize("lo", 512, 768)
        w_low(768, 1024, nc.vector)
        w_quantize("hi", 768, 1024)
        x_round(1, 0, on_vector)
        w_quantize("lo", 768, 1024)
        x_round(1, 1, on_vector)
        x_round(2, 0, on_vector)
        x_quantize(1, 0, PACK)

        strips = [(0, 0, 2, 768, M), (0, 2, 4, 768, M)]
        strips += [(a, r, r + 1, half * HALF, (half + 1) * HALF) for a in (1, 2) for r in range(PACK) for half in range(2)]
        panel_back(0)
        panel_in(2)
        panel_back(1)
        panel_in(3)
        panel_back(2)
        panel_sum(0, 4)
        panel_sum(0, 5)
        x_round(2, 1, on_scalar)
        x_quantize(2, 0, PACK)
        panel_silu(0, 4)
        panel_silu(0, 5)
        panel_back(3)
        strip_sum(*strips[0])
        strip_sum(*strips[1])
        panel_back(4)
        panel_back(5)

        stage("out0", 0, M, "x1_0")
        stage("out1", 0, M)
        stage("out2", 0, 512)
        stage("out2", 512, 1024)
        out_round(0, 0, 512, on_gpsimd, 1)
        for i, strip in enumerate(strips):
            a, r0, r1, n0, n1 = strip
            if (a, r0, n0) not in sums:
                strip_sum(*strip)
            strip_out(*strip)
            if i == 1:
                store_result(0, 0, PACK, 768, M)
                out_round(0, 512, M, on_gpsimd, 1)
            elif a and n0:
                store_result(a, r0, r1, 0, M)
            if i == 9:
                out_round(1, 0, G_END, on_gpsimd, 1)

        out_round(2, 0, 512, on_scalar)
        out_round(2, S_LAST, 1024, on_scalar)
        out_quantize(0, 0, M)
        store_codes(0, 0, M)
        store_scales(0, 1, nc.sync)
        out_round(1, G_END, 1024, on_vector)
        out_quantize(1, 0, 512)
        out_quantize(1, 512, M)
        store_codes(1, 0, M)
        out_round(2, 512, S_LAST, on_vector)
        out_quantize(2, 0, 512)
        store_codes(2, 0, 512)
        out_quantize(2, 512, 768)
        store_codes(2, 512, 768)
        out_quantize(2, 768, 1024)
        store_codes(2, 768, 1024)
        store_scales(1, 3, nc.sync)
